import numpy as np
import ml_dtypes


def mxq(x, axis, fmt="e4m3"):
    dtype, down = {"e4m3": (ml_dtypes.float8_e4m3fn, 7), "e5m2": (ml_dtypes.float8_e5m2, 14)}[fmt]
    v = np.moveaxis(np.asarray(x, np.float32).astype(ml_dtypes.bfloat16).astype(np.float64), axis, -1)
    blocks = v.reshape(v.shape[:-1] + (-1, 32))
    amax = np.abs(blocks).max(-1, keepdims=True)
    byte = np.maximum(np.where(amax > 0, np.frexp(amax)[1] - 1 + 127, 0) - down, 1)
    scale = np.exp2(byte - 127.0)
    codes = (blocks / scale).astype(np.float32).astype(dtype).astype(np.float64)
    return np.moveaxis((codes * scale).reshape(v.shape), -1, axis)


WIDE = False


def mx_kscale(k):
    if not WIDE:
        return np.ones(k)
    levels = np.array([18, -18])
    if k % 512:
        return np.exp2(np.random.permutation(np.resize(levels, k // 32))).repeat(32)
    a = np.empty((k // 512, 16))
    for p in range(k // 512):
        a[p, :8] = np.random.permutation(np.resize(levels, 8))
        for g in range(8):
            far = levels[np.abs(levels - a[p, g]) >= 10]
            a[p, g + 8] = far[np.random.randint(len(far))]
    return np.exp2(a.ravel()).repeat(32)


def f64(x):
    return np.asarray(x).astype(np.float64)


def striped(idx):
    return np.tile(np.asarray(idx).reshape(-1, 16).T, (8, 1)).astype(np.uint16)


def unstriped(offs):
    return offs[:16].T.reshape(-1).astype(np.int64)


def setup_inputs():
    n = np.random.standard_normal
    uni = np.random.uniform
    idx = np.random.permutation(2048)[:512]
    f_d = mx_kscale(512)
    f_r = mx_kscale(512)
    return {
        "wT": (np.round(n((512, 2048)) * 64) / 64 * f_d[:, None]).astype(np.float32),
        "mT": (np.round(0.5 * n((512, 2048)) * 64) / 64 * f_d[:, None]).astype(np.float32),
        "xT": (n((512, 512)) / np.sqrt(512) / f_d[:, None] * f_r[None, :]).astype(np.float32),
        "y": (n((512, 512))).astype(np.float32),
        "ts": np.tile(uni(0.75, 1.3, 2048), (128, 1)).astype(np.float32),
        "us": (uni(0.75, 1.3, (512, 1)) / f_r[:, None]).astype(np.float32),
        "wt": (uni(0.75, 1.3, (512, 1)) / np.sqrt(512)).astype(np.float32),
        "fd": (uni(0.75, 1.3, (512, 1)) * f_d[:, None]).astype(np.float32),
        "offs": striped(idx),
    }


def reference(wT, mT, xT, y, ts, us, wt, fd, offs):
    idx = unstriped(offs)
    wT_i = f64(wT)[:, idx]
    mT_i = f64(mT)[:, idx]
    ts_i = f64(ts)[:1][:, idx]
    w2 = wT_i + mT_i
    a = mxq(f64(xT), 0, "e4m3").T @ mxq(w2, 0, "e4m3")
    g = f64(wt) * f64(us) * ts_i * (f64(us) * ts_i * a - f64(y))
    dw = mxq(f64(xT), 1, "e4m3") @ mxq(g, 0, "e5m2")
    nm = mT_i - np.square(f64(fd)) * dw
    out_0 = np.zeros((512, 2048))
    out_0[:, idx] = nm
    out_1 = np.zeros((512, 2048))
    out_1[:, idx] = dw
    return out_0, out_1

@@ -1,0 +1,220 @@
+from contextlib import ExitStack
+
+import concourse.mybir as mybir
+from concourse.masks import make_identity
+
+D, R, SLOTS, TABLE = 512, 512, 512, 2048
+FLOPS = 2 * 2 * D * R * SLOTS
+
+F32 = mybir.dt.float32
+BF16 = mybir.dt.bfloat16
+U32 = mybir.dt.uint32
+U16 = mybir.dt.uint16
+U8 = mybir.dt.uint8
+E4M3 = mybir.dt.float8_e4m3fn_x4
+E5M2 = mybir.dt.float8_e5m2_x4
+MULT = mybir.AluOpType.mult
+ADD = mybir.AluOpType.add
+SUB = mybir.AluOpType.subtract
+COPY = mybir.ActivationFunctionType.Copy
+SQUARE = mybir.ActivationFunctionType.Square
+
+P = 128
+PACK = 4
+QUARTERS = 4
+QSLOTS = SLOTS // QUARTERS
+OFFS_PER_COL = 16
+RUN = 4
+
+
+def tile_attend_gahead_nag_sq_kernel(tc, wT, mT, xT, y, ts, us, wt, fd, offs, out_0, out_1):
+    nc = tc.nc
+    with ExitStack() as ctx:
+        keep = ctx.enter_context(tc.tile_pool(name="keep", bufs=1))
+        psum = ctx.enter_context(tc.psum_pool(name="psum", bufs=1))
+
+        def by_plane(ap):
+            return ap.rearrange("(p t) c -> p t c", t=PACK)
+
+        def bank(tag, name):
+            return psum.tile([P, 512], F32, name=name, tag=tag)
+
+        offsets = keep.tile([P, SLOTS // OFFS_PER_COL], U16, name="offsets")
+        nc.sync.dma_start(offsets[:], offs)
+
+        m_win = [keep.tile([P, TABLE], F32, name=f"m_win{t}") for t in range(PACK)]
+        w_win = [keep.tile([P, TABLE], F32, name=f"w_win{t}") for t in range(PACK)]
+        x_raw = keep.tile([P, PACK, R], F32, name="x_raw")
+        y_raw = keep.tile([P, PACK, SLOTS], F32, name="y_raw")
+        ts_win = keep.tile([P, TABLE], F32, name="ts_win")
+        us_c = keep.tile([P, PACK], F32, name="us_c")
+        wt_c = keep.tile([P, PACK], F32, name="wt_c")
+        fd_c = keep.tile([P, PACK], F32, name="fd_c")
+
+        ts_row = keep.tile([P, TABLE // P], F32, name="ts_row")
+        nc.scalar.dma_start(ts_row[:], ts[0:1, :].rearrange("o (p j) -> p (o j)", p=P))
+        for t in range(PACK):
+            nc.sync.dma_start(m_win[t][:], by_plane(mT)[:, t, :])
+            nc.sync.dma_start(w_win[t][:], by_plane(wT)[:, t, :])
+            if t == 0:
+                nc.sync.dma_start(x_raw[:], by_plane(xT))
+                for tile, vec in ((us_c, us), (wt_c, wt), (fd_c, fd)):
+                    nc.sync.dma_start(tile[:], vec.rearrange("(p t) o -> p (t o)", t=PACK))
+        nc.sync.dma_start(y_raw[:], by_plane(y))
+
+        grad_win = [keep.tile([P, TABLE], F32, name=f"grad_win{k}") for k in range(2)]
+        mom_win = [keep.tile([P, TABLE], F32, name=f"mom_win{k}") for k in range(2)]
+        ident = keep.tile([P, P], F32, name="ident")
+        make_identity(nc, ident[:])
+        for k in range(2):
+            nc.gpsimd.memset(grad_win[k][:], 0.0)
+            nc.gpsimd.memset(mom_win[k][:], 0.0)
+
+        for b in range(4):
+            spread = bank(f"a{b}", f"ts_spread{b}")
+            for k in range(4):
+                j = 4 * b + k
+                nc.tensor.transpose(spread[:, k * P : (k + 1) * P], ts_row[:, j : j + 1].to_broadcast([P, P]), ident[:])
+            nc.scalar.activation(
+                ts_win[:].rearrange("p (n b k) -> p n b k", b=4, k=4)[:, :, b, :],
+                spread[:].rearrange("p (k n) -> p n k", k=4),
+                COPY,
+            )
+
+        c2 = keep.tile([P, PACK], F32, name="c2")
+        c1 = keep.tile([P, PACK], F32, name="c1")
+        neg_fd2 = keep.tile([P, PACK], F32, name="neg_fd2")
+
+        m_g = [keep.tile([P, SLOTS], F32, name=f"m_g{t}") for t in range(PACK)]
+        w2 = [keep.tile([P, PACK, QSLOTS], F32, name=f"w2_{q}") for q in range(QUARTERS)]
+
+        def q_offsets(q):
+            cols = QSLOTS // OFFS_PER_COL
+            return offsets[:, q * cols : (q + 1) * cols]
+
+        def q_cols(q):
+            return slice(q * QSLOTS, (q + 1) * QSLOTS)
+
+        def gather_plane(t):
+            nc.vector.tensor_copy(m_g[t][:], m_win[t][:].indirect(offsets[:]))
+            for q in range(QUARTERS):
+                nc.vector.tensor_tensor(w2[q][:, t, :], w_win[t][:].indirect(q_offsets(q)), m_g[t][:, q_cols(q)], ADD)
+
+        ts_g = keep.tile([P, SLOTS], F32, name="ts_g")
+        nc.vector.tensor_copy(ts_g[:], ts_win[:].indirect(offsets[:]))
+        gather_plane(0)
+        nc.vector.tensor_tensor(c2[:], wt_c[:], us_c[:], MULT)
+        nc.vector.scalar_tensor_tensor(neg_fd2[:], fd_c[:], -1.0, fd_c[:], MULT, MULT)
+        nc.vector.tensor_tensor(c1[:], c2[:], us_c[:], MULT)
+
+        x_bf = keep.tile([P, PACK, R], BF16, name="x_bf", align_bytes=64)
+        nc.scalar.copy(x_bf[:], x_raw[:])
+        x_words = x_bf[:].rearrange("p t r -> p (t r)").bitcast(F32)
+        xr_il = keep.tile([P, D, PACK], BF16, name="xr_il", align_bytes=64)
+        xr_words = xr_il[:].rearrange("p d s -> p (d s)").bitcast(F32)
+        for b in range(2):
+            xt = bank(f"d{b}", f"x_turned{b}")
+            for k in range(2):
+                t = 2 * b + k
+                for u in range(2):
+                    nc.tensor.transpose(
+                        xt[:, (2 * k + u) * P : (2 * k + u + 1) * P],
+                        x_words[:, t * 256 + u : (t + 1) * 256 : 2],
+                        ident[:],
+                    )
+            nc.scalar.copy(
+                xr_words[:, b * 512 : (b + 1) * 512].rearrange("p (k d u) -> p k d u", k=2, u=2),
+                xt[:].rearrange("p (k u d) -> p k d u", k=2, u=2),
+            )
+        xd_il = keep.tile([P, R, PACK], BF16, name="xd_il", align_bytes=64)
+        nc.scalar.copy(
+            xd_il[:].rearrange("p (s r) t -> p s r t", s=PACK),
+            x_bf[:].rearrange("p t (r s) -> p s r t", s=PACK),
+        )
+
+        ts_sq = keep.tile([P, SLOTS], F32, name="ts_sq")
+        a_fac = keep.tile([P, PACK, SLOTS], F32, name="a_fac")
+        y_fac = keep.tile([P, PACK, SLOTS], F32, name="y_fac")
+        nc.scalar.activation(ts_sq[:], ts_g[:], SQUARE)
+        for s in range(PACK):
+            nc.scalar.activation(y_fac[:, s, :], ts_g[:], COPY, scale=c2[:, s : s + 1])
+            nc.scalar.activation(a_fac[:, s, :], ts_sq[:], COPY, scale=c1[:, s : s + 1])
+
+        gather_plane(1)
+
+        xd_codes = keep.tile([P, R], U32, name="xd_codes", align_bytes=64)
+        xd_scales = keep.tile([P, R], U8, name="xd_scales", align_bytes=64)
+        xr_codes = keep.tile([P, D], U32, name="xr_codes", align_bytes=64)
+        xr_scales = keep.tile([P, D], U8, name="xr_scales", align_bytes=64)
+        gather_plane(2)
+        nc.vector.quantize_mx(xr_codes[:].bitcast(E4M3), xr_scales[:], xr_il[:].rearrange("p d s -> p (d s)"))
+        nc.vector.quantize_mx(xd_codes[:].bitcast(E4M3), xd_scales[:], xd_il[:].rearrange("p r t -> p (r t)"))
+        gather_plane(3)
+
+        def woven(tile):
+            return tile.rearrange("p (c i) t -> p c t i", i=RUN)
+
+        def planar(tile):
+            return tile.rearrange("p t (c i) -> p c t i", i=RUN)
+
+        g_codes = keep.tile([P, SLOTS], U32, name="g_codes", align_bytes=64)
+        g_scales = keep.tile([P, SLOTS], U8, name="g_scales", align_bytes=64)
+        scores = []
+        for q in range(QUARTERS):
+            w2_il = keep.tile([P, QSLOTS, PACK], BF16, name=f"w2_il{q}", align_bytes=64)
+            nc.scalar.copy(woven(w2_il[:]), planar(w2[q][:]))
+            w2_codes = keep.tile([P, QSLOTS], U32, name=f"w2_codes{q}", align_bytes=64)
+            w2_scales = keep.tile([P, QSLOTS], U8, name=f"w2_scales{q}", align_bytes=64)
+            nc.vector.quantize_mx(w2_codes[:].bitcast(E4M3), w2_scales[:], w2_il[:].rearrange("p n t -> p (n t)"))
+            a_q = bank(f"a{q}", f"a{q}")
+            for s in range(PACK):
+                rows = slice(s * P, (s + 1) * P)
+                nc.tensor.matmul_mx(
+                    a_q[:, rows],
+                    lhsT=xd_codes[:, rows].bitcast(E4M3),
+                    lhsT_scale=xd_scales[:, rows],
+                    rhs=w2_codes[:].bitcast(E4M3),
+                    rhs_scale=w2_scales[:],
+                    start=True,
+                    stop=True,
+                )
+            scores.append(a_q)
+
+        y_term = [keep.tile([P, PACK, QSLOTS], F32, name=f"y_term{q}") for q in range(QUARTERS)]
+        a_term = [keep.tile([P, PACK, QSLOTS], F32, name=f"a_term{q}") for q in range(QUARTERS)]
+        g_il = [keep.tile([P, QSLOTS, PACK], BF16, name=f"g_il{q}", align_bytes=64) for q in range(QUARTERS)]
+        for q in range(QUARTERS + 2):
+            if q < QUARTERS:
+                nc.vector.tensor_tensor(y_term[q][:], y_raw[:, :, q_cols(q)], y_fac[:, :, q_cols(q)], MULT)
+                nc.vector.tensor_tensor(
+                    a_term[q][:], scores[q][:].rearrange("p (s n) -> p s n", s=PACK), a_fac[:, :, q_cols(q)], MULT
+                )
+            if 1 <= q <= QUARTERS:
+                nc.vector.tensor_tensor(woven(g_il[q - 1][:]), planar(a_term[q - 1][:]), planar(y_term[q - 1][:]), SUB)
+            if q >= 2:
+                nc.vector.quantize_mx(
+                    g_codes[:, q_cols(q - 2)].bitcast(E5M2),
+                    g_scales[:, q_cols(q - 2)],
+                    g_il[q - 2][:].rearrange("p n s -> p (n s)"),
+                )
+
+        for t in range(PACK):
+            feats = slice(t * P, (t + 1) * P)
+            dw_ps = bank(f"d{t}", f"dw_ps{t}")
+            nc.tensor.matmul_mx(
+                dw_ps[:],
+                lhsT=xr_codes[:, feats].bitcast(E4M3),
+                lhsT_scale=xr_scales[:, feats],
+                rhs=g_codes[:].bitcast(E5M2),
+                rhs_scale=g_scales[:],
+                start=True,
+                stop=True,
+            )
+            dw = keep.tile([P, SLOTS], F32, name=f"dw{t}")
+            step = keep.tile([P, SLOTS], F32, name=f"step{t}")
+            nc.scalar.copy(dw[:], dw_ps[:])
+            nc.scalar.activation(step[:], dw_ps[:], COPY, scale=neg_fd2[:, t : t + 1])
+            nc.vector.tensor_copy(grad_win[t % 2][:].indirect(offsets[:]), dw[:])
+            nc.sync.dma_start(by_plane(out_1)[:, t, :], grad_win[t % 2][:])
+            nc.vector.tensor_tensor(mom_win[t % 2][:].indirect(offsets[:]), m_g[t][:], step[:], ADD)
+            nc.sync.dma_start(by_plane(out_0)[:, t, :], mom_win[t % 2][:])

@@ -25,6 +25,7 @@ QUARTERS = 4
 QSLOTS = SLOTS // QUARTERS
 OFFS_PER_COL = 16
 RUN = 4
+EARLY = 2
 
 
 def tile_attend_gahead_nag_sq_kernel(tc, wT, mT, xT, y, ts, us, wt, fd, offs, out_0, out_1):
@@ -40,7 +41,6 @@ def tile_attend_gahead_nag_sq_kernel(tc, wT, mT, xT, y, ts, us, wt, fd, offs, ou
             return psum.tile([P, 512], F32, name=name, tag=tag)
 
         offsets = keep.tile([P, SLOTS // OFFS_PER_COL], U16, name="offsets")
-        nc.sync.dma_start(offsets[:], offs)
 
         m_win = [keep.tile([P, TABLE], F32, name=f"m_win{t}") for t in range(PACK)]
         w_win = [keep.tile([P, TABLE], F32, name=f"w_win{t}") for t in range(PACK)]
@@ -53,13 +53,14 @@ def tile_attend_gahead_nag_sq_kernel(tc, wT, mT, xT, y, ts, us, wt, fd, offs, ou
 
         ts_row = keep.tile([P, TABLE // P], F32, name="ts_row")
         nc.scalar.dma_start(ts_row[:], ts[0:1, :].rearrange("o (p j) -> p (o j)", p=P))
+        nc.sync.dma_start(x_raw[:], by_plane(xT))
+        nc.sync.dma_start(offsets[:], offs)
+        nc.scalar.dma_start(us_c[:], by_plane(us)[:, :, 0])
+        nc.scalar.dma_start(wt_c[:], by_plane(wt)[:, :, 0])
+        nc.scalar.dma_start(fd_c[:], by_plane(fd)[:, :, 0])
         for t in range(PACK):
             nc.sync.dma_start(m_win[t][:], by_plane(mT)[:, t, :])
             nc.sync.dma_start(w_win[t][:], by_plane(wT)[:, t, :])
-            if t == 0:
-                nc.sync.dma_start(x_raw[:], by_plane(xT))
-                for tile, vec in ((us_c, us), (wt_c, wt), (fd_c, fd)):
-                    nc.sync.dma_start(tile[:], vec.rearrange("(p t) o -> p (t o)", t=PACK))
         nc.sync.dma_start(y_raw[:], by_plane(y))
 
         grad_win = [keep.tile([P, TABLE], F32, name=f"grad_win{k}") for k in range(2)]
@@ -67,8 +68,8 @@ def tile_attend_gahead_nag_sq_kernel(tc, wT, mT, xT, y, ts, us, wt, fd, offs, ou
         ident = keep.tile([P, P], F32, name="ident")
         make_identity(nc, ident[:])
         for k in range(2):
-            nc.gpsimd.memset(grad_win[k][:], 0.0)
-            nc.gpsimd.memset(mom_win[k][:], 0.0)
+            nc.vector.memset(grad_win[k][:], 0.0)
+            nc.vector.memset(mom_win[k][:], 0.0)
 
         for b in range(4):
             spread = bank(f"a{b}", f"ts_spread{b}")
@@ -100,12 +101,12 @@ def tile_attend_gahead_nag_sq_kernel(tc, wT, mT, xT, y, ts, us, wt, fd, offs, ou
             for q in range(QUARTERS):
                 nc.vector.tensor_tensor(w2[q][:, t, :], w_win[t][:].indirect(q_offsets(q)), m_g[t][:, q_cols(q)], ADD)
 
-        ts_g = keep.tile([P, SLOTS], F32, name="ts_g")
-        nc.vector.tensor_copy(ts_g[:], ts_win[:].indirect(offsets[:]))
-        gather_plane(0)
         nc.vector.tensor_tensor(c2[:], wt_c[:], us_c[:], MULT)
         nc.vector.scalar_tensor_tensor(neg_fd2[:], fd_c[:], -1.0, fd_c[:], MULT, MULT)
         nc.vector.tensor_tensor(c1[:], c2[:], us_c[:], MULT)
+        ts_g = keep.tile([P, SLOTS], F32, name="ts_g")
+        nc.vector.tensor_copy(ts_g[:], ts_win[:].indirect(offsets[:]))
+        gather_plane(0)
 
         x_bf = keep.tile([P, PACK, R], BF16, name="x_bf", align_bytes=64)
         nc.scalar.copy(x_bf[:], x_raw[:])
@@ -181,7 +182,7 @@ def tile_attend_gahead_nag_sq_kernel(tc, wT, mT, xT, y, ts, us, wt, fd, offs, ou
             scores.append(a_q)
 
         y_term = [keep.tile([P, PACK, QSLOTS], F32, name=f"y_term{q}") for q in range(QUARTERS)]
-        a_term = [keep.tile([P, PACK, QSLOTS], F32, name=f"a_term{q}") for q in range(QUARTERS)]
+        a_term = [keep.tile([P, PACK, QSLOTS], F32, name=f"a_term{q}", tag=f"a_term{q}") for q in range(QUARTERS)]
         g_il = [keep.tile([P, QSLOTS, PACK], BF16, name=f"g_il{q}", align_bytes=64) for q in range(QUARTERS)]
         for q in range(QUARTERS + 2):
             if q < QUARTERS:
@@ -198,6 +199,26 @@ def tile_attend_gahead_nag_sq_kernel(tc, wT, mT, xT, y, ts, us, wt, fd, offs, ou
                     g_il[q - 2][:].rearrange("p n s -> p (n s)"),
                 )
 
+        early_ps = bank("a0", "early_ps")
+        nc.tensor.matmul_mx(
+            early_ps[:],
+            lhsT=g_codes[:, q_cols(0)].bitcast(E5M2),
+            lhsT_scale=g_scales[:, q_cols(0)],
+            rhs=xr_codes[:].bitcast(E4M3),
+            rhs_scale=xr_scales[:],
+            start=True,
+            stop=True,
+        )
+        early_sb = keep.tile([P, EARLY * P], F32, name="early_sb")
+        nc.scalar.copy(early_sb[:], early_ps[:, 0 : EARLY * P])
+        early_back = bank("a1", "early_back")
+        for t in range(EARLY):
+            nc.tensor.transpose(early_back[:, t * P : (t + 1) * P], early_sb[:, t * P : (t + 1) * P], ident[:])
+        early_step = keep.tile([P, EARLY, QSLOTS], F32, name="early_step", tag=f"a_term{QUARTERS - 1}")
+        for t in range(EARLY):
+            nc.scalar.activation(early_step[:, t, :], early_back[:, t * P : (t + 1) * P], COPY, scale=neg_fd2[:, t : t + 1])
+            nc.vector.tensor_tensor(mom_win[t][:].indirect(q_offsets(0)), m_g[t][:, q_cols(0)], early_step[:, t, :], ADD)
+
         for t in range(PACK):
             feats = slice(t * P, (t + 1) * P)
             dw_ps = bank(f"d{t}", f"dw_ps{t}")
@@ -213,8 +234,9 @@ def tile_attend_gahead_nag_sq_kernel(tc, wT, mT, xT, y, ts, us, wt, fd, offs, ou
             dw = keep.tile([P, SLOTS], F32, name=f"dw{t}")
             step = keep.tile([P, SLOTS], F32, name=f"step{t}")
             nc.scalar.copy(dw[:], dw_ps[:])
-            nc.scalar.activation(step[:], dw_ps[:], COPY, scale=neg_fd2[:, t : t + 1])
+            first = QSLOTS if t < EARLY else 0
+            nc.scalar.activation(step[:, first:], dw_ps[:, first:], COPY, scale=neg_fd2[:, t : t + 1])
             nc.vector.tensor_copy(grad_win[t % 2][:].indirect(offsets[:]), dw[:])
             nc.sync.dma_start(by_plane(out_1)[:, t, :], grad_win[t % 2][:])
-            nc.vector.tensor_tensor(mom_win[t % 2][:].indirect(offsets[:]), m_g[t][:], step[:], ADD)
+            nc.vector.tensor_tensor(mom_win[t % 2][:].indirect(offsets[:, first // OFFS_PER_COL :]), m_g[t][:, first:], step[:, first:], ADD)
             nc.sync.dma_start(by_plane(out_0)[:, t, :], mom_win[t % 2][:])

@@ -23,6 +23,7 @@ P = 128
 PACK = 4
 QUARTERS = 4
 QSLOTS = SLOTS // QUARTERS
+HSLOTS = SLOTS // 2
 OFFS_PER_COL = 16
 RUN = 4
 EARLY = 2
@@ -45,7 +46,7 @@ def tile_attend_gahead_nag_sq_kernel(tc, wT, mT, xT, y, ts, us, wt, fd, offs, ou
         m_win = [keep.tile([P, TABLE], F32, name=f"m_win{t}") for t in range(PACK)]
         w_win = [keep.tile([P, TABLE], F32, name=f"w_win{t}") for t in range(PACK)]
         x_raw = keep.tile([P, PACK, R], F32, name="x_raw")
-        y_raw = keep.tile([P, PACK, SLOTS], F32, name="y_raw")
+        y_raw = [keep.tile([P, PACK, HSLOTS], F32, name=f"y_raw{h}") for h in range(2)]
         ts_win = keep.tile([P, TABLE], F32, name="ts_win")
         us_c = keep.tile([P, PACK], F32, name="us_c")
         wt_c = keep.tile([P, PACK], F32, name="wt_c")
@@ -57,11 +58,12 @@ def tile_attend_gahead_nag_sq_kernel(tc, wT, mT, xT, y, ts, us, wt, fd, offs, ou
         nc.sync.dma_start(offsets[:], offs)
         nc.scalar.dma_start(us_c[:], by_plane(us)[:, :, 0])
         nc.scalar.dma_start(wt_c[:], by_plane(wt)[:, :, 0])
-        nc.scalar.dma_start(fd_c[:], by_plane(fd)[:, :, 0])
         for t in range(PACK):
             nc.sync.dma_start(m_win[t][:], by_plane(mT)[:, t, :])
             nc.sync.dma_start(w_win[t][:], by_plane(wT)[:, t, :])
-        nc.sync.dma_start(y_raw[:], by_plane(y))
+        for h in range(2):
+            nc.sync.dma_start(y_raw[h][:], by_plane(y)[:, :, h * HSLOTS : (h + 1) * HSLOTS])
+        nc.sync.dma_start(fd_c[:], by_plane(fd)[:, :, 0])
 
         grad_win = [keep.tile([P, TABLE], F32, name=f"grad_win{k}") for k in range(2)]
         mom_win = [keep.tile([P, TABLE], F32, name=f"mom_win{k}") for k in range(2)]
@@ -87,7 +89,7 @@ def tile_attend_gahead_nag_sq_kernel(tc, wT, mT, xT, y, ts, us, wt, fd, offs, ou
         neg_fd2 = keep.tile([P, PACK], F32, name="neg_fd2")
 
         m_g = [keep.tile([P, SLOTS], F32, name=f"m_g{t}") for t in range(PACK)]
-        w2 = [keep.tile([P, PACK, QSLOTS], F32, name=f"w2_{q}") for q in range(QUARTERS)]
+        w2 = [keep.tile([P, PACK, HSLOTS], F32, name=f"w2_{h}") for h in range(2)]
 
         def q_offsets(q):
             cols = QSLOTS // OFFS_PER_COL
@@ -98,11 +100,16 @@ def tile_attend_gahead_nag_sq_kernel(tc, wT, mT, xT, y, ts, us, wt, fd, offs, ou
 
         def gather_plane(t):
             nc.vector.tensor_copy(m_g[t][:], m_win[t][:].indirect(offsets[:]))
-            for q in range(QUARTERS):
-                nc.vector.tensor_tensor(w2[q][:, t, :], w_win[t][:].indirect(q_offsets(q)), m_g[t][:, q_cols(q)], ADD)
+            for h in range(2):
+                cols = HSLOTS // OFFS_PER_COL
+                nc.vector.tensor_tensor(
+                    w2[h][:, t, :],
+                    w_win[t][:].indirect(offsets[:, h * cols : (h + 1) * cols]),
+                    m_g[t][:, h * HSLOTS : (h + 1) * HSLOTS],
+                    ADD,
+                )
 
         nc.vector.tensor_tensor(c2[:], wt_c[:], us_c[:], MULT)
-        nc.vector.scalar_tensor_tensor(neg_fd2[:], fd_c[:], -1.0, fd_c[:], MULT, MULT)
         nc.vector.tensor_tensor(c1[:], c2[:], us_c[:], MULT)
         ts_g = keep.tile([P, SLOTS], F32, name="ts_g")
         nc.vector.tensor_copy(ts_g[:], ts_win[:].indirect(offsets[:]))
@@ -160,38 +167,42 @@ def tile_attend_gahead_nag_sq_kernel(tc, wT, mT, xT, y, ts, us, wt, fd, offs, ou
 
         g_codes = keep.tile([P, SLOTS], U32, name="g_codes", align_bytes=64)
         g_scales = keep.tile([P, SLOTS], U8, name="g_scales", align_bytes=64)
+        fd2 = keep.tile([P, PACK], F32, name="fd2")
+        nc.gpsimd.tensor_tensor(fd2[:], fd_c[:], fd_c[:], MULT)
+        nc.gpsimd.tensor_scalar(neg_fd2[:], fd2[:], -1.0, 0.0, MULT, ADD)
         scores = []
-        for q in range(QUARTERS):
-            w2_il = keep.tile([P, QSLOTS, PACK], BF16, name=f"w2_il{q}", align_bytes=64)
-            nc.scalar.copy(woven(w2_il[:]), planar(w2[q][:]))
-            w2_codes = keep.tile([P, QSLOTS], U32, name=f"w2_codes{q}", align_bytes=64)
-            w2_scales = keep.tile([P, QSLOTS], U8, name=f"w2_scales{q}", align_bytes=64)
+        y_term = [keep.tile([P, PACK, HSLOTS], F32, name=f"y_term{h}") for h in range(2)]
+        for h in range(2):
+            nc.vector.tensor_tensor(y_term[h][:], y_raw[h][:], y_fac[:, :, h * HSLOTS : (h + 1) * HSLOTS], MULT)
+            w2_il = keep.tile([P, HSLOTS, PACK], BF16, name=f"w2_il{h}", align_bytes=64)
+            nc.scalar.copy(woven(w2_il[:]), planar(w2[h][:]))
+            w2_codes = keep.tile([P, HSLOTS], U32, name=f"w2_codes{h}", align_bytes=64)
+            w2_scales = keep.tile([P, HSLOTS], U8, name=f"w2_scales{h}", align_bytes=64)
             nc.vector.quantize_mx(w2_codes[:].bitcast(E4M3), w2_scales[:], w2_il[:].rearrange("p n t -> p (n t)"))
-            a_q = bank(f"a{q}", f"a{q}")
-            for s in range(PACK):
-                rows = slice(s * P, (s + 1) * P)
-                nc.tensor.matmul_mx(
-                    a_q[:, rows],
-                    lhsT=xd_codes[:, rows].bitcast(E4M3),
-                    lhsT_scale=xd_scales[:, rows],
-                    rhs=w2_codes[:].bitcast(E4M3),
-                    rhs_scale=w2_scales[:],
-                    start=True,
-                    stop=True,
-                )
-            scores.append(a_q)
+            for k in range(2):
+                a_q = bank(f"a{2 * h + k}", f"a{2 * h + k}")
+                for s in range(PACK):
+                    rows = slice(s * P, (s + 1) * P)
+                    nc.tensor.matmul_mx(
+                        a_q[:, rows],
+                        lhsT=xd_codes[:, rows].bitcast(E4M3),
+                        lhsT_scale=xd_scales[:, rows],
+                        rhs=w2_codes[:, q_cols(k)].bitcast(E4M3),
+                        rhs_scale=w2_scales[:, q_cols(k)],
+                        start=True,
+                        stop=True,
+                    )
+                scores.append(a_q)
 
-        y_term = [keep.tile([P, PACK, QSLOTS], F32, name=f"y_term{q}") for q in range(QUARTERS)]
         a_term = [keep.tile([P, PACK, QSLOTS], F32, name=f"a_term{q}", tag=f"a_term{q}") for q in range(QUARTERS)]
         g_il = [keep.tile([P, QSLOTS, PACK], BF16, name=f"g_il{q}", align_bytes=64) for q in range(QUARTERS)]
         for q in range(QUARTERS + 2):
             if q < QUARTERS:
-                nc.vector.tensor_tensor(y_term[q][:], y_raw[:, :, q_cols(q)], y_fac[:, :, q_cols(q)], MULT)
                 nc.vector.tensor_tensor(
                     a_term[q][:], scores[q][:].rearrange("p (s n) -> p s n", s=PACK), a_fac[:, :, q_cols(q)], MULT
                 )
             if 1 <= q <= QUARTERS:
-                nc.vector.tensor_tensor(woven(g_il[q - 1][:]), planar(a_term[q - 1][:]), planar(y_term[q - 1][:]), SUB)
+                nc.vector.tensor_tensor(woven(g_il[q - 1][:]), planar(a_term[q - 1][:]), planar(y_term[(q - 1) // 2][:, :, q_cols((q - 1) % 2)]), SUB)
             if q >= 2:
                 nc.vector.quantize_mx(
                     g_codes[:, q_cols(q - 2)].bitcast(E5M2),

@@ -25,8 +25,8 @@ QUARTERS = 4
 QSLOTS = SLOTS // QUARTERS
 HSLOTS = SLOTS // 2
 OFFS_PER_COL = 16
-RUN = 4
-EARLY = 2
+RUN = 2
+PAD = SLOTS - HSLOTS
 
 
 def tile_attend_gahead_nag_sq_kernel(tc, wT, mT, xT, y, ts, us, wt, fd, offs, out_0, out_1):
@@ -61,9 +61,10 @@ def tile_attend_gahead_nag_sq_kernel(tc, wT, mT, xT, y, ts, us, wt, fd, offs, ou
         for t in range(PACK):
             nc.sync.dma_start(m_win[t][:], by_plane(mT)[:, t, :])
             nc.sync.dma_start(w_win[t][:], by_plane(wT)[:, t, :])
+            if t == 1:
+                nc.sync.dma_start(fd_c[:], by_plane(fd)[:, :, 0])
         for h in range(2):
             nc.sync.dma_start(y_raw[h][:], by_plane(y)[:, :, h * HSLOTS : (h + 1) * HSLOTS])
-        nc.sync.dma_start(fd_c[:], by_plane(fd)[:, :, 0])
 
         grad_win = [keep.tile([P, TABLE], F32, name=f"grad_win{k}") for k in range(2)]
         mom_win = [keep.tile([P, TABLE], F32, name=f"mom_win{k}") for k in range(2)]
@@ -74,7 +75,7 @@ def tile_attend_gahead_nag_sq_kernel(tc, wT, mT, xT, y, ts, us, wt, fd, offs, ou
             nc.vector.memset(mom_win[k][:], 0.0)
 
         for b in range(4):
-            spread = bank(f"a{b}", f"ts_spread{b}")
+            spread = bank(f"b{b}", f"ts_spread{b}")
             for k in range(4):
                 j = 4 * b + k
                 nc.tensor.transpose(spread[:, k * P : (k + 1) * P], ts_row[:, j : j + 1].to_broadcast([P, P]), ident[:])
@@ -86,31 +87,28 @@ def tile_attend_gahead_nag_sq_kernel(tc, wT, mT, xT, y, ts, us, wt, fd, offs, ou
 
         c2 = keep.tile([P, PACK], F32, name="c2")
         c1 = keep.tile([P, PACK], F32, name="c1")
+        neg_c2 = keep.tile([P, PACK], F32, name="neg_c2")
         neg_fd2 = keep.tile([P, PACK], F32, name="neg_fd2")
 
         m_g = [keep.tile([P, SLOTS], F32, name=f"m_g{t}") for t in range(PACK)]
-        w2 = [keep.tile([P, PACK, HSLOTS], F32, name=f"w2_{h}") for h in range(2)]
+        pieces = [(0, QSLOTS), (QSLOTS, HSLOTS), (HSLOTS, SLOTS)]
+        w2 = [keep.tile([P, PACK, hi - lo], F32, name=f"w2_{lo}") for lo, hi in pieces]
 
-        def q_offsets(q):
-            cols = QSLOTS // OFFS_PER_COL
-            return offsets[:, q * cols : (q + 1) * cols]
+        def offs_of(lo, hi):
+            return offsets[:, lo // OFFS_PER_COL : hi // OFFS_PER_COL]
 
         def q_cols(q):
             return slice(q * QSLOTS, (q + 1) * QSLOTS)
 
         def gather_plane(t):
             nc.vector.tensor_copy(m_g[t][:], m_win[t][:].indirect(offsets[:]))
-            for h in range(2):
-                cols = HSLOTS // OFFS_PER_COL
-                nc.vector.tensor_tensor(
-                    w2[h][:, t, :],
-                    w_win[t][:].indirect(offsets[:, h * cols : (h + 1) * cols]),
-                    m_g[t][:, h * HSLOTS : (h + 1) * HSLOTS],
-                    ADD,
-                )
+            for k in range(3):
+                lo, hi = pieces[k]
+                nc.vector.tensor_tensor(w2[k][:, t, :], w_win[t][:].indirect(offs_of(lo, hi)), m_g[t][:, lo:hi], ADD)
 
         nc.vector.tensor_tensor(c2[:], wt_c[:], us_c[:], MULT)
         nc.vector.tensor_tensor(c1[:], c2[:], us_c[:], MULT)
+        nc.vector.tensor_scalar(neg_c2[:], c2[:], -1.0, 0.0, MULT, ADD)
         ts_g = keep.tile([P, SLOTS], F32, name="ts_g")
         nc.vector.tensor_copy(ts_g[:], ts_win[:].indirect(offsets[:]))
         gather_plane(0)
@@ -121,7 +119,7 @@ def tile_attend_gahead_nag_sq_kernel(tc, wT, mT, xT, y, ts, us, wt, fd, offs, ou
         xr_il = keep.tile([P, D, PACK], BF16, name="xr_il", align_bytes=64)
         xr_words = xr_il[:].rearrange("p d s -> p (d s)").bitcast(F32)
         for b in range(2):
-            xt = bank(f"d{b}", f"x_turned{b}")
+            xt = bank(f"b{4 + b}", f"x_turned{b}")
             for k in range(2):
                 t = 2 * b + k
                 for u in range(2):
@@ -140,13 +138,27 @@ def tile_attend_gahead_nag_sq_kernel(tc, wT, mT, xT, y, ts, us, wt, fd, offs, ou
             x_bf[:].rearrange("p t (r s) -> p s r t", s=PACK),
         )
 
-        ts_sq = keep.tile([P, SLOTS], F32, name="ts_sq")
-        a_fac = keep.tile([P, PACK, SLOTS], F32, name="a_fac")
-        y_fac = keep.tile([P, PACK, SLOTS], F32, name="y_fac")
-        nc.scalar.activation(ts_sq[:], ts_g[:], SQUARE)
+        ts_turned = bank("b6", "ts_turned")
+        for k in range(2):
+            nc.tensor.transpose(ts_turned[:, q_cols(k)], ts_g[:, q_cols(2 + k)], ident[:])
+        ts_col = keep.tile([P, 2], F32, name="ts_col")
+        ts2_col = keep.tile([P, 2], F32, name="ts2_col")
+        inv_col = keep.tile([P, 2], F32, name="inv_col")
+        nc.scalar.activation(ts_col[:], ts_turned[:, 0 : HSLOTS : QSLOTS], COPY)
+        nc.scalar.activation(ts2_col[:], ts_col[:], SQUARE)
+        nc.vector.reciprocal(inv_col[:], ts_col[:])
+        inv_spread = bank("b7", "inv_spread")
+        for k in range(2):
+            nc.tensor.transpose(inv_spread[:, q_cols(k)], inv_col[:, k : k + 1].to_broadcast([P, P]), ident[:])
+
+        ts_sq = keep.tile([P, HSLOTS], F32, name="ts_sq")
+        a_fac = keep.tile([P, PACK, HSLOTS], F32, name="a_fac")
+        y_fac = [keep.tile([P, PACK, HSLOTS], F32, name=f"y_fac{h}") for h in range(2)]
+        nc.scalar.activation(ts_sq[:], ts_g[:, 0:HSLOTS], SQUARE)
         for s in range(PACK):
-            nc.scalar.activation(y_fac[:, s, :], ts_g[:], COPY, scale=c2[:, s : s + 1])
+            nc.scalar.activation(y_fac[0][:, s, :], ts_g[:, 0:HSLOTS], COPY, scale=c2[:, s : s + 1])
             nc.scalar.activation(a_fac[:, s, :], ts_sq[:], COPY, scale=c1[:, s : s + 1])
+            nc.scalar.activation(y_fac[1][:, s, :], inv_spread[:, 0:HSLOTS], COPY, scale=neg_c2[:, s : s + 1])
 
         gather_plane(1)
 
@@ -155,6 +167,7 @@ def tile_attend_gahead_nag_sq_kernel(tc, wT, mT, xT, y, ts, us, wt, fd, offs, ou
         xr_codes = keep.tile([P, D], U32, name="xr_codes", align_bytes=64)
         xr_scales = keep.tile([P, D], U8, name="xr_scales", align_bytes=64)
         gather_plane(2)
+        nc.vector.scalar_tensor_tensor(neg_fd2[:], fd_c[:], -1.0, fd_c[:], MULT, MULT)
         nc.vector.quantize_mx(xr_codes[:].bitcast(E4M3), xr_scales[:], xr_il[:].rearrange("p d s -> p (d s)"))
         nc.vector.quantize_mx(xd_codes[:].bitcast(E4M3), xd_scales[:], xd_il[:].rearrange("p r t -> p (r t)"))
         gather_plane(3)
@@ -165,89 +178,132 @@ def tile_attend_gahead_nag_sq_kernel(tc, wT, mT, xT, y, ts, us, wt, fd, offs, ou
         def planar(tile):
             return tile.rearrange("p t (c i) -> p c t i", i=RUN)
 
-        g_codes = keep.tile([P, SLOTS], U32, name="g_codes", align_bytes=64)
-        g_scales = keep.tile([P, SLOTS], U8, name="g_scales", align_bytes=64)
-        fd2 = keep.tile([P, PACK], F32, name="fd2")
-        nc.gpsimd.tensor_tensor(fd2[:], fd_c[:], fd_c[:], MULT)
-        nc.gpsimd.tensor_scalar(neg_fd2[:], fd2[:], -1.0, 0.0, MULT, ADD)
-        scores = []
-        y_term = [keep.tile([P, PACK, HSLOTS], F32, name=f"y_term{h}") for h in range(2)]
-        for h in range(2):
-            nc.vector.tensor_tensor(y_term[h][:], y_raw[h][:], y_fac[:, :, h * HSLOTS : (h + 1) * HSLOTS], MULT)
-            w2_il = keep.tile([P, HSLOTS, PACK], BF16, name=f"w2_il{h}", align_bytes=64)
-            nc.scalar.copy(woven(w2_il[:]), planar(w2[h][:]))
-            w2_codes = keep.tile([P, HSLOTS], U32, name=f"w2_codes{h}", align_bytes=64)
-            w2_scales = keep.tile([P, HSLOTS], U8, name=f"w2_scales{h}", align_bytes=64)
-            nc.vector.quantize_mx(w2_codes[:].bitcast(E4M3), w2_scales[:], w2_il[:].rearrange("p n t -> p (n t)"))
-            for k in range(2):
-                a_q = bank(f"a{2 * h + k}", f"a{2 * h + k}")
-                for s in range(PACK):
-                    rows = slice(s * P, (s + 1) * P)
-                    nc.tensor.matmul_mx(
-                        a_q[:, rows],
-                        lhsT=xd_codes[:, rows].bitcast(E4M3),
-                        lhsT_scale=xd_scales[:, rows],
-                        rhs=w2_codes[:, q_cols(k)].bitcast(E4M3),
-                        rhs_scale=w2_scales[:, q_cols(k)],
-                        start=True,
-                        stop=True,
-                    )
-                scores.append(a_q)
+        g_codes = keep.tile([P, PAD + SLOTS], U32, name="g_codes", align_bytes=64)
+        g_scales = keep.tile([P, PAD + SLOTS], U8, name="g_scales", align_bytes=64)
+        nc.vector.memset(g_codes[:, 0:PAD], 0)
+        nc.vector.memset(g_scales[:, 0:PAD].bitcast(U32), 0)
 
-        a_term = [keep.tile([P, PACK, QSLOTS], F32, name=f"a_term{q}", tag=f"a_term{q}") for q in range(QUARTERS)]
-        g_il = [keep.tile([P, QSLOTS, PACK], BF16, name=f"g_il{q}", align_bytes=64) for q in range(QUARTERS)]
-        for q in range(QUARTERS + 2):
-            if q < QUARTERS:
-                nc.vector.tensor_tensor(
-                    a_term[q][:], scores[q][:].rearrange("p (s n) -> p s n", s=PACK), a_fac[:, :, q_cols(q)], MULT
-                )
-            if 1 <= q <= QUARTERS:
-                nc.vector.tensor_tensor(woven(g_il[q - 1][:]), planar(a_term[q - 1][:]), planar(y_term[(q - 1) // 2][:, :, q_cols((q - 1) % 2)]), SUB)
-            if q >= 2:
-                nc.vector.quantize_mx(
-                    g_codes[:, q_cols(q - 2)].bitcast(E5M2),
-                    g_scales[:, q_cols(q - 2)],
-                    g_il[q - 2][:].rearrange("p n s -> p (n s)"),
-                )
+        w2_il = [keep.tile([P, hi - lo, PACK], BF16, name=f"w2_il{lo}", tag=f"w2_il{lo}", align_bytes=64) for lo, hi in pieces]
+        w2_codes = [keep.tile([P, hi - lo], U32, name=f"w2_codes{lo}", align_bytes=64) for lo, hi in pieces]
+        w2_scales = [keep.tile([P, hi - lo], U8, name=f"w2_scales{lo}", align_bytes=64) for lo, hi in pieces]
+        for k in range(3):
+            nc.scalar.copy(woven(w2_il[k][:]), planar(w2[k][:]))
 
-        early_ps = bank("a0", "early_ps")
-        nc.tensor.matmul_mx(
-            early_ps[:],
-            lhsT=g_codes[:, q_cols(0)].bitcast(E5M2),
-            lhsT_scale=g_scales[:, q_cols(0)],
-            rhs=xr_codes[:].bitcast(E4M3),
-            rhs_scale=xr_scales[:],
-            start=True,
-            stop=True,
-        )
-        early_sb = keep.tile([P, EARLY * P], F32, name="early_sb")
-        nc.scalar.copy(early_sb[:], early_ps[:, 0 : EARLY * P])
-        early_back = bank("a1", "early_back")
-        for t in range(EARLY):
-            nc.tensor.transpose(early_back[:, t * P : (t + 1) * P], early_sb[:, t * P : (t + 1) * P], ident[:])
-        early_step = keep.tile([P, EARLY, QSLOTS], F32, name="early_step", tag=f"a_term{QUARTERS - 1}")
-        for t in range(EARLY):
-            nc.scalar.activation(early_step[:, t, :], early_back[:, t * P : (t + 1) * P], COPY, scale=neg_fd2[:, t : t + 1])
-            nc.vector.tensor_tensor(mom_win[t][:].indirect(q_offsets(0)), m_g[t][:, q_cols(0)], early_step[:, t, :], ADD)
+        def quantise_w2(k):
+            nc.vector.quantize_mx(w2_codes[k][:].bitcast(E4M3), w2_scales[k][:], w2_il[k][:].rearrange("p n t -> p (n t)"))
 
-        for t in range(PACK):
-            feats = slice(t * P, (t + 1) * P)
-            dw_ps = bank(f"d{t}", f"dw_ps{t}")
+        def score(out, s, k):
+            rows = slice(s * P, (s + 1) * P)
             nc.tensor.matmul_mx(
-                dw_ps[:],
-                lhsT=xr_codes[:, feats].bitcast(E4M3),
-                lhsT_scale=xr_scales[:, feats],
-                rhs=g_codes[:].bitcast(E5M2),
-                rhs_scale=g_scales[:],
+                out,
+                lhsT=xd_codes[:, rows].bitcast(E4M3),
+                lhsT_scale=xd_scales[:, rows],
+                rhs=w2_codes[k][:].bitcast(E4M3),
+                rhs_scale=w2_scales[k][:],
                 start=True,
                 stop=True,
             )
+
+        a_term = [keep.tile([P, PACK, QSLOTS], F32, name=f"a_term{q}") for q in range(2)]
+        g_il = [keep.tile([P, QSLOTS, PACK], BF16, name=f"g_il{q}", tag=f"g_il{q}", align_bytes=64) for q in range(QUARTERS)]
+        scores = [bank(f"b{q}", f"a{q}") for q in range(2)]
+        late_scores = [bank(f"b{2 + j}", f"a_late{j}") for j in range(2)]
+
+        def form_a_term(q):
+            nc.vector.tensor_tensor(
+                a_term[q][:], scores[q][:].rearrange("p (s n) -> p s n", s=PACK), a_fac[:, :, q_cols(q)], MULT
+            )
+
+        def form_g(q):
+            nc.vector.tensor_tensor(woven(g_il[q][:]), planar(a_term[q][:]), planar(y_term[:, :, q_cols(q)]), SUB)
+
+        def quantise_g(q):
+            cols = slice(PAD + q * QSLOTS, PAD + (q + 1) * QSLOTS)
+            nc.vector.quantize_mx(g_codes[:, cols].bitcast(E5M2), g_scales[:, cols], g_il[q][:].rearrange("p n s -> p (n s)"))
+
+        def gradient_pass(out, t, first_col):
+            feats = slice(t * P, (t + 1) * P)
+            cols = slice(first_col, first_col + SLOTS)
+            nc.tensor.matmul_mx(
+                out,
+                lhsT=xr_codes[:, feats].bitcast(E4M3),
+                lhsT_scale=xr_scales[:, feats],
+                rhs=g_codes[:, cols].bitcast(E5M2),
+                rhs_scale=g_scales[:, cols],
+                start=True,
+                stop=True,
+            )
+
+        for q in range(2):
+            quantise_w2(q)
+            for s in range(PACK):
+                score(scores[q][:, q_cols(s)], s, q)
+        y_term = keep.tile([P, PACK, HSLOTS], F32, name="y_term")
+        nc.vector.tensor_tensor(y_term[:], y_raw[0][:], y_fac[0][:], MULT)
+        quantise_w2(2)
+        for s in range(PACK):
+            score(late_scores[s // 2][:, (s % 2) * HSLOTS : (s % 2 + 1) * HSLOTS], s, 2)
+        a_late = [keep.tile([P, HSLOTS], F32, name=f"a_late_sb{s}") for s in range(PACK)]
+        for s in range(PACK):
+            nc.scalar.activation(
+                a_late[s][:], late_scores[s // 2][:, (s % 2) * HSLOTS : (s % 2 + 1) * HSLOTS], COPY, scale=c1[:, s : s + 1]
+            )
+        summed = [bank(f"b{4 + k}", f"summed{k}") for k in range(2)]
+        for s in range(PACK):
+            for k in range(2):
+                nc.tensor.matmul(summed[k][:, q_cols(s)], a_late[s][:, q_cols(k)], ident[:], start=(s == 0), stop=False, is_transpose=True)
+        for q in range(2):
+            form_a_term(q)
+        for q in range(2):
+            form_g(q)
+        for q in range(2):
+            quantise_g(q)
+
+        early = [bank(f"b{6 + t}", f"early{t}") for t in range(2)]
+        dw_early = [keep.tile([P, HSLOTS], F32, name=f"dw_early{t}") for t in range(2)]
+        for t in range(2):
+            gradient_pass(early[t][:], t, 0)
+            nc.scalar.copy(dw_early[t][:], early[t][:, PAD:SLOTS])
+        step_early0 = keep.tile([P, HSLOTS], F32, name="step_early0")
+        nc.scalar.activation(step_early0[:], early[0][:, PAD:SLOTS], COPY, scale=neg_fd2[:, 0:1])
+
+        y_late = keep.tile([P, PACK, HSLOTS], F32, name="y_late", tag="g_il1", align_bytes=64)
+        nc.vector.tensor_tensor(y_late[:], y_raw[1][:], y_fac[1][:], MULT)
+        g_words = [bank(f"b{k}", f"g_words{k}") for k in range(2)]
+        for k in range(2):
+            for s in range(PACK):
+                nc.tensor.matmul(summed[k][:, q_cols(s)], y_late[:, s, q_cols(k)], ident[:], start=False, stop=(s == PACK - 1), is_transpose=True)
+            g_turned = keep.tile([P, 2, P, 2], BF16, name=f"g_turned{k}")
+            nc.scalar.activation(
+                g_turned[:], summed[k][:].rearrange("i (u e p) -> i u p e", u=2, e=2), COPY, scale=ts2_col[:, k : k + 1]
+            )
+            words = g_turned[:].rearrange("i u p e -> i (u p e)").bitcast(F32)
+            for u in range(2):
+                nc.tensor.transpose(g_words[k][:, q_cols(u)], words[:, q_cols(u)], ident[:])
+        for k in range(2):
+            nc.scalar.copy(
+                g_il[2 + k][:].rearrange("p n s -> p (n s)").bitcast(F32).rearrange("p (n u) -> p n u", u=2),
+                g_words[k][:, 0:HSLOTS].rearrange("p (u n) -> p n u", u=2),
+            )
+
+        for t in range(2):
+            nc.vector.tensor_copy(grad_win[t][:].indirect(offs_of(0, HSLOTS)), dw_early[t][:])
+        nc.vector.tensor_tensor(mom_win[0][:].indirect(offs_of(0, HSLOTS)), m_g[0][:, 0:HSLOTS], step_early0[:], ADD)
+        quantise_g(2)
+        step_early1 = keep.tile([P, HSLOTS], F32, name="step_early1", tag="g_il2", align_bytes=64)
+        nc.scalar.activation(step_early1[:], early[1][:, PAD:SLOTS], COPY, scale=neg_fd2[:, 1:2])
+        quantise_g(3)
+        nc.vector.tensor_tensor(mom_win[1][:].indirect(offs_of(0, HSLOTS)), m_g[1][:, 0:HSLOTS], step_early1[:], ADD)
+
+        for t in range(PACK):
+            dw_ps = bank(f"b{2 + t}", f"dw_ps{t}")
+            gradient_pass(dw_ps[:], t, PAD)
             dw = keep.tile([P, SLOTS], F32, name=f"dw{t}")
             step = keep.tile([P, SLOTS], F32, name=f"step{t}")
-            nc.scalar.copy(dw[:], dw_ps[:])
-            first = QSLOTS if t < EARLY else 0
+            first = HSLOTS if t < 2 else 0
+            nc.scalar.copy(dw[:, first:], dw_ps[:, first:])
             nc.scalar.activation(step[:, first:], dw_ps[:, first:], COPY, scale=neg_fd2[:, t : t + 1])
-            nc.vector.tensor_copy(grad_win[t % 2][:].indirect(offsets[:]), dw[:])
+            nc.vector.tensor_copy(grad_win[t % 2][:].indirect(offs_of(first, SLOTS)), dw[:, first:])
             nc.sync.dma_start(by_plane(out_1)[:, t, :], grad_win[t % 2][:])
-            nc.vector.tensor_tensor(mom_win[t % 2][:].indirect(offsets[:, first // OFFS_PER_COL :]), m_g[t][:, first:], step[:, first:], ADD)
+            nc.vector.tensor_tensor(mom_win[t % 2][:].indirect(offs_of(first, SLOTS)), m_g[t][:, first:], step[:, first:], ADD)
             nc.sync.dma_start(by_plane(out_0)[:, t, :], mom_win[t % 2][:])

@@ -43,7 +43,7 @@ def tile_attend_gahead_nag_sq_kernel(tc, wT, mT, xT, y, ts, us, wt, fd, offs, ou
 
         offsets = keep.tile([P, SLOTS // OFFS_PER_COL], U16, name="offsets")
 
-        m_win = [keep.tile([P, TABLE], F32, name=f"m_win{t}") for t in range(PACK)]
+        m_pair = [keep.tile([P, 2, TABLE], F32, name=f"m_pair{j}") for j in range(2)]
         w_win = [keep.tile([P, TABLE], F32, name=f"w_win{t}") for t in range(PACK)]
         x_raw = keep.tile([P, PACK, R], F32, name="x_raw")
         y_raw = [keep.tile([P, PACK, HSLOTS], F32, name=f"y_raw{h}") for h in range(2)]
@@ -59,12 +59,13 @@ def tile_attend_gahead_nag_sq_kernel(tc, wT, mT, xT, y, ts, us, wt, fd, offs, ou
         nc.scalar.dma_start(us_c[:], by_plane(us)[:, :, 0])
         nc.scalar.dma_start(wt_c[:], by_plane(wt)[:, :, 0])
         for t in range(PACK):
-            nc.sync.dma_start(m_win[t][:], by_plane(mT)[:, t, :])
+            if t % 2 == 0:
+                nc.sync.dma_start(m_pair[t // 2][:], by_plane(mT)[:, t : t + 2, :])
             nc.sync.dma_start(w_win[t][:], by_plane(wT)[:, t, :])
-            if t == 1:
-                nc.sync.dma_start(fd_c[:], by_plane(fd)[:, :, 0])
         for h in range(2):
             nc.sync.dma_start(y_raw[h][:], by_plane(y)[:, :, h * HSLOTS : (h + 1) * HSLOTS])
+
+        nc.sync.dma_start(fd_c[:], by_plane(fd)[:, :, 0])
 
         grad_win = [keep.tile([P, TABLE], F32, name=f"grad_win{k}") for k in range(2)]
         mom_win = [keep.tile([P, TABLE], F32, name=f"mom_win{k}") for k in range(2)]
@@ -101,7 +102,7 @@ def tile_attend_gahead_nag_sq_kernel(tc, wT, mT, xT, y, ts, us, wt, fd, offs, ou
             return slice(q * QSLOTS, (q + 1) * QSLOTS)
 
         def gather_plane(t):
-            nc.vector.tensor_copy(m_g[t][:], m_win[t][:].indirect(offsets[:]))
+            nc.vector.tensor_copy(m_g[t][:], m_pair[t // 2][:, t % 2, :].indirect(offsets[:]))
             for k in range(3):
                 lo, hi = pieces[k]
                 nc.vector.tensor_tensor(w2[k][:, t, :], w_win[t][:].indirect(offs_of(lo, hi)), m_g[t][:, lo:hi], ADD)
@@ -167,7 +168,6 @@ def tile_attend_gahead_nag_sq_kernel(tc, wT, mT, xT, y, ts, us, wt, fd, offs, ou
         xr_codes = keep.tile([P, D], U32, name="xr_codes", align_bytes=64)
         xr_scales = keep.tile([P, D], U8, name="xr_scales", align_bytes=64)
         gather_plane(2)
-        nc.vector.scalar_tensor_tensor(neg_fd2[:], fd_c[:], -1.0, fd_c[:], MULT, MULT)
         nc.vector.quantize_mx(xr_codes[:].bitcast(E4M3), xr_scales[:], xr_il[:].rearrange("p d s -> p (d s)"))
         nc.vector.quantize_mx(xd_codes[:].bitcast(E4M3), xd_scales[:], xd_il[:].rearrange("p r t -> p (r t)"))
         gather_plane(3)
@@ -183,6 +183,9 @@ def tile_attend_gahead_nag_sq_kernel(tc, wT, mT, xT, y, ts, us, wt, fd, offs, ou
         nc.vector.memset(g_codes[:, 0:PAD], 0)
         nc.vector.memset(g_scales[:, 0:PAD].bitcast(U32), 0)
 
+        fd2 = keep.tile([P, PACK], F32, name="fd2")
+        nc.gpsimd.tensor_tensor(fd2[:], fd_c[:], fd_c[:], MULT)
+        nc.gpsimd.tensor_scalar(neg_fd2[:], fd2[:], -1.0, 0.0, MULT, ADD)
         w2_il = [keep.tile([P, hi - lo, PACK], BF16, name=f"w2_il{lo}", tag=f"w2_il{lo}", align_bytes=64) for lo, hi in pieces]
         w2_codes = [keep.tile([P, hi - lo], U32, name=f"w2_codes{lo}", align_bytes=64) for lo, hi in pieces]
         w2_scales = [keep.tile([P, hi - lo], U8, name=f"w2_scales{lo}", align_bytes=64) for lo, hi in pieces]
@@ -269,7 +272,7 @@ def tile_attend_gahead_nag_sq_kernel(tc, wT, mT, xT, y, ts, us, wt, fd, offs, ou
 
         y_late = keep.tile([P, PACK, HSLOTS], F32, name="y_late", tag="g_il1", align_bytes=64)
         nc.vector.tensor_tensor(y_late[:], y_raw[1][:], y_fac[1][:], MULT)
-        g_words = [bank(f"b{k}", f"g_words{k}") for k in range(2)]
+        g_words = bank("b0", "g_words")
         for k in range(2):
             for s in range(PACK):
                 nc.tensor.matmul(summed[k][:, q_cols(s)], y_late[:, s, q_cols(k)], ident[:], start=False, stop=(s == PACK - 1), is_transpose=True)
@@ -279,11 +282,11 @@ def tile_attend_gahead_nag_sq_kernel(tc, wT, mT, xT, y, ts, us, wt, fd, offs, ou
             )
             words = g_turned[:].rearrange("i u p e -> i (u p e)").bitcast(F32)
             for u in range(2):
-                nc.tensor.transpose(g_words[k][:, q_cols(u)], words[:, q_cols(u)], ident[:])
+                nc.tensor.transpose(g_words[:, q_cols(2 * k + u)], words[:, q_cols(u)], ident[:])
         for k in range(2):
             nc.scalar.copy(
                 g_il[2 + k][:].rearrange("p n s -> p (n s)").bitcast(F32).rearrange("p (n u) -> p n u", u=2),
-                g_words[k][:, 0:HSLOTS].rearrange("p (u n) -> p n u", u=2),
+                g_words[:, k * HSLOTS : (k + 1) * HSLOTS].rearrange("p (u n) -> p n u", u=2),
             )
 
         for t in range(2):

@@ -105,7 +105,9 @@ def tile_attend_gahead_nag_sq_kernel(tc, wT, mT, xT, y, ts, us, wt, fd, offs, ou
             nc.vector.tensor_copy(m_g[t][:], m_pair[t // 2][:, t % 2, :].indirect(offsets[:]))
             for k in range(3):
                 lo, hi = pieces[k]
-                nc.vector.tensor_tensor(w2[k][:, t, :], w_win[t][:].indirect(offs_of(lo, hi)), m_g[t][:, lo:hi], ADD)
+                if t == PACK - 1:
+                    hi = lo + QSLOTS
+                nc.vector.tensor_tensor(w2[k][:, t, 0 : hi - lo], w_win[t][:].indirect(offs_of(lo, hi)), m_g[t][:, lo:hi], ADD)
 
         nc.vector.tensor_tensor(c2[:], wt_c[:], us_c[:], MULT)
         nc.vector.tensor_tensor(c1[:], c2[:], us_c[:], MULT)
@@ -186,11 +188,12 @@ def tile_attend_gahead_nag_sq_kernel(tc, wT, mT, xT, y, ts, us, wt, fd, offs, ou
         fd2 = keep.tile([P, PACK], F32, name="fd2")
         nc.gpsimd.tensor_tensor(fd2[:], fd_c[:], fd_c[:], MULT)
         nc.gpsimd.tensor_scalar(neg_fd2[:], fd2[:], -1.0, 0.0, MULT, ADD)
-        w2_il = [keep.tile([P, hi - lo, PACK], BF16, name=f"w2_il{lo}", tag=f"w2_il{lo}", align_bytes=64) for lo, hi in pieces]
-        w2_codes = [keep.tile([P, hi - lo], U32, name=f"w2_codes{lo}", align_bytes=64) for lo, hi in pieces]
-        w2_scales = [keep.tile([P, hi - lo], U8, name=f"w2_scales{lo}", align_bytes=64) for lo, hi in pieces]
-        for k in range(3):
-            nc.scalar.copy(woven(w2_il[k][:]), planar(w2[k][:]))
+        w2_il = [keep.tile([P, QSLOTS, PACK], BF16, name=f"w2_il{q}", align_bytes=64) for q in range(QUARTERS)]
+        w2_codes = [keep.tile([P, QSLOTS], U32, name=f"w2_codes{q}", align_bytes=64) for q in range(QUARTERS)]
+        w2_scales = [keep.tile([P, QSLOTS], U8, name=f"w2_scales{q}", align_bytes=64) for q in range(QUARTERS)]
+        nc.scalar.copy(woven(w2_il[3][:, :, 0:3]), planar(w2[2][:, 0:3, QSLOTS:HSLOTS]))
+        for q in range(3):
+            nc.scalar.copy(woven(w2_il[q][:]), planar(w2[q][:, :, 0:QSLOTS]))
 
         def quantise_w2(k):
             nc.vector.quantize_mx(w2_codes[k][:].bitcast(E4M3), w2_scales[k][:], w2_il[k][:].rearrange("p n t -> p (n t)"))
@@ -218,7 +221,7 @@ def tile_attend_gahead_nag_sq_kernel(tc, wT, mT, xT, y, ts, us, wt, fd, offs, ou
             )
 
         def form_g(q):
-            nc.vector.tensor_tensor(woven(g_il[q][:]), planar(a_term[q][:]), planar(y_term[:, :, q_cols(q)]), SUB)
+            nc.vector.tensor_tensor(woven(g_il[q][:]), planar(a_term[q][:]), planar(y_term[q][:]), SUB)
 
         def quantise_g(q):
             cols = slice(PAD + q * QSLOTS, PAD + (q + 1) * QSLOTS)
@@ -237,24 +240,31 @@ def tile_attend_gahead_nag_sq_kernel(tc, wT, mT, xT, y, ts, us, wt, fd, offs, ou
                 stop=True,
             )
 
+        y_term = [keep.tile([P, PACK, QSLOTS], F32, name=f"y_term{q}") for q in range(2)]
         for q in range(2):
             quantise_w2(q)
             for s in range(PACK):
                 score(scores[q][:, q_cols(s)], s, q)
-        y_term = keep.tile([P, PACK, HSLOTS], F32, name="y_term")
-        nc.vector.tensor_tensor(y_term[:], y_raw[0][:], y_fac[0][:], MULT)
-        quantise_w2(2)
-        for s in range(PACK):
-            score(late_scores[s // 2][:, (s % 2) * HSLOTS : (s % 2 + 1) * HSLOTS], s, 2)
-        a_late = [keep.tile([P, HSLOTS], F32, name=f"a_late_sb{s}") for s in range(PACK)]
-        for s in range(PACK):
-            nc.scalar.activation(
-                a_late[s][:], late_scores[s // 2][:, (s % 2) * HSLOTS : (s % 2 + 1) * HSLOTS], COPY, scale=c1[:, s : s + 1]
-            )
+            nc.vector.tensor_tensor(y_term[q][:], y_raw[0][:, :, q_cols(q)], y_fac[0][:, :, q_cols(q)], MULT)
+        a_late = [keep.tile([P, PACK, QSLOTS], F32, name=f"a_late_sb{k}") for k in range(2)]
         summed = [bank(f"b{4 + k}", f"summed{k}") for k in range(2)]
-        for s in range(PACK):
-            for k in range(2):
-                nc.tensor.matmul(summed[k][:, q_cols(s)], a_late[s][:, q_cols(k)], ident[:], start=(s == 0), stop=False, is_transpose=True)
+
+        def late_score(k):
+            quantise_w2(2 + k)
+            for s in range(PACK):
+                score(late_scores[k][:, q_cols(s)], s, 2 + k)
+            for s in range(PACK):
+                nc.scalar.activation(a_late[k][:, s, :], late_scores[k][:, q_cols(s)], COPY, scale=c1[:, s : s + 1])
+
+        def turn_into_sum(k, term, opens):
+            for s in range(PACK):
+                nc.tensor.matmul(
+                    summed[k][:, q_cols(s)], term[:, s, :], ident[:],
+                    start=(opens and s == 0), stop=(not opens and s == PACK - 1), is_transpose=True,
+                )
+
+        late_score(0)
+        turn_into_sum(0, a_late[0][:], True)
         for q in range(2):
             form_a_term(q)
         for q in range(2):
@@ -270,12 +280,17 @@ def tile_attend_gahead_nag_sq_kernel(tc, wT, mT, xT, y, ts, us, wt, fd, offs, ou
         step_early0 = keep.tile([P, HSLOTS], F32, name="step_early0")
         nc.scalar.activation(step_early0[:], early[0][:, PAD:SLOTS], COPY, scale=neg_fd2[:, 0:1])
 
+        w2_last = keep.tile([P, QSLOTS], F32, name="w2_last", tag="g_il0", align_bytes=64)
+        nc.vector.tensor_tensor(w2_last[:], w_win[3][:].indirect(offs_of(SLOTS - QSLOTS, SLOTS)), m_g[3][:, q_cols(3)], ADD)
+        nc.scalar.copy(w2_il[3][:, :, 3], w2_last[:])
         y_late = keep.tile([P, PACK, HSLOTS], F32, name="y_late", tag="g_il1", align_bytes=64)
         nc.vector.tensor_tensor(y_late[:], y_raw[1][:], y_fac[1][:], MULT)
+        late_score(1)
         g_words = bank("b0", "g_words")
         for k in range(2):
-            for s in range(PACK):
-                nc.tensor.matmul(summed[k][:, q_cols(s)], y_late[:, s, q_cols(k)], ident[:], start=False, stop=(s == PACK - 1), is_transpose=True)
+            turn_into_sum(k, y_late[:, :, q_cols(k)], k == 1)
+            if k == 1:
+                turn_into_sum(k, a_late[1][:], False)
             g_turned = keep.tile([P, 2, P, 2], BF16, name=f"g_turned{k}")
             nc.scalar.activation(
                 g_turned[:], summed[k][:].rearrange("i (u e p) -> i u p e", u=2, e=2), COPY, scale=ts2_col[:, k : k + 1]

@@ -16,11 +16,14 @@ E5M2 = mybir.dt.float8_e5m2_x4
 MULT = mybir.AluOpType.mult
 ADD = mybir.AluOpType.add
 SUB = mybir.AluOpType.subtract
+IS_EQUAL = mybir.AluOpType.is_equal
 COPY = mybir.ActivationFunctionType.Copy
 SQUARE = mybir.ActivationFunctionType.Square
 
 P = 128
 PACK = 4
+LAST = PACK - 1
+BANK = 512
 QUARTERS = 4
 QSLOTS = SLOTS // QUARTERS
 HSLOTS = SLOTS // 2
@@ -38,10 +41,22 @@ def tile_attend_gahead_nag_sq_kernel(tc, wT, mT, xT, y, ts, us, wt, fd, offs, ou
         def by_plane(ap):
             return ap.rearrange("(p t) c -> p t c", t=PACK)
 
-        def bank(tag, name):
-            return psum.tile([P, 512], F32, name=name, tag=tag)
+        def bank(number, name):
+            return psum.tile([P, BANK], F32, name=name, tag=f"bank{number}")
+
+        def q_cols(q):
+            return slice(q * QSLOTS, (q + 1) * QSLOTS)
+
+        def woven(tile):
+            return tile.rearrange("p (c i) t -> p c t i", i=RUN)
+
+        def planar(tile):
+            return tile.rearrange("p t (c i) -> p c t i", i=RUN)
 
         offsets = keep.tile([P, SLOTS // OFFS_PER_COL], U16, name="offsets")
+
+        def offs_of(lo, hi):
+            return offsets[:, lo // OFFS_PER_COL : hi // OFFS_PER_COL]
 
         m_pair = [keep.tile([P, 2, TABLE], F32, name=f"m_pair{j}") for j in range(2)]
         w_win = [keep.tile([P, TABLE], F32, name=f"w_win{t}") for t in range(PACK)]
@@ -64,7 +79,6 @@ def tile_attend_gahead_nag_sq_kernel(tc, wT, mT, xT, y, ts, us, wt, fd, offs, ou
             nc.sync.dma_start(w_win[t][:], by_plane(wT)[:, t, :])
         for h in range(2):
             nc.sync.dma_start(y_raw[h][:], by_plane(y)[:, :, h * HSLOTS : (h + 1) * HSLOTS])
-
         nc.sync.dma_start(fd_c[:], by_plane(fd)[:, :, 0])
 
         grad_win = [keep.tile([P, TABLE], F32, name=f"grad_win{k}") for k in range(2)]
@@ -76,7 +90,7 @@ def tile_attend_gahead_nag_sq_kernel(tc, wT, mT, xT, y, ts, us, wt, fd, offs, ou
             nc.vector.memset(mom_win[k][:], 0.0)
 
         for b in range(4):
-            spread = bank(f"b{b}", f"ts_spread{b}")
+            spread = bank(b, f"ts_spread{b}")
             for k in range(4):
                 j = 4 * b + k
                 nc.tensor.transpose(spread[:, k * P : (k + 1) * P], ts_row[:, j : j + 1].to_broadcast([P, P]), ident[:])
@@ -86,32 +100,24 @@ def tile_attend_gahead_nag_sq_kernel(tc, wT, mT, xT, y, ts, us, wt, fd, offs, ou
                 COPY,
             )
 
-        c2 = keep.tile([P, PACK], F32, name="c2")
-        c1 = keep.tile([P, PACK], F32, name="c1")
-        neg_c2 = keep.tile([P, PACK], F32, name="neg_c2")
+        y_row = keep.tile([P, PACK], F32, name="y_row")
+        a_row = keep.tile([P, PACK], F32, name="a_row")
+        neg_y_row = keep.tile([P, PACK], F32, name="neg_y_row")
         neg_fd2 = keep.tile([P, PACK], F32, name="neg_fd2")
 
         m_g = [keep.tile([P, SLOTS], F32, name=f"m_g{t}") for t in range(PACK)]
         pieces = [(0, QSLOTS), (QSLOTS, HSLOTS), (HSLOTS, SLOTS)]
         w2 = [keep.tile([P, PACK, hi - lo], F32, name=f"w2_{lo}") for lo, hi in pieces]
 
-        def offs_of(lo, hi):
-            return offsets[:, lo // OFFS_PER_COL : hi // OFFS_PER_COL]
-
-        def q_cols(q):
-            return slice(q * QSLOTS, (q + 1) * QSLOTS)
-
         def gather_plane(t):
             nc.vector.tensor_copy(m_g[t][:], m_pair[t // 2][:, t % 2, :].indirect(offsets[:]))
-            for k in range(3):
-                lo, hi = pieces[k]
-                if t == PACK - 1:
-                    hi = lo + QSLOTS
-                nc.vector.tensor_tensor(w2[k][:, t, 0 : hi - lo], w_win[t][:].indirect(offs_of(lo, hi)), m_g[t][:, lo:hi], ADD)
+            for piece, (lo, hi) in zip(w2, pieces):
+                end = lo + QSLOTS if t == LAST else hi
+                nc.vector.tensor_tensor(piece[:, t, 0 : end - lo], w_win[t][:].indirect(offs_of(lo, end)), m_g[t][:, lo:end], ADD)
 
-        nc.vector.tensor_tensor(c2[:], wt_c[:], us_c[:], MULT)
-        nc.vector.tensor_tensor(c1[:], c2[:], us_c[:], MULT)
-        nc.vector.tensor_scalar(neg_c2[:], c2[:], -1.0, 0.0, MULT, ADD)
+        nc.vector.tensor_tensor(y_row[:], wt_c[:], us_c[:], MULT)
+        nc.vector.tensor_tensor(a_row[:], y_row[:], us_c[:], MULT)
+        nc.vector.tensor_scalar(neg_y_row[:], y_row[:], -1.0, 0.0, MULT, ADD)
         ts_g = keep.tile([P, SLOTS], F32, name="ts_g")
         nc.vector.tensor_copy(ts_g[:], ts_win[:].indirect(offsets[:]))
         gather_plane(0)
@@ -121,19 +127,20 @@ def tile_attend_gahead_nag_sq_kernel(tc, wT, mT, xT, y, ts, us, wt, fd, offs, ou
         x_words = x_bf[:].rearrange("p t r -> p (t r)").bitcast(F32)
         xr_il = keep.tile([P, D, PACK], BF16, name="xr_il", align_bytes=64)
         xr_words = xr_il[:].rearrange("p d s -> p (d s)").bitcast(F32)
+        words_per_plane = R // 2
         for b in range(2):
-            xt = bank(f"b{4 + b}", f"x_turned{b}")
+            x_turned = bank(4 + b, f"x_turned{b}")
             for k in range(2):
                 t = 2 * b + k
                 for u in range(2):
                     nc.tensor.transpose(
-                        xt[:, (2 * k + u) * P : (2 * k + u + 1) * P],
-                        x_words[:, t * 256 + u : (t + 1) * 256 : 2],
+                        x_turned[:, (2 * k + u) * P : (2 * k + u + 1) * P],
+                        x_words[:, t * words_per_plane + u : (t + 1) * words_per_plane : 2],
                         ident[:],
                     )
             nc.scalar.copy(
-                xr_words[:, b * 512 : (b + 1) * 512].rearrange("p (k d u) -> p k d u", k=2, u=2),
-                xt[:].rearrange("p (k u d) -> p k d u", k=2, u=2),
+                xr_words[:, b * BANK : (b + 1) * BANK].rearrange("p (k d u) -> p k d u", k=2, u=2),
+                x_turned[:].rearrange("p (k u d) -> p k d u", k=2, u=2),
             )
         xd_il = keep.tile([P, R, PACK], BF16, name="xd_il", align_bytes=64)
         nc.scalar.copy(
@@ -141,16 +148,18 @@ def tile_attend_gahead_nag_sq_kernel(tc, wT, mT, xT, y, ts, us, wt, fd, offs, ou
             x_bf[:].rearrange("p t (r s) -> p s r t", s=PACK),
         )
 
-        ts_turned = bank("b6", "ts_turned")
+        ts_turned = bank(6, "ts_turned")
         for k in range(2):
             nc.tensor.transpose(ts_turned[:, q_cols(k)], ts_g[:, q_cols(2 + k)], ident[:])
         ts_col = keep.tile([P, 2], F32, name="ts_col")
         ts2_col = keep.tile([P, 2], F32, name="ts2_col")
+        nonzero_col = keep.tile([P, 2], F32, name="nonzero_col")
         inv_col = keep.tile([P, 2], F32, name="inv_col")
-        nc.scalar.activation(ts_col[:], ts_turned[:, 0 : HSLOTS : QSLOTS], COPY)
+        nc.scalar.activation(ts_col[:], ts_turned[:, 0:HSLOTS:QSLOTS], COPY)
         nc.scalar.activation(ts2_col[:], ts_col[:], SQUARE)
-        nc.vector.reciprocal(inv_col[:], ts_col[:])
-        inv_spread = bank("b7", "inv_spread")
+        nc.vector.scalar_tensor_tensor(nonzero_col[:], ts_col[:], 0.0, ts_col[:], IS_EQUAL, ADD)
+        nc.vector.reciprocal(inv_col[:], nonzero_col[:])
+        inv_spread = bank(7, "inv_spread")
         for k in range(2):
             nc.tensor.transpose(inv_spread[:, q_cols(k)], inv_col[:, k : k + 1].to_broadcast([P, P]), ident[:])
 
@@ -159,9 +168,9 @@ def tile_attend_gahead_nag_sq_kernel(tc, wT, mT, xT, y, ts, us, wt, fd, offs, ou
         y_fac = [keep.tile([P, PACK, HSLOTS], F32, name=f"y_fac{h}") for h in range(2)]
         nc.scalar.activation(ts_sq[:], ts_g[:, 0:HSLOTS], SQUARE)
         for s in range(PACK):
-            nc.scalar.activation(y_fac[0][:, s, :], ts_g[:, 0:HSLOTS], COPY, scale=c2[:, s : s + 1])
-            nc.scalar.activation(a_fac[:, s, :], ts_sq[:], COPY, scale=c1[:, s : s + 1])
-            nc.scalar.activation(y_fac[1][:, s, :], inv_spread[:, 0:HSLOTS], COPY, scale=neg_c2[:, s : s + 1])
+            nc.scalar.activation(y_fac[0][:, s, :], ts_g[:, 0:HSLOTS], COPY, scale=y_row[:, s : s + 1])
+            nc.scalar.activation(a_fac[:, s, :], ts_sq[:], COPY, scale=a_row[:, s : s + 1])
+            nc.scalar.activation(y_fac[1][:, s, :], inv_spread[:, 0:HSLOTS], COPY, scale=neg_y_row[:, s : s + 1])
 
         gather_plane(1)
 
@@ -172,13 +181,7 @@ def tile_attend_gahead_nag_sq_kernel(tc, wT, mT, xT, y, ts, us, wt, fd, offs, ou
         gather_plane(2)
         nc.vector.quantize_mx(xr_codes[:].bitcast(E4M3), xr_scales[:], xr_il[:].rearrange("p d s -> p (d s)"))
         nc.vector.quantize_mx(xd_codes[:].bitcast(E4M3), xd_scales[:], xd_il[:].rearrange("p r t -> p (r t)"))
-        gather_plane(3)
-
-        def woven(tile):
-            return tile.rearrange("p (c i) t -> p c t i", i=RUN)
-
-        def planar(tile):
-            return tile.rearrange("p t (c i) -> p c t i", i=RUN)
+        gather_plane(LAST)
 
         g_codes = keep.tile([P, PAD + SLOTS], U32, name="g_codes", align_bytes=64)
         g_scales = keep.tile([P, PAD + SLOTS], U8, name="g_scales", align_bytes=64)
@@ -188,40 +191,31 @@ def tile_attend_gahead_nag_sq_kernel(tc, wT, mT, xT, y, ts, us, wt, fd, offs, ou
         fd2 = keep.tile([P, PACK], F32, name="fd2")
         nc.gpsimd.tensor_tensor(fd2[:], fd_c[:], fd_c[:], MULT)
         nc.gpsimd.tensor_scalar(neg_fd2[:], fd2[:], -1.0, 0.0, MULT, ADD)
+
         w2_il = [keep.tile([P, QSLOTS, PACK], BF16, name=f"w2_il{q}", align_bytes=64) for q in range(QUARTERS)]
         w2_codes = [keep.tile([P, QSLOTS], U32, name=f"w2_codes{q}", align_bytes=64) for q in range(QUARTERS)]
         w2_scales = [keep.tile([P, QSLOTS], U8, name=f"w2_scales{q}", align_bytes=64) for q in range(QUARTERS)]
-        nc.scalar.copy(woven(w2_il[3][:, :, 0:3]), planar(w2[2][:, 0:3, QSLOTS:HSLOTS]))
+        nc.scalar.copy(woven(w2_il[3][:, :, 0:LAST]), planar(w2[2][:, 0:LAST, QSLOTS:HSLOTS]))
         for q in range(3):
             nc.scalar.copy(woven(w2_il[q][:]), planar(w2[q][:, :, 0:QSLOTS]))
 
-        def quantise_w2(k):
-            nc.vector.quantize_mx(w2_codes[k][:].bitcast(E4M3), w2_scales[k][:], w2_il[k][:].rearrange("p n t -> p (n t)"))
-
-        def score(out, s, k):
-            rows = slice(s * P, (s + 1) * P)
-            nc.tensor.matmul_mx(
-                out,
-                lhsT=xd_codes[:, rows].bitcast(E4M3),
-                lhsT_scale=xd_scales[:, rows],
-                rhs=w2_codes[k][:].bitcast(E4M3),
-                rhs_scale=w2_scales[k][:],
-                start=True,
-                stop=True,
-            )
-
         a_term = [keep.tile([P, PACK, QSLOTS], F32, name=f"a_term{q}") for q in range(2)]
         g_il = [keep.tile([P, QSLOTS, PACK], BF16, name=f"g_il{q}", tag=f"g_il{q}", align_bytes=64) for q in range(QUARTERS)]
-        scores = [bank(f"b{q}", f"a{q}") for q in range(2)]
-        late_scores = [bank(f"b{2 + j}", f"a_late{j}") for j in range(2)]
+        scores = [bank(q, f"scores{q}") for q in range(QUARTERS)]
 
-        def form_a_term(q):
-            nc.vector.tensor_tensor(
-                a_term[q][:], scores[q][:].rearrange("p (s n) -> p s n", s=PACK), a_fac[:, :, q_cols(q)], MULT
-            )
-
-        def form_g(q):
-            nc.vector.tensor_tensor(woven(g_il[q][:]), planar(a_term[q][:]), planar(y_term[q][:]), SUB)
+        def score_quarter(q):
+            nc.vector.quantize_mx(w2_codes[q][:].bitcast(E4M3), w2_scales[q][:], w2_il[q][:].rearrange("p n t -> p (n t)"))
+            for s in range(PACK):
+                rows = slice(s * P, (s + 1) * P)
+                nc.tensor.matmul_mx(
+                    scores[q][:, q_cols(s)],
+                    lhsT=xd_codes[:, rows].bitcast(E4M3),
+                    lhsT_scale=xd_scales[:, rows],
+                    rhs=w2_codes[q][:].bitcast(E4M3),
+                    rhs_scale=w2_scales[q][:],
+                    start=True,
+                    stop=True,
+                )
 
         def quantise_g(q):
             cols = slice(PAD + q * QSLOTS, PAD + (q + 1) * QSLOTS)
@@ -242,37 +236,40 @@ def tile_attend_gahead_nag_sq_kernel(tc, wT, mT, xT, y, ts, us, wt, fd, offs, ou
 
         y_term = [keep.tile([P, PACK, QSLOTS], F32, name=f"y_term{q}") for q in range(2)]
         for q in range(2):
-            quantise_w2(q)
-            for s in range(PACK):
-                score(scores[q][:, q_cols(s)], s, q)
+            score_quarter(q)
             nc.vector.tensor_tensor(y_term[q][:], y_raw[0][:, :, q_cols(q)], y_fac[0][:, :, q_cols(q)], MULT)
-        a_late = [keep.tile([P, PACK, QSLOTS], F32, name=f"a_late_sb{k}") for k in range(2)]
-        summed = [bank(f"b{4 + k}", f"summed{k}") for k in range(2)]
+        a_scaled = [keep.tile([P, PACK, QSLOTS], F32, name=f"a_scaled{k}") for k in range(2)]
+        summed = [bank(4 + k, f"summed{k}") for k in range(2)]
 
-        def late_score(k):
-            quantise_w2(2 + k)
+        def score_and_scale(k):
+            score_quarter(2 + k)
             for s in range(PACK):
-                score(late_scores[k][:, q_cols(s)], s, 2 + k)
-            for s in range(PACK):
-                nc.scalar.activation(a_late[k][:, s, :], late_scores[k][:, q_cols(s)], COPY, scale=c1[:, s : s + 1])
+                nc.scalar.activation(a_scaled[k][:, s, :], scores[2 + k][:, q_cols(s)], COPY, scale=a_row[:, s : s + 1])
 
         def turn_into_sum(k, term, opens):
             for s in range(PACK):
                 nc.tensor.matmul(
-                    summed[k][:, q_cols(s)], term[:, s, :], ident[:],
-                    start=(opens and s == 0), stop=(not opens and s == PACK - 1), is_transpose=True,
+                    summed[k][:, q_cols(s)],
+                    term[:, s, :],
+                    ident[:],
+                    start=(opens and s == 0),
+                    stop=(not opens and s == PACK - 1),
+                    is_transpose=True,
                 )
 
-        late_score(0)
-        turn_into_sum(0, a_late[0][:], True)
+        score_and_scale(0)
+        turn_into_sum(0, a_scaled[0][:], opens=True)
+
         for q in range(2):
-            form_a_term(q)
+            nc.vector.tensor_tensor(
+                a_term[q][:], scores[q][:].rearrange("p (s n) -> p s n", s=PACK), a_fac[:, :, q_cols(q)], MULT
+            )
         for q in range(2):
-            form_g(q)
+            nc.vector.tensor_tensor(woven(g_il[q][:]), planar(a_term[q][:]), planar(y_term[q][:]), SUB)
         for q in range(2):
             quantise_g(q)
 
-        early = [bank(f"b{6 + t}", f"early{t}") for t in range(2)]
+        early = [bank(6 + t, f"early{t}") for t in range(2)]
         dw_early = [keep.tile([P, HSLOTS], F32, name=f"dw_early{t}") for t in range(2)]
         for t in range(2):
             gradient_pass(early[t][:], t, 0)
@@ -281,16 +278,13 @@ def tile_attend_gahead_nag_sq_kernel(tc, wT, mT, xT, y, ts, us, wt, fd, offs, ou
         nc.scalar.activation(step_early0[:], early[0][:, PAD:SLOTS], COPY, scale=neg_fd2[:, 0:1])
 
         w2_last = keep.tile([P, QSLOTS], F32, name="w2_last", tag="g_il0", align_bytes=64)
-        nc.vector.tensor_tensor(w2_last[:], w_win[3][:].indirect(offs_of(SLOTS - QSLOTS, SLOTS)), m_g[3][:, q_cols(3)], ADD)
-        nc.scalar.copy(w2_il[3][:, :, 3], w2_last[:])
-        y_late = keep.tile([P, PACK, HSLOTS], F32, name="y_late", tag="g_il1", align_bytes=64)
-        nc.vector.tensor_tensor(y_late[:], y_raw[1][:], y_fac[1][:], MULT)
-        late_score(1)
-        g_words = bank("b0", "g_words")
-        for k in range(2):
-            turn_into_sum(k, y_late[:, :, q_cols(k)], k == 1)
-            if k == 1:
-                turn_into_sum(k, a_late[1][:], False)
+        nc.vector.tensor_tensor(w2_last[:], w_win[LAST][:].indirect(offs_of(SLOTS - QSLOTS, SLOTS)), m_g[LAST][:, q_cols(3)], ADD)
+        nc.scalar.copy(w2_il[3][:, :, LAST], w2_last[:])
+        y_scaled = keep.tile([P, PACK, HSLOTS], F32, name="y_scaled", tag="g_il1", align_bytes=64)
+        nc.vector.tensor_tensor(y_scaled[:], y_raw[1][:], y_fac[1][:], MULT)
+        score_and_scale(1)
+
+        def round_and_turn_back(k):
             g_turned = keep.tile([P, 2, P, 2], BF16, name=f"g_turned{k}")
             nc.scalar.activation(
                 g_turned[:], summed[k][:].rearrange("i (u e p) -> i u p e", u=2, e=2), COPY, scale=ts2_col[:, k : k + 1]
@@ -298,27 +292,35 @@ def tile_attend_gahead_nag_sq_kernel(tc, wT, mT, xT, y, ts, us, wt, fd, offs, ou
             words = g_turned[:].rearrange("i u p e -> i (u p e)").bitcast(F32)
             for u in range(2):
                 nc.tensor.transpose(g_words[:, q_cols(2 * k + u)], words[:, q_cols(u)], ident[:])
+
+        g_words = bank(0, "g_words")
+        turn_into_sum(0, y_scaled[:, :, q_cols(0)], opens=False)
+        round_and_turn_back(0)
+        turn_into_sum(1, y_scaled[:, :, q_cols(1)], opens=True)
+        turn_into_sum(1, a_scaled[1][:], opens=False)
+        round_and_turn_back(1)
         for k in range(2):
             nc.scalar.copy(
                 g_il[2 + k][:].rearrange("p n s -> p (n s)").bitcast(F32).rearrange("p (n u) -> p n u", u=2),
                 g_words[:, k * HSLOTS : (k + 1) * HSLOTS].rearrange("p (u n) -> p n u", u=2),
             )
 
+        direct = offs_of(0, HSLOTS)
         for t in range(2):
-            nc.vector.tensor_copy(grad_win[t][:].indirect(offs_of(0, HSLOTS)), dw_early[t][:])
-        nc.vector.tensor_tensor(mom_win[0][:].indirect(offs_of(0, HSLOTS)), m_g[0][:, 0:HSLOTS], step_early0[:], ADD)
+            nc.vector.tensor_copy(grad_win[t][:].indirect(direct), dw_early[t][:])
+        nc.vector.tensor_tensor(mom_win[0][:].indirect(direct), m_g[0][:, 0:HSLOTS], step_early0[:], ADD)
         quantise_g(2)
         step_early1 = keep.tile([P, HSLOTS], F32, name="step_early1", tag="g_il2", align_bytes=64)
         nc.scalar.activation(step_early1[:], early[1][:, PAD:SLOTS], COPY, scale=neg_fd2[:, 1:2])
         quantise_g(3)
-        nc.vector.tensor_tensor(mom_win[1][:].indirect(offs_of(0, HSLOTS)), m_g[1][:, 0:HSLOTS], step_early1[:], ADD)
+        nc.vector.tensor_tensor(mom_win[1][:].indirect(direct), m_g[1][:, 0:HSLOTS], step_early1[:], ADD)
 
         for t in range(PACK):
-            dw_ps = bank(f"b{2 + t}", f"dw_ps{t}")
+            dw_ps = bank(2 + t, f"dw_ps{t}")
             gradient_pass(dw_ps[:], t, PAD)
             dw = keep.tile([P, SLOTS], F32, name=f"dw{t}")
             step = keep.tile([P, SLOTS], F32, name=f"step{t}")
-            first = HSLOTS if t < 2 else 0
+            first = HSLOTS if t < len(early) else 0
             nc.scalar.copy(dw[:, first:], dw_ps[:, first:])
             nc.scalar.activation(step[:, first:], dw_ps[:, first:], COPY, scale=neg_fd2[:, t : t + 1])
             nc.vector.tensor_copy(grad_win[t % 2][:].indirect(offs_of(first, SLOTS)), dw[:, first:])

@@ -29,6 +29,7 @@ QSLOTS = SLOTS // QUARTERS
 HSLOTS = SLOTS // 2
 OFFS_PER_COL = 16
 RUN = 2
+GRAD_WIN = (0, 1, 2, 1)
 PAD = SLOTS - HSLOTS
 
 
@@ -73,21 +74,22 @@ def tile_attend_gahead_nag_sq_kernel(tc, wT, mT, xT, y, ts, us, wt, fd, offs, ou
         nc.sync.dma_start(offsets[:], offs)
         nc.scalar.dma_start(us_c[:], by_plane(us)[:, :, 0])
         nc.scalar.dma_start(wt_c[:], by_plane(wt)[:, :, 0])
+        for j in range(2):
+            nc.sync.dma_start(m_pair[j][:], by_plane(mT)[:, 2 * j : 2 * j + 2, :])
         for t in range(PACK):
-            if t % 2 == 0:
-                nc.sync.dma_start(m_pair[t // 2][:], by_plane(mT)[:, t : t + 2, :])
             nc.sync.dma_start(w_win[t][:], by_plane(wT)[:, t, :])
         for h in range(2):
             nc.sync.dma_start(y_raw[h][:], by_plane(y)[:, :, h * HSLOTS : (h + 1) * HSLOTS])
         nc.sync.dma_start(fd_c[:], by_plane(fd)[:, :, 0])
 
-        grad_win = [keep.tile([P, TABLE], F32, name=f"grad_win{k}") for k in range(2)]
+        grad_win = [keep.tile([P, TABLE], F32, name=f"grad_win{k}") for k in range(3)]
         mom_win = [keep.tile([P, TABLE], F32, name=f"mom_win{k}") for k in range(2)]
         ident = keep.tile([P, P], F32, name="ident")
         make_identity(nc, ident[:])
         for k in range(2):
             nc.vector.memset(grad_win[k][:], 0.0)
             nc.vector.memset(mom_win[k][:], 0.0)
+        nc.gpsimd.memset(grad_win[2][:], 0.0)
 
         for b in range(4):
             spread = bank(b, f"ts_spread{b}")
@@ -323,7 +325,7 @@ def tile_attend_gahead_nag_sq_kernel(tc, wT, mT, xT, y, ts, us, wt, fd, offs, ou
             first = HSLOTS if t < len(early) else 0
             nc.scalar.copy(dw[:, first:], dw_ps[:, first:])
             nc.scalar.activation(step[:, first:], dw_ps[:, first:], COPY, scale=neg_fd2[:, t : t + 1])
-            nc.vector.tensor_copy(grad_win[t % 2][:].indirect(offs_of(first, SLOTS)), dw[:, first:])
-            nc.sync.dma_start(by_plane(out_1)[:, t, :], grad_win[t % 2][:])
+            nc.vector.tensor_copy(grad_win[GRAD_WIN[t]][:].indirect(offs_of(first, SLOTS)), dw[:, first:])
+            nc.sync.dma_start(by_plane(out_1)[:, t, :], grad_win[GRAD_WIN[t]][:])
             nc.vector.tensor_tensor(mom_win[t % 2][:].indirect(offs_of(first, SLOTS)), m_g[t][:, first:], step[:, first:], ADD)
             nc.sync.dma_start(by_plane(out_0)[:, t, :], mom_win[t % 2][:])

@@ -30,7 +30,8 @@ HSLOTS = SLOTS // 2
 OFFS_PER_COL = 16
 RUN = 2
 GRAD_WIN = (0, 1, 2, 1)
-PAD = SLOTS - HSLOTS
+TURNED = QUARTERS - 1
+PAD = SLOTS - QSLOTS
 
 
 def tile_attend_gahead_nag_sq_kernel(tc, wT, mT, xT, y, ts, us, wt, fd, offs, out_0, out_1):
@@ -61,7 +62,7 @@ def tile_attend_gahead_nag_sq_kernel(tc, wT, mT, xT, y, ts, us, wt, fd, offs, ou
 
         m_pair = [keep.tile([P, 2, TABLE], F32, name=f"m_pair{j}") for j in range(2)]
         w_win = [keep.tile([P, TABLE], F32, name=f"w_win{t}") for t in range(PACK)]
-        x_raw = keep.tile([P, PACK, R], F32, name="x_raw")
+        x_raw = keep.tile([P, PACK, R], F32, name="x_raw", tag="x_raw")
         y_raw = [keep.tile([P, PACK, HSLOTS], F32, name=f"y_raw{h}") for h in range(2)]
         ts_win = keep.tile([P, TABLE], F32, name="ts_win")
         us_c = keep.tile([P, PACK], F32, name="us_c")
@@ -83,13 +84,16 @@ def tile_attend_gahead_nag_sq_kernel(tc, wT, mT, xT, y, ts, us, wt, fd, offs, ou
         nc.sync.dma_start(fd_c[:], by_plane(fd)[:, :, 0])
 
         grad_win = [keep.tile([P, TABLE], F32, name=f"grad_win{k}") for k in range(3)]
-        mom_win = [keep.tile([P, TABLE], F32, name=f"mom_win{k}") for k in range(2)]
+        mom_win = [keep.tile([P, TABLE], F32, name=f"mom_win{k}") for k in range(3)]
         ident = keep.tile([P, P], F32, name="ident")
         make_identity(nc, ident[:])
         for k in range(2):
             nc.vector.memset(grad_win[k][:], 0.0)
             nc.vector.memset(mom_win[k][:], 0.0)
         nc.gpsimd.memset(grad_win[2][:], 0.0)
+        nc.gpsimd.memset(mom_win[2][:], 0.0)
+        zeros = keep.tile([P, QSLOTS], F32, name="zeros")
+        nc.gpsimd.memset(zeros[:], 0.0)
 
         for b in range(4):
             spread = bank(b, f"ts_spread{b}")
@@ -108,14 +112,15 @@ def tile_attend_gahead_nag_sq_kernel(tc, wT, mT, xT, y, ts, us, wt, fd, offs, ou
         neg_fd2 = keep.tile([P, PACK], F32, name="neg_fd2")
 
         m_g = [keep.tile([P, SLOTS], F32, name=f"m_g{t}") for t in range(PACK)]
-        pieces = [(0, QSLOTS), (QSLOTS, HSLOTS), (HSLOTS, SLOTS)]
-        w2 = [keep.tile([P, PACK, hi - lo], F32, name=f"w2_{lo}") for lo, hi in pieces]
+        w2 = keep.tile([P, PACK, SLOTS], F32, name="w2")
 
         def gather_plane(t):
             nc.vector.tensor_copy(m_g[t][:], m_pair[t // 2][:, t % 2, :].indirect(offsets[:]))
-            for piece, (lo, hi) in zip(w2, pieces):
-                end = lo + QSLOTS if t == LAST else hi
-                nc.vector.tensor_tensor(piece[:, t, 0 : end - lo], w_win[t][:].indirect(offs_of(lo, end)), m_g[t][:, lo:end], ADD)
+            width = QSLOTS if t == LAST else SLOTS
+            for lo in range(0, SLOTS, width):
+                nc.vector.tensor_tensor(
+                    w2[:, t, lo : lo + width], w_win[t][:].indirect(offs_of(lo, lo + width)), m_g[t][:, lo : lo + width], ADD
+                )
 
         nc.vector.tensor_tensor(y_row[:], wt_c[:], us_c[:], MULT)
         nc.vector.tensor_tensor(a_row[:], y_row[:], us_c[:], MULT)
@@ -151,28 +156,28 @@ def tile_attend_gahead_nag_sq_kernel(tc, wT, mT, xT, y, ts, us, wt, fd, offs, ou
         )
 
         ts_turned = bank(6, "ts_turned")
-        for k in range(2):
-            nc.tensor.transpose(ts_turned[:, q_cols(k)], ts_g[:, q_cols(2 + k)], ident[:])
-        ts_col = keep.tile([P, 2], F32, name="ts_col")
-        ts2_col = keep.tile([P, 2], F32, name="ts2_col")
-        nonzero_col = keep.tile([P, 2], F32, name="nonzero_col")
-        inv_col = keep.tile([P, 2], F32, name="inv_col")
-        nc.scalar.activation(ts_col[:], ts_turned[:, 0:HSLOTS:QSLOTS], COPY)
+        for k in range(TURNED):
+            nc.tensor.transpose(ts_turned[:, q_cols(k)], ts_g[:, q_cols(1 + k)], ident[:])
+        ts_col = keep.tile([P, TURNED], F32, name="ts_col")
+        ts2_col = keep.tile([P, TURNED], F32, name="ts2_col")
+        nonzero_col = keep.tile([P, TURNED], F32, name="nonzero_col")
+        inv_col = keep.tile([P, TURNED], F32, name="inv_col")
+        nc.scalar.activation(ts_col[:], ts_turned[:, 0 : TURNED * QSLOTS : QSLOTS], COPY)
         nc.scalar.activation(ts2_col[:], ts_col[:], SQUARE)
         nc.vector.scalar_tensor_tensor(nonzero_col[:], ts_col[:], 0.0, ts_col[:], IS_EQUAL, ADD)
         nc.vector.reciprocal(inv_col[:], nonzero_col[:])
         inv_spread = bank(7, "inv_spread")
-        for k in range(2):
+        for k in range(TURNED):
             nc.tensor.transpose(inv_spread[:, q_cols(k)], inv_col[:, k : k + 1].to_broadcast([P, P]), ident[:])
 
-        ts_sq = keep.tile([P, HSLOTS], F32, name="ts_sq")
-        a_fac = keep.tile([P, PACK, HSLOTS], F32, name="a_fac")
-        y_fac = [keep.tile([P, PACK, HSLOTS], F32, name=f"y_fac{h}") for h in range(2)]
-        nc.scalar.activation(ts_sq[:], ts_g[:, 0:HSLOTS], SQUARE)
+        ts_sq = keep.tile([P, QSLOTS], F32, name="ts_sq")
+        a_fac = keep.tile([P, PACK, QSLOTS], F32, name="a_fac")
+        y_fac = keep.tile([P, PACK, SLOTS], F32, name="y_fac")
+        nc.scalar.activation(ts_sq[:], ts_g[:, 0:QSLOTS], SQUARE)
         for s in range(PACK):
-            nc.scalar.activation(y_fac[0][:, s, :], ts_g[:, 0:HSLOTS], COPY, scale=y_row[:, s : s + 1])
+            nc.scalar.activation(y_fac[:, s, 0:QSLOTS], ts_g[:, 0:QSLOTS], COPY, scale=y_row[:, s : s + 1])
             nc.scalar.activation(a_fac[:, s, :], ts_sq[:], COPY, scale=a_row[:, s : s + 1])
-            nc.scalar.activation(y_fac[1][:, s, :], inv_spread[:, 0:HSLOTS], COPY, scale=neg_y_row[:, s : s + 1])
+            nc.scalar.activation(y_fac[:, s, QSLOTS:SLOTS], inv_spread[:, 0 : TURNED * QSLOTS], COPY, scale=neg_y_row[:, s : s + 1])
 
         gather_plane(1)
 
@@ -197,11 +202,9 @@ def tile_attend_gahead_nag_sq_kernel(tc, wT, mT, xT, y, ts, us, wt, fd, offs, ou
         w2_il = [keep.tile([P, QSLOTS, PACK], BF16, name=f"w2_il{q}", align_bytes=64) for q in range(QUARTERS)]
         w2_codes = [keep.tile([P, QSLOTS], U32, name=f"w2_codes{q}", align_bytes=64) for q in range(QUARTERS)]
         w2_scales = [keep.tile([P, QSLOTS], U8, name=f"w2_scales{q}", align_bytes=64) for q in range(QUARTERS)]
-        nc.scalar.copy(woven(w2_il[3][:, :, 0:LAST]), planar(w2[2][:, 0:LAST, QSLOTS:HSLOTS]))
-        for q in range(3):
-            nc.scalar.copy(woven(w2_il[q][:]), planar(w2[q][:, :, 0:QSLOTS]))
+        for q in range(QUARTERS):
+            nc.scalar.copy(woven(w2_il[q][:]), planar(w2[:, :, q_cols(q)]))
 
-        a_term = [keep.tile([P, PACK, QSLOTS], F32, name=f"a_term{q}") for q in range(2)]
         g_il = [keep.tile([P, QSLOTS, PACK], BF16, name=f"g_il{q}", tag=f"g_il{q}", align_bytes=64) for q in range(QUARTERS)]
         scores = [bank(q, f"scores{q}") for q in range(QUARTERS)]
 
@@ -219,39 +222,49 @@ def tile_attend_gahead_nag_sq_kernel(tc, wT, mT, xT, y, ts, us, wt, fd, offs, ou
                     stop=True,
                 )
 
-        def quantise_g(q):
-            cols = slice(PAD + q * QSLOTS, PAD + (q + 1) * QSLOTS)
-            nc.vector.quantize_mx(g_codes[:, cols].bitcast(E5M2), g_scales[:, cols], g_il[q][:].rearrange("p n s -> p (n s)"))
+        def g_cols(q):
+            return slice(PAD + q * QSLOTS, PAD + (q + 1) * QSLOTS)
 
-        def gradient_pass(out, t, first_col):
-            feats = slice(t * P, (t + 1) * P)
+        def quantise_g(q):
+            nc.vector.quantize_mx(g_codes[:, g_cols(q)].bitcast(E5M2), g_scales[:, g_cols(q)], g_il[q][:].rearrange("p n s -> p (n s)"))
+
+        def plane0_pass(out, first_col):
             cols = slice(first_col, first_col + SLOTS)
             nc.tensor.matmul_mx(
                 out,
-                lhsT=xr_codes[:, feats].bitcast(E4M3),
-                lhsT_scale=xr_scales[:, feats],
+                lhsT=xr_codes[:, 0:P].bitcast(E4M3),
+                lhsT_scale=xr_scales[:, 0:P],
                 rhs=g_codes[:, cols].bitcast(E5M2),
                 rhs_scale=g_scales[:, cols],
                 start=True,
                 stop=True,
             )
 
-        y_term = [keep.tile([P, PACK, QSLOTS], F32, name=f"y_term{q}") for q in range(2)]
-        for q in range(2):
-            score_quarter(q)
-            nc.vector.tensor_tensor(y_term[q][:], y_raw[0][:, :, q_cols(q)], y_fac[0][:, :, q_cols(q)], MULT)
-        a_scaled = [keep.tile([P, PACK, QSLOTS], F32, name=f"a_scaled{k}") for k in range(2)]
-        summed = [bank(4 + k, f"summed{k}") for k in range(2)]
+        def quarter_pass(out, q):
+            nc.tensor.matmul_mx(
+                out,
+                lhsT=g_codes[:, g_cols(q)].bitcast(E5M2),
+                lhsT_scale=g_scales[:, g_cols(q)],
+                rhs=xr_codes[:].bitcast(E4M3),
+                rhs_scale=xr_scales[:],
+                start=True,
+                stop=True,
+            )
 
-        def score_and_scale(k):
-            score_quarter(2 + k)
+        def y_of(q):
+            return y_raw[q // 2][:, :, q_cols(q % 2)]
+
+        a_scaled = {q: keep.tile([P, PACK, QSLOTS], F32, name=f"a_scaled{q}") for q in range(1, QUARTERS)}
+        summed = {q: bank(3 + q, f"summed{q}") for q in range(1, QUARTERS)}
+
+        def scale_scores(q):
             for s in range(PACK):
-                nc.scalar.activation(a_scaled[k][:, s, :], scores[2 + k][:, q_cols(s)], COPY, scale=a_row[:, s : s + 1])
+                nc.scalar.activation(a_scaled[q][:, s, :], scores[q][:, q_cols(s)], COPY, scale=a_row[:, s : s + 1])
 
-        def turn_into_sum(k, term, opens):
+        def turn_into_sum(q, term, opens):
             for s in range(PACK):
                 nc.tensor.matmul(
-                    summed[k][:, q_cols(s)],
+                    summed[q][:, q_cols(s)],
                     term[:, s, :],
                     ident[:],
                     start=(opens and s == 0),
@@ -259,73 +272,110 @@ def tile_attend_gahead_nag_sq_kernel(tc, wT, mT, xT, y, ts, us, wt, fd, offs, ou
                     is_transpose=True,
                 )
 
-        score_and_scale(0)
-        turn_into_sum(0, a_scaled[0][:], opens=True)
-
-        for q in range(2):
-            nc.vector.tensor_tensor(
-                a_term[q][:], scores[q][:].rearrange("p (s n) -> p s n", s=PACK), a_fac[:, :, q_cols(q)], MULT
-            )
-        for q in range(2):
-            nc.vector.tensor_tensor(woven(g_il[q][:]), planar(a_term[q][:]), planar(y_term[q][:]), SUB)
-        for q in range(2):
-            quantise_g(q)
-
-        early = [bank(6 + t, f"early{t}") for t in range(2)]
-        dw_early = [keep.tile([P, HSLOTS], F32, name=f"dw_early{t}") for t in range(2)]
-        for t in range(2):
-            gradient_pass(early[t][:], t, 0)
-            nc.scalar.copy(dw_early[t][:], early[t][:, PAD:SLOTS])
-        step_early0 = keep.tile([P, HSLOTS], F32, name="step_early0")
-        nc.scalar.activation(step_early0[:], early[0][:, PAD:SLOTS], COPY, scale=neg_fd2[:, 0:1])
-
-        w2_last = keep.tile([P, QSLOTS], F32, name="w2_last", tag="g_il0", align_bytes=64)
-        nc.vector.tensor_tensor(w2_last[:], w_win[LAST][:].indirect(offs_of(SLOTS - QSLOTS, SLOTS)), m_g[LAST][:, q_cols(3)], ADD)
-        nc.scalar.copy(w2_il[3][:, :, LAST], w2_last[:])
-        y_scaled = keep.tile([P, PACK, HSLOTS], F32, name="y_scaled", tag="g_il1", align_bytes=64)
-        nc.vector.tensor_tensor(y_scaled[:], y_raw[1][:], y_fac[1][:], MULT)
-        score_and_scale(1)
-
-        def round_and_turn_back(k):
-            g_turned = keep.tile([P, 2, P, 2], BF16, name=f"g_turned{k}")
+        def round_and_turn_back(q, g_words):
+            g_turned = keep.tile([P, 2, P, 2], BF16, name=f"g_turned{q}")
             nc.scalar.activation(
-                g_turned[:], summed[k][:].rearrange("i (u e p) -> i u p e", u=2, e=2), COPY, scale=ts2_col[:, k : k + 1]
+                g_turned[:], summed[q][:].rearrange("i (u e p) -> i u p e", u=2, e=2), COPY, scale=ts2_col[:, q - 1 : q]
             )
             words = g_turned[:].rearrange("i u p e -> i (u p e)").bitcast(F32)
             for u in range(2):
-                nc.tensor.transpose(g_words[:, q_cols(2 * k + u)], words[:, q_cols(u)], ident[:])
+                nc.tensor.transpose(g_words[:, q_cols(u)], words[:, q_cols(u)], ident[:])
 
-        g_words = bank(0, "g_words")
-        turn_into_sum(0, y_scaled[:, :, q_cols(0)], opens=False)
-        round_and_turn_back(0)
-        turn_into_sum(1, y_scaled[:, :, q_cols(1)], opens=True)
-        turn_into_sum(1, a_scaled[1][:], opens=False)
-        round_and_turn_back(1)
-        for k in range(2):
+        def weave_words(q, g_words):
             nc.scalar.copy(
-                g_il[2 + k][:].rearrange("p n s -> p (n s)").bitcast(F32).rearrange("p (n u) -> p n u", u=2),
-                g_words[:, k * HSLOTS : (k + 1) * HSLOTS].rearrange("p (u n) -> p n u", u=2),
+                g_il[q][:].rearrange("p n s -> p (n s)").bitcast(F32).rearrange("p (n u) -> p n u", u=2),
+                g_words[:, 0:HSLOTS].rearrange("p (u n) -> p n u", u=2),
             )
 
-        direct = offs_of(0, HSLOTS)
-        for t in range(2):
-            nc.vector.tensor_copy(grad_win[t][:].indirect(direct), dw_early[t][:])
-        nc.vector.tensor_tensor(mom_win[0][:].indirect(direct), m_g[0][:, 0:HSLOTS], step_early0[:], ADD)
-        quantise_g(2)
-        step_early1 = keep.tile([P, HSLOTS], F32, name="step_early1", tag="g_il2", align_bytes=64)
-        nc.scalar.activation(step_early1[:], early[1][:, PAD:SLOTS], COPY, scale=neg_fd2[:, 1:2])
-        quantise_g(3)
-        nc.vector.tensor_tensor(mom_win[1][:].indirect(direct), m_g[1][:, 0:HSLOTS], step_early1[:], ADD)
+        dw = [keep.tile([P, SLOTS], F32, name=f"dw{t}") for t in range(PACK)]
+        step = [keep.tile([P, SLOTS], F32, name=f"step{t}") for t in range(PACK)]
+        dw_by_slot = keep.tile([P, QUARTERS, D], F32, name="dw_by_slot", tag="x_raw")
+        dw_turned = [dw_by_slot[:, q, :] for q in range(QUARTERS)]
 
-        for t in range(PACK):
-            dw_ps = bank(2 + t, f"dw_ps{t}")
-            gradient_pass(dw_ps[:], t, PAD)
-            dw = keep.tile([P, SLOTS], F32, name=f"dw{t}")
-            step = keep.tile([P, SLOTS], F32, name=f"step{t}")
-            first = HSLOTS if t < len(early) else 0
-            nc.scalar.copy(dw[:, first:], dw_ps[:, first:])
-            nc.scalar.activation(step[:, first:], dw_ps[:, first:], COPY, scale=neg_fd2[:, t : t + 1])
-            nc.vector.tensor_copy(grad_win[GRAD_WIN[t]][:].indirect(offs_of(first, SLOTS)), dw[:, first:])
-            nc.sync.dma_start(by_plane(out_1)[:, t, :], grad_win[GRAD_WIN[t]][:])
-            nc.vector.tensor_tensor(mom_win[t % 2][:].indirect(offs_of(first, SLOTS)), m_g[t][:, first:], step[:, first:], ADD)
-            nc.sync.dma_start(by_plane(out_0)[:, t, :], mom_win[t % 2][:])
+        def fetch(t, lo, hi, source):
+            nc.scalar.copy(dw[t][:, lo:hi], source)
+            nc.scalar.activation(step[t][:, lo:hi], source, COPY, scale=neg_fd2[:, t : t + 1])
+
+        def scatter(t, lo, hi):
+            window = grad_win[GRAD_WIN[t]]
+            if hi - lo == QSLOTS:
+                nc.vector.tensor_tensor(window[:].indirect(offs_of(lo, hi)), dw[t][:, lo:hi], zeros[:], ADD)
+            else:
+                nc.vector.tensor_copy(window[:].indirect(offs_of(lo, hi)), dw[t][:, lo:hi])
+            if hi == SLOTS:
+                nc.sync.dma_start(by_plane(out_1)[:, t, :], window[:])
+            window = mom_win[GRAD_WIN[t]]
+            nc.vector.tensor_tensor(window[:].indirect(offs_of(lo, hi)), m_g[t][:, lo:hi], step[t][:, lo:hi], ADD)
+            if hi == SLOTS:
+                nc.sync.dma_start(by_plane(out_0)[:, t, :], window[:])
+
+        def turn_back(out, q, t):
+            nc.tensor.transpose(out, dw_turned[q][:, q_cols(t)], ident[:])
+
+        y_term = keep.tile([P, PACK, QSLOTS], F32, name="y_term")
+        a_term = keep.tile([P, PACK, QSLOTS], F32, name="a_term")
+        score_quarter(0)
+        score_quarter(1)
+        nc.vector.tensor_tensor(y_term[:], y_of(0), y_fac[:, :, q_cols(0)], MULT)
+        score_quarter(2)
+        nc.vector.tensor_tensor(a_term[:], scores[0][:].rearrange("p (s n) -> p s n", s=PACK), a_fac[:], MULT)
+        score_quarter(3)
+        nc.vector.tensor_tensor(woven(g_il[0][:]), planar(a_term[:]), planar(y_term[:]), SUB)
+        quantise_g(0)
+        y_scaled = keep.tile([P, TURNED, PACK, QSLOTS], F32, name="y_scaled", tag="g_il0", align_bytes=64)
+        for q in range(1, QUARTERS):
+            nc.vector.tensor_tensor(y_scaled[:, q - 1], y_of(q), y_fac[:, :, q_cols(q)], MULT)
+        early = bank(7, "early")
+        plane0_pass(early[:], 0)
+        fetch(0, 0, QSLOTS, early[:, PAD:SLOTS])
+        by_slot0 = bank(0, "by_slot0")
+        quarter_pass(by_slot0[:], 0)
+        nc.scalar.copy(dw_turned[0][:, P : 3 * P], by_slot0[:, P : 3 * P])
+        scatter(0, 0, QSLOTS)
+
+        scale_scores(1)
+        turn_into_sum(1, a_scaled[1][:], opens=True)
+        turn_into_sum(1, y_scaled[:, 0], opens=False)
+        mixed1 = bank(1, "mixed1")
+        round_and_turn_back(1, mixed1)
+        for t in (1, 2):
+            turn_back(mixed1[:, q_cols(1 + t)], 0, t)
+        weave_words(1, mixed1)
+        quantise_g(1)
+        for t in (1, 2):
+            fetch(t, 0, QSLOTS, mixed1[:, q_cols(1 + t)])
+            scatter(t, 0, QSLOTS)
+        by_slot1 = bank(7, "by_slot1")
+        quarter_pass(by_slot1[:], 1)
+        nc.scalar.copy(dw_turned[1][:, 0 : 2 * P], by_slot1[:, 0 : 2 * P])
+
+        mixed = {}
+        for q in (2, 3):
+            scale_scores(q)
+            turn_into_sum(q, a_scaled[q][:], opens=True)
+            turn_into_sum(q, y_scaled[:, q - 1], opens=False)
+            mixed[q] = bank(q, f"mixed{q}")
+            round_and_turn_back(q, mixed[q])
+            turn_back(mixed[q][:, q_cols(2)], 1, q - 2)
+            weave_words(q, mixed[q])
+            quantise_g(q)
+            fetch(q - 2, QSLOTS, HSLOTS, mixed[q][:, q_cols(2)])
+            scatter(q - 2, QSLOTS, HSLOTS)
+
+        whole0 = bank(4, "whole0")
+        plane0_pass(whole0[:], PAD)
+        fetch(0, HSLOTS, SLOTS, whole0[:, HSLOTS:SLOTS])
+        scatter(0, HSLOTS, SLOTS)
+        for q, number in ((3, 5), (2, 3)):
+            by_slot = bank(number, f"by_slot{q}")
+            quarter_pass(by_slot[:], q)
+            nc.scalar.copy(dw_turned[q][:, P:D], by_slot[:, P:D])
+        nc.scalar.copy(dw_turned[0][:, 3 * P : D], by_slot0[:, 3 * P : D])
+        nc.scalar.copy(dw_turned[1][:, 2 * P : D], by_slot1[:, 2 * P : D])
+        for t, number in ((1, 6), (2, 4), (3, 5)):
+            back = bank(number, f"back{t}")
+            first = LAST - t
+            for q in range(first, QUARTERS):
+                turn_back(back[:, q_cols(q)], q, t)
+            fetch(t, first * QSLOTS, SLOTS, back[:, first * QSLOTS : SLOTS])
+            scatter(t, first * QSLOTS, SLOTS)

@@ -29,7 +29,7 @@ QSLOTS = SLOTS // QUARTERS
 HSLOTS = SLOTS // 2
 OFFS_PER_COL = 16
 RUN = 2
-GRAD_WIN = (0, 1, 2, 1)
+MOM_WIN = (0, 1, 2, 1)
 TURNED = QUARTERS - 1
 PAD = SLOTS - QSLOTS
 
@@ -64,7 +64,7 @@ def tile_attend_gahead_nag_sq_kernel(tc, wT, mT, xT, y, ts, us, wt, fd, offs, ou
         w_win = [keep.tile([P, TABLE], F32, name=f"w_win{t}") for t in range(PACK)]
         x_raw = keep.tile([P, PACK, R], F32, name="x_raw", tag="x_raw")
         y_raw = [keep.tile([P, PACK, HSLOTS], F32, name=f"y_raw{h}") for h in range(2)]
-        ts_win = keep.tile([P, TABLE], F32, name="ts_win")
+        ts_win = keep.tile([P, TABLE], F32, name="ts_win", tag="ts_win")
         us_c = keep.tile([P, PACK], F32, name="us_c")
         wt_c = keep.tile([P, PACK], F32, name="wt_c")
         fd_c = keep.tile([P, PACK], F32, name="fd_c")
@@ -127,6 +127,8 @@ def tile_attend_gahead_nag_sq_kernel(tc, wT, mT, xT, y, ts, us, wt, fd, offs, ou
         nc.vector.tensor_scalar(neg_y_row[:], y_row[:], -1.0, 0.0, MULT, ADD)
         ts_g = keep.tile([P, SLOTS], F32, name="ts_g")
         nc.vector.tensor_copy(ts_g[:], ts_win[:].indirect(offsets[:]))
+        grad_win.append(keep.tile([P, TABLE], F32, name="grad_win3", tag="ts_win"))
+        nc.gpsimd.memset(grad_win[3][:], 0.0)
         gather_plane(0)
 
         x_bf = keep.tile([P, PACK, R], BF16, name="x_bf", align_bytes=64)
@@ -296,18 +298,23 @@ def tile_attend_gahead_nag_sq_kernel(tc, wT, mT, xT, y, ts, us, wt, fd, offs, ou
             nc.scalar.copy(dw[t][:, lo:hi], source)
             nc.scalar.activation(step[t][:, lo:hi], source, COPY, scale=neg_fd2[:, t : t + 1])
 
-        def scatter(t, lo, hi):
-            window = grad_win[GRAD_WIN[t]]
+        def scatter_grad(t, lo, hi):
             if hi - lo == QSLOTS:
-                nc.vector.tensor_tensor(window[:].indirect(offs_of(lo, hi)), dw[t][:, lo:hi], zeros[:], ADD)
+                nc.vector.tensor_tensor(grad_win[t][:].indirect(offs_of(lo, hi)), dw[t][:, lo:hi], zeros[:], ADD)
             else:
-                nc.vector.tensor_copy(window[:].indirect(offs_of(lo, hi)), dw[t][:, lo:hi])
+                nc.vector.tensor_copy(grad_win[t][:].indirect(offs_of(lo, hi)), dw[t][:, lo:hi])
             if hi == SLOTS:
-                nc.sync.dma_start(by_plane(out_1)[:, t, :], window[:])
-            window = mom_win[GRAD_WIN[t]]
+                nc.sync.dma_start(by_plane(out_1)[:, t, :], grad_win[t][:])
+
+        def scatter_mom(t, lo, hi):
+            window = mom_win[MOM_WIN[t]]
             nc.vector.tensor_tensor(window[:].indirect(offs_of(lo, hi)), m_g[t][:, lo:hi], step[t][:, lo:hi], ADD)
             if hi == SLOTS:
                 nc.sync.dma_start(by_plane(out_0)[:, t, :], window[:])
+
+        def scatter(t, lo, hi):
+            scatter_grad(t, lo, hi)
+            scatter_mom(t, lo, hi)
 
         def turn_back(out, q, t):
             nc.tensor.transpose(out, dw_turned[q][:, q_cols(t)], ident[:])
@@ -330,21 +337,26 @@ def tile_attend_gahead_nag_sq_kernel(tc, wT, mT, xT, y, ts, us, wt, fd, offs, ou
         fetch(0, 0, QSLOTS, early[:, PAD:SLOTS])
         by_slot0 = bank(0, "by_slot0")
         quarter_pass(by_slot0[:], 0)
-        nc.scalar.copy(dw_turned[0][:, P : 3 * P], by_slot0[:, P : 3 * P])
+        nc.scalar.copy(dw_turned[0][:, P:D], by_slot0[:, P:D])
         scatter(0, 0, QSLOTS)
+        back01 = bank(7, "back01")
+        turn_back(back01[:, q_cols(0)], 0, 1)
+        fetch(1, 0, QSLOTS, back01[:, q_cols(0)])
+        scatter(1, 0, QSLOTS)
 
         scale_scores(1)
         turn_into_sum(1, a_scaled[1][:], opens=True)
         turn_into_sum(1, y_scaled[:, 0], opens=False)
         mixed1 = bank(1, "mixed1")
         round_and_turn_back(1, mixed1)
-        for t in (1, 2):
-            turn_back(mixed1[:, q_cols(1 + t)], 0, t)
+        for t in (2, 3):
+            turn_back(mixed1[:, q_cols(t)], 0, t)
         weave_words(1, mixed1)
         quantise_g(1)
-        for t in (1, 2):
-            fetch(t, 0, QSLOTS, mixed1[:, q_cols(1 + t)])
-            scatter(t, 0, QSLOTS)
+        for t in (2, 3):
+            fetch(t, 0, QSLOTS, mixed1[:, q_cols(t)])
+        scatter(2, 0, QSLOTS)
+        scatter_grad(3, 0, QSLOTS)
         by_slot1 = bank(7, "by_slot1")
         quarter_pass(by_slot1[:], 1)
         nc.scalar.copy(dw_turned[1][:, 0 : 2 * P], by_slot1[:, 0 : 2 * P])
@@ -360,22 +372,24 @@ def tile_attend_gahead_nag_sq_kernel(tc, wT, mT, xT, y, ts, us, wt, fd, offs, ou
             weave_words(q, mixed[q])
             quantise_g(q)
             fetch(q - 2, QSLOTS, HSLOTS, mixed[q][:, q_cols(2)])
-            scatter(q - 2, QSLOTS, HSLOTS)
+            scatter_grad(q - 2, QSLOTS, HSLOTS)
+        scatter_mom(1, QSLOTS, HSLOTS)
 
         whole0 = bank(4, "whole0")
         plane0_pass(whole0[:], PAD)
         fetch(0, HSLOTS, SLOTS, whole0[:, HSLOTS:SLOTS])
-        scatter(0, HSLOTS, SLOTS)
+        scatter_grad(0, HSLOTS, SLOTS)
+        scatter_mom(0, QSLOTS, SLOTS)
         for q, number in ((3, 5), (2, 3)):
             by_slot = bank(number, f"by_slot{q}")
             quarter_pass(by_slot[:], q)
             nc.scalar.copy(dw_turned[q][:, P:D], by_slot[:, P:D])
-        nc.scalar.copy(dw_turned[0][:, 3 * P : D], by_slot0[:, 3 * P : D])
         nc.scalar.copy(dw_turned[1][:, 2 * P : D], by_slot1[:, 2 * P : D])
         for t, number in ((1, 6), (2, 4), (3, 5)):
             back = bank(number, f"back{t}")
-            first = LAST - t
+            first = 2 if t == 1 else 1
             for q in range(first, QUARTERS):
                 turn_back(back[:, q_cols(q)], q, t)
             fetch(t, first * QSLOTS, SLOTS, back[:, first * QSLOTS : SLOTS])
-            scatter(t, first * QSLOTS, SLOTS)
+            scatter_grad(t, first * QSLOTS, SLOTS)
+            scatter_mom(t, 0 if t == LAST else first * QSLOTS, SLOTS)

@@ -16,7 +16,6 @@ E5M2 = mybir.dt.float8_e5m2_x4
 MULT = mybir.AluOpType.mult
 ADD = mybir.AluOpType.add
 SUB = mybir.AluOpType.subtract
-IS_EQUAL = mybir.AluOpType.is_equal
 COPY = mybir.ActivationFunctionType.Copy
 SQUARE = mybir.ActivationFunctionType.Square
 
@@ -29,9 +28,6 @@ QSLOTS = SLOTS // QUARTERS
 HSLOTS = SLOTS // 2
 OFFS_PER_COL = 16
 RUN = 2
-MOM_WIN = (0, 1, 2, 1)
-TURNED = QUARTERS - 1
-PAD = SLOTS - QSLOTS
 
 
 def tile_attend_gahead_nag_sq_kernel(tc, wT, mT, xT, y, ts, us, wt, fd, offs, out_0, out_1):
@@ -62,9 +58,9 @@ def tile_attend_gahead_nag_sq_kernel(tc, wT, mT, xT, y, ts, us, wt, fd, offs, ou
 
         m_pair = [keep.tile([P, 2, TABLE], F32, name=f"m_pair{j}") for j in range(2)]
         w_win = [keep.tile([P, TABLE], F32, name=f"w_win{t}") for t in range(PACK)]
-        x_raw = keep.tile([P, PACK, R], F32, name="x_raw", tag="x_raw")
+        x_raw = keep.tile([P, PACK, R], F32, name="x_raw")
         y_raw = [keep.tile([P, PACK, HSLOTS], F32, name=f"y_raw{h}") for h in range(2)]
-        ts_win = keep.tile([P, TABLE], F32, name="ts_win", tag="ts_win")
+        ts_win = keep.tile([P, TABLE], F32, name="ts_win")
         us_c = keep.tile([P, PACK], F32, name="us_c")
         wt_c = keep.tile([P, PACK], F32, name="wt_c")
         fd_c = keep.tile([P, PACK], F32, name="fd_c")
@@ -92,8 +88,6 @@ def tile_attend_gahead_nag_sq_kernel(tc, wT, mT, xT, y, ts, us, wt, fd, offs, ou
             nc.vector.memset(mom_win[k][:], 0.0)
         nc.gpsimd.memset(grad_win[2][:], 0.0)
         nc.gpsimd.memset(mom_win[2][:], 0.0)
-        zeros = keep.tile([P, QSLOTS], F32, name="zeros")
-        nc.gpsimd.memset(zeros[:], 0.0)
 
         for b in range(4):
             spread = bank(b, f"ts_spread{b}")
@@ -108,7 +102,6 @@ def tile_attend_gahead_nag_sq_kernel(tc, wT, mT, xT, y, ts, us, wt, fd, offs, ou
 
         y_row = keep.tile([P, PACK], F32, name="y_row")
         a_row = keep.tile([P, PACK], F32, name="a_row")
-        neg_y_row = keep.tile([P, PACK], F32, name="neg_y_row")
         neg_fd2 = keep.tile([P, PACK], F32, name="neg_fd2")
 
         m_g = [keep.tile([P, SLOTS], F32, name=f"m_g{t}") for t in range(PACK)]
@@ -124,11 +117,8 @@ def tile_attend_gahead_nag_sq_kernel(tc, wT, mT, xT, y, ts, us, wt, fd, offs, ou
 
         nc.vector.tensor_tensor(y_row[:], wt_c[:], us_c[:], MULT)
         nc.vector.tensor_tensor(a_row[:], y_row[:], us_c[:], MULT)
-        nc.vector.tensor_scalar(neg_y_row[:], y_row[:], -1.0, 0.0, MULT, ADD)
         ts_g = keep.tile([P, SLOTS], F32, name="ts_g")
         nc.vector.tensor_copy(ts_g[:], ts_win[:].indirect(offsets[:]))
-        grad_win.append(keep.tile([P, TABLE], F32, name="grad_win3", tag="ts_win"))
-        nc.gpsimd.memset(grad_win[3][:], 0.0)
         gather_plane(0)
 
         x_bf = keep.tile([P, PACK, R], BF16, name="x_bf", align_bytes=64)
@@ -157,29 +147,13 @@ def tile_attend_gahead_nag_sq_kernel(tc, wT, mT, xT, y, ts, us, wt, fd, offs, ou
             x_bf[:].rearrange("p t (r s) -> p s r t", s=PACK),
         )
 
-        ts_turned = bank(6, "ts_turned")
-        for k in range(TURNED):
-            nc.tensor.transpose(ts_turned[:, q_cols(k)], ts_g[:, q_cols(1 + k)], ident[:])
-        ts_col = keep.tile([P, TURNED], F32, name="ts_col")
-        ts2_col = keep.tile([P, TURNED], F32, name="ts2_col")
-        nonzero_col = keep.tile([P, TURNED], F32, name="nonzero_col")
-        inv_col = keep.tile([P, TURNED], F32, name="inv_col")
-        nc.scalar.activation(ts_col[:], ts_turned[:, 0 : TURNED * QSLOTS : QSLOTS], COPY)
-        nc.scalar.activation(ts2_col[:], ts_col[:], SQUARE)
-        nc.vector.scalar_tensor_tensor(nonzero_col[:], ts_col[:], 0.0, ts_col[:], IS_EQUAL, ADD)
-        nc.vector.reciprocal(inv_col[:], nonzero_col[:])
-        inv_spread = bank(7, "inv_spread")
-        for k in range(TURNED):
-            nc.tensor.transpose(inv_spread[:, q_cols(k)], inv_col[:, k : k + 1].to_broadcast([P, P]), ident[:])
-
-        ts_sq = keep.tile([P, QSLOTS], F32, name="ts_sq")
-        a_fac = keep.tile([P, PACK, QSLOTS], F32, name="a_fac")
+        ts_sq = keep.tile([P, SLOTS], F32, name="ts_sq")
+        a_fac = keep.tile([P, PACK, SLOTS], F32, name="a_fac")
         y_fac = keep.tile([P, PACK, SLOTS], F32, name="y_fac")
-        nc.scalar.activation(ts_sq[:], ts_g[:, 0:QSLOTS], SQUARE)
+        nc.scalar.activation(ts_sq[:], ts_g[:], SQUARE)
         for s in range(PACK):
-            nc.scalar.activation(y_fac[:, s, 0:QSLOTS], ts_g[:, 0:QSLOTS], COPY, scale=y_row[:, s : s + 1])
+            nc.scalar.activation(y_fac[:, s, :], ts_g[:], COPY, scale=y_row[:, s : s + 1])
             nc.scalar.activation(a_fac[:, s, :], ts_sq[:], COPY, scale=a_row[:, s : s + 1])
-            nc.scalar.activation(y_fac[:, s, QSLOTS:SLOTS], inv_spread[:, 0 : TURNED * QSLOTS], COPY, scale=neg_y_row[:, s : s + 1])
 
         gather_plane(1)
 
@@ -192,11 +166,6 @@ def tile_attend_gahead_nag_sq_kernel(tc, wT, mT, xT, y, ts, us, wt, fd, offs, ou
         nc.vector.quantize_mx(xd_codes[:].bitcast(E4M3), xd_scales[:], xd_il[:].rearrange("p r t -> p (r t)"))
         gather_plane(LAST)
 
-        g_codes = keep.tile([P, PAD + SLOTS], U32, name="g_codes", align_bytes=64)
-        g_scales = keep.tile([P, PAD + SLOTS], U8, name="g_scales", align_bytes=64)
-        nc.vector.memset(g_codes[:, 0:PAD], 0)
-        nc.vector.memset(g_scales[:, 0:PAD].bitcast(U32), 0)
-
         fd2 = keep.tile([P, PACK], F32, name="fd2")
         nc.gpsimd.tensor_tensor(fd2[:], fd_c[:], fd_c[:], MULT)
         nc.gpsimd.tensor_scalar(neg_fd2[:], fd2[:], -1.0, 0.0, MULT, ADD)
@@ -207,8 +176,12 @@ def tile_attend_gahead_nag_sq_kernel(tc, wT, mT, xT, y, ts, us, wt, fd, offs, ou
         for q in range(QUARTERS):
             nc.scalar.copy(woven(w2_il[q][:]), planar(w2[:, :, q_cols(q)]))
 
-        g_il = [keep.tile([P, QSLOTS, PACK], BF16, name=f"g_il{q}", tag=f"g_il{q}", align_bytes=64) for q in range(QUARTERS)]
+        g_il = [keep.tile([P, QSLOTS, PACK], BF16, name=f"g_il{q}", align_bytes=64) for q in range(QUARTERS)]
+        g_codes = keep.tile([P, SLOTS], U32, name="g_codes", align_bytes=64)
+        g_scales = keep.tile([P, SLOTS], U8, name="g_scales", align_bytes=64)
         scores = [bank(q, f"scores{q}") for q in range(QUARTERS)]
+        y_term = [keep.tile([P, PACK, QSLOTS], F32, name=f"y_term{q}") for q in range(QUARTERS)]
+        a_term = [keep.tile([P, PACK, QSLOTS], F32, name=f"a_term{q}") for q in range(QUARTERS)]
 
         def score_quarter(q):
             nc.vector.quantize_mx(w2_codes[q][:].bitcast(E4M3), w2_scales[q][:], w2_il[q][:].rearrange("p n t -> p (n t)"))
@@ -224,172 +197,89 @@ def tile_attend_gahead_nag_sq_kernel(tc, wT, mT, xT, y, ts, us, wt, fd, offs, ou
                     stop=True,
                 )
 
-        def g_cols(q):
-            return slice(PAD + q * QSLOTS, PAD + (q + 1) * QSLOTS)
+        def form_y_term(q):
+            nc.vector.tensor_tensor(y_term[q][:], y_raw[q // 2][:, :, q_cols(q % 2)], y_fac[:, :, q_cols(q)], MULT)
+
+        def form_a_term(q):
+            nc.vector.tensor_tensor(a_term[q][:], scores[q][:].rearrange("p (s n) -> p s n", s=PACK), a_fac[:, :, q_cols(q)], MULT)
+
+        def form_g(q):
+            nc.vector.tensor_tensor(woven(g_il[q][:]), planar(a_term[q][:]), planar(y_term[q][:]), SUB)
 
         def quantise_g(q):
-            nc.vector.quantize_mx(g_codes[:, g_cols(q)].bitcast(E5M2), g_scales[:, g_cols(q)], g_il[q][:].rearrange("p n s -> p (n s)"))
+            nc.vector.quantize_mx(g_codes[:, q_cols(q)].bitcast(E5M2), g_scales[:, q_cols(q)], g_il[q][:].rearrange("p n s -> p (n s)"))
 
-        def plane0_pass(out, first_col):
-            cols = slice(first_col, first_col + SLOTS)
+        grad = [bank(4 + t, f"grad{t}") for t in range(PACK)]
+
+        def grad_pass(t, lo, hi):
+            rows = slice(t * P, (t + 1) * P)
             nc.tensor.matmul_mx(
-                out,
-                lhsT=xr_codes[:, 0:P].bitcast(E4M3),
-                lhsT_scale=xr_scales[:, 0:P],
-                rhs=g_codes[:, cols].bitcast(E5M2),
-                rhs_scale=g_scales[:, cols],
+                grad[t][:, lo:hi],
+                lhsT=xr_codes[:, rows].bitcast(E4M3),
+                lhsT_scale=xr_scales[:, rows],
+                rhs=g_codes[:, lo:hi].bitcast(E5M2),
+                rhs_scale=g_scales[:, lo:hi],
                 start=True,
                 stop=True,
-            )
-
-        def quarter_pass(out, q):
-            nc.tensor.matmul_mx(
-                out,
-                lhsT=g_codes[:, g_cols(q)].bitcast(E5M2),
-                lhsT_scale=g_scales[:, g_cols(q)],
-                rhs=xr_codes[:].bitcast(E4M3),
-                rhs_scale=xr_scales[:],
-                start=True,
-                stop=True,
-            )
-
-        def y_of(q):
-            return y_raw[q // 2][:, :, q_cols(q % 2)]
-
-        a_scaled = {q: keep.tile([P, PACK, QSLOTS], F32, name=f"a_scaled{q}") for q in range(1, QUARTERS)}
-        summed = {q: bank(3 + q, f"summed{q}") for q in range(1, QUARTERS)}
-
-        def scale_scores(q):
-            for s in range(PACK):
-                nc.scalar.activation(a_scaled[q][:, s, :], scores[q][:, q_cols(s)], COPY, scale=a_row[:, s : s + 1])
-
-        def turn_into_sum(q, term, opens):
-            for s in range(PACK):
-                nc.tensor.matmul(
-                    summed[q][:, q_cols(s)],
-                    term[:, s, :],
-                    ident[:],
-                    start=(opens and s == 0),
-                    stop=(not opens and s == PACK - 1),
-                    is_transpose=True,
-                )
-
-        def round_and_turn_back(q, g_words):
-            g_turned = keep.tile([P, 2, P, 2], BF16, name=f"g_turned{q}")
-            nc.scalar.activation(
-                g_turned[:], summed[q][:].rearrange("i (u e p) -> i u p e", u=2, e=2), COPY, scale=ts2_col[:, q - 1 : q]
-            )
-            words = g_turned[:].rearrange("i u p e -> i (u p e)").bitcast(F32)
-            for u in range(2):
-                nc.tensor.transpose(g_words[:, q_cols(u)], words[:, q_cols(u)], ident[:])
-
-        def weave_words(q, g_words):
-            nc.scalar.copy(
-                g_il[q][:].rearrange("p n s -> p (n s)").bitcast(F32).rearrange("p (n u) -> p n u", u=2),
-                g_words[:, 0:HSLOTS].rearrange("p (u n) -> p n u", u=2),
             )
 
         dw = [keep.tile([P, SLOTS], F32, name=f"dw{t}") for t in range(PACK)]
-        step = [keep.tile([P, SLOTS], F32, name=f"step{t}") for t in range(PACK)]
-        dw_by_slot = keep.tile([P, QUARTERS, D], F32, name="dw_by_slot", tag="x_raw")
-        dw_turned = [dw_by_slot[:, q, :] for q in range(QUARTERS)]
+        nm = [keep.tile([P, SLOTS], F32, name=f"nm{t}") for t in range(PACK)]
 
-        def fetch(t, lo, hi, source):
-            nc.scalar.copy(dw[t][:, lo:hi], source)
-            nc.scalar.activation(step[t][:, lo:hi], source, COPY, scale=neg_fd2[:, t : t + 1])
+        def scalar_scatter(window, values, lo, hi):
+            for at in range(lo, hi, HSLOTS):
+                nc.scalar.activation(window[:].indirect(offs_of(at, at + HSLOTS)), values[:, at : at + HSLOTS], COPY)
 
-        def scatter_grad(t, lo, hi):
-            if hi - lo == QSLOTS:
-                nc.vector.tensor_tensor(grad_win[t][:].indirect(offs_of(lo, hi)), dw[t][:, lo:hi], zeros[:], ADD)
-            else:
-                nc.vector.tensor_copy(grad_win[t][:].indirect(offs_of(lo, hi)), dw[t][:, lo:hi])
+        def scalar_grad(t, lo, hi):
+            nc.scalar.copy(dw[t][:, lo:hi], grad[t][:, lo:hi])
+            scalar_scatter(grad_win[t % 3], dw[t], lo, hi)
             if hi == SLOTS:
-                nc.sync.dma_start(by_plane(out_1)[:, t, :], grad_win[t][:])
+                nc.scalar.dma_start(by_plane(out_1)[:, t, :], grad_win[t % 3][:])
 
-        def scatter_mom(t, lo, hi):
-            window = mom_win[MOM_WIN[t]]
-            nc.vector.tensor_tensor(window[:].indirect(offs_of(lo, hi)), m_g[t][:, lo:hi], step[t][:, lo:hi], ADD)
-            if hi == SLOTS:
-                nc.sync.dma_start(by_plane(out_0)[:, t, :], window[:])
+        def form_nm(t):
+            nc.vector.scalar_tensor_tensor(nm[t][:], grad[t][:], neg_fd2[:, t : t + 1], m_g[t][:], MULT, ADD)
 
-        def scatter(t, lo, hi):
-            scatter_grad(t, lo, hi)
-            scatter_mom(t, lo, hi)
+        def vector_mom(t):
+            form_nm(t)
+            nc.vector.tensor_copy(mom_win[t][:].indirect(offsets[:]), nm[t][:])
+            nc.sync.dma_start(by_plane(out_0)[:, t, :], mom_win[t][:])
 
-        def turn_back(out, q, t):
-            nc.tensor.transpose(out, dw_turned[q][:, q_cols(t)], ident[:])
-
-        y_term = keep.tile([P, PACK, QSLOTS], F32, name="y_term")
-        a_term = keep.tile([P, PACK, QSLOTS], F32, name="a_term")
         score_quarter(0)
+        form_y_term(0)
         score_quarter(1)
-        nc.vector.tensor_tensor(y_term[:], y_of(0), y_fac[:, :, q_cols(0)], MULT)
+        form_a_term(0)
         score_quarter(2)
-        nc.vector.tensor_tensor(a_term[:], scores[0][:].rearrange("p (s n) -> p s n", s=PACK), a_fac[:], MULT)
+        form_y_term(1)
+        form_a_term(1)
         score_quarter(3)
-        nc.vector.tensor_tensor(woven(g_il[0][:]), planar(a_term[:]), planar(y_term[:]), SUB)
+        form_g(0)
+        form_g(1)
         quantise_g(0)
-        y_scaled = keep.tile([P, TURNED, PACK, QSLOTS], F32, name="y_scaled", tag="g_il0", align_bytes=64)
-        for q in range(1, QUARTERS):
-            nc.vector.tensor_tensor(y_scaled[:, q - 1], y_of(q), y_fac[:, :, q_cols(q)], MULT)
-        early = bank(7, "early")
-        plane0_pass(early[:], 0)
-        fetch(0, 0, QSLOTS, early[:, PAD:SLOTS])
-        by_slot0 = bank(0, "by_slot0")
-        quarter_pass(by_slot0[:], 0)
-        nc.scalar.copy(dw_turned[0][:, P:D], by_slot0[:, P:D])
-        scatter(0, 0, QSLOTS)
-        back01 = bank(7, "back01")
-        turn_back(back01[:, q_cols(0)], 0, 1)
-        fetch(1, 0, QSLOTS, back01[:, q_cols(0)])
-        scatter(1, 0, QSLOTS)
-
-        scale_scores(1)
-        turn_into_sum(1, a_scaled[1][:], opens=True)
-        turn_into_sum(1, y_scaled[:, 0], opens=False)
-        mixed1 = bank(1, "mixed1")
-        round_and_turn_back(1, mixed1)
-        for t in (2, 3):
-            turn_back(mixed1[:, q_cols(t)], 0, t)
-        weave_words(1, mixed1)
+        form_y_term(2)
         quantise_g(1)
-        for t in (2, 3):
-            fetch(t, 0, QSLOTS, mixed1[:, q_cols(t)])
-        scatter(2, 0, QSLOTS)
-        scatter_grad(3, 0, QSLOTS)
-        by_slot1 = bank(7, "by_slot1")
-        quarter_pass(by_slot1[:], 1)
-        nc.scalar.copy(dw_turned[1][:, 0 : 2 * P], by_slot1[:, 0 : 2 * P])
-
-        mixed = {}
-        for q in (2, 3):
-            scale_scores(q)
-            turn_into_sum(q, a_scaled[q][:], opens=True)
-            turn_into_sum(q, y_scaled[:, q - 1], opens=False)
-            mixed[q] = bank(q, f"mixed{q}")
-            round_and_turn_back(q, mixed[q])
-            turn_back(mixed[q][:, q_cols(2)], 1, q - 2)
-            weave_words(q, mixed[q])
-            quantise_g(q)
-            fetch(q - 2, QSLOTS, HSLOTS, mixed[q][:, q_cols(2)])
-            scatter_grad(q - 2, QSLOTS, HSLOTS)
-        scatter_mom(1, QSLOTS, HSLOTS)
-
-        whole0 = bank(4, "whole0")
-        plane0_pass(whole0[:], PAD)
-        fetch(0, HSLOTS, SLOTS, whole0[:, HSLOTS:SLOTS])
-        scatter_grad(0, HSLOTS, SLOTS)
-        scatter_mom(0, QSLOTS, SLOTS)
-        for q, number in ((3, 5), (2, 3)):
-            by_slot = bank(number, f"by_slot{q}")
-            quarter_pass(by_slot[:], q)
-            nc.scalar.copy(dw_turned[q][:, P:D], by_slot[:, P:D])
-        nc.scalar.copy(dw_turned[1][:, 2 * P : D], by_slot1[:, 2 * P : D])
-        for t, number in ((1, 6), (2, 4), (3, 5)):
-            back = bank(number, f"back{t}")
-            first = 2 if t == 1 else 1
-            for q in range(first, QUARTERS):
-                turn_back(back[:, q_cols(q)], q, t)
-            fetch(t, first * QSLOTS, SLOTS, back[:, first * QSLOTS : SLOTS])
-            scatter_grad(t, first * QSLOTS, SLOTS)
-            scatter_mom(t, 0 if t == LAST else first * QSLOTS, SLOTS)
+        for t in range(2):
+            grad_pass(t, 0, HSLOTS)
+            scalar_grad(t, 0, HSLOTS)
+        form_a_term(2)
+        form_y_term(3)
+        form_a_term(3)
+        form_g(2)
+        form_g(3)
+        quantise_g(2)
+        quantise_g(3)
+        for t in range(2):
+            grad_pass(t, HSLOTS, SLOTS)
+        for t in range(2, PACK):
+            grad_pass(t, 0, SLOTS)
+        scalar_grad(0, HSLOTS, SLOTS)
+        nc.vector.tensor_copy(dw[1][:, HSLOTS:SLOTS], grad[1][:, HSLOTS:SLOTS])
+        nc.vector.tensor_copy(grad_win[1][:].indirect(offs_of(HSLOTS, SLOTS)), dw[1][:, HSLOTS:SLOTS])
+        nc.sync.dma_start(by_plane(out_1)[:, 1, :], grad_win[1][:])
+        scalar_grad(2, 0, SLOTS)
+        vector_mom(0)
+        scalar_grad(3, 0, SLOTS)
+        vector_mom(1)
+        form_nm(LAST)
+        vector_mom(2)
+        scalar_scatter(mom_win[0], nm[LAST], 0, SLOTS)
+        nc.scalar.dma_start(by_plane(out_0)[:, LAST, :], mom_win[0][:])

@@ -27,6 +27,8 @@ QUARTERS = 4
 QSLOTS = SLOTS // QUARTERS
 HSLOTS = SLOTS // 2
 OFFS_PER_COL = 16
+TURNED = (0, 1)
+DIRECT = (2, 3)
 RUN = 2
 
 
@@ -58,9 +60,9 @@ def tile_attend_gahead_nag_sq_kernel(tc, wT, mT, xT, y, ts, us, wt, fd, offs, ou
 
         m_pair = [keep.tile([P, 2, TABLE], F32, name=f"m_pair{j}") for j in range(2)]
         w_win = [keep.tile([P, TABLE], F32, name=f"w_win{t}") for t in range(PACK)]
-        x_raw = keep.tile([P, PACK, R], F32, name="x_raw")
+        x_raw = keep.tile([P, PACK, R], F32, name="x_raw", tag="x_raw")
         y_raw = [keep.tile([P, PACK, HSLOTS], F32, name=f"y_raw{h}") for h in range(2)]
-        ts_win = keep.tile([P, TABLE], F32, name="ts_win")
+        ts_win = keep.tile([P, TABLE], F32, name="ts_win", tag="ts_win")
         us_c = keep.tile([P, PACK], F32, name="us_c")
         wt_c = keep.tile([P, PACK], F32, name="wt_c")
         fd_c = keep.tile([P, PACK], F32, name="fd_c")
@@ -104,7 +106,7 @@ def tile_attend_gahead_nag_sq_kernel(tc, wT, mT, xT, y, ts, us, wt, fd, offs, ou
         a_row = keep.tile([P, PACK], F32, name="a_row")
         neg_fd2 = keep.tile([P, PACK], F32, name="neg_fd2")
 
-        m_g = [keep.tile([P, SLOTS], F32, name=f"m_g{t}") for t in range(PACK)]
+        m_g = [keep.tile([P, SLOTS], F32, name=f"m_g{t}", tag=f"m_g{t}") for t in range(PACK)]
         w2 = keep.tile([P, PACK, SLOTS], F32, name="w2")
 
         def gather_plane(t):
@@ -117,12 +119,18 @@ def tile_attend_gahead_nag_sq_kernel(tc, wT, mT, xT, y, ts, us, wt, fd, offs, ou
 
         nc.vector.tensor_tensor(y_row[:], wt_c[:], us_c[:], MULT)
         nc.vector.tensor_tensor(a_row[:], y_row[:], us_c[:], MULT)
+        neg_y_row = keep.tile([P, PACK], F32, name="neg_y_row")
+        nc.vector.tensor_scalar(neg_y_row[:], y_row[:], -1.0, 0.0, MULT, ADD)
         ts_g = keep.tile([P, SLOTS], F32, name="ts_g")
         nc.vector.tensor_copy(ts_g[:], ts_win[:].indirect(offsets[:]))
+        mom_win.append(keep.tile([P, TABLE], F32, name="mom_win3", tag="ts_win"))
+        nc.gpsimd.memset(mom_win[LAST][:], 0.0)
         gather_plane(0)
 
         x_bf = keep.tile([P, PACK, R], BF16, name="x_bf", align_bytes=64)
         nc.scalar.copy(x_bf[:], x_raw[:])
+        grad_win.append(keep.tile([P, TABLE], F32, name="grad_win3", tag="x_raw"))
+        nc.gpsimd.memset(grad_win[LAST][:], 0.0)
         x_words = x_bf[:].rearrange("p t r -> p (t r)").bitcast(F32)
         xr_il = keep.tile([P, D, PACK], BF16, name="xr_il", align_bytes=64)
         xr_words = xr_il[:].rearrange("p d s -> p (d s)").bitcast(F32)
@@ -147,13 +155,20 @@ def tile_attend_gahead_nag_sq_kernel(tc, wT, mT, xT, y, ts, us, wt, fd, offs, ou
             x_bf[:].rearrange("p t (r s) -> p s r t", s=PACK),
         )
 
-        ts_sq = keep.tile([P, SLOTS], F32, name="ts_sq")
+        ts_turned = bank(6, "ts_turned")
+        for k, q in enumerate(TURNED):
+            nc.tensor.transpose(ts_turned[:, q_cols(k)], ts_g[:, q_cols(q)], ident[:])
+        ts_col = keep.tile([P, len(TURNED)], F32, name="ts_col")
+        nc.scalar.copy(ts_col[:], ts_turned[:, 0 : len(TURNED) * QSLOTS : QSLOTS])
+
+        ts_pow = keep.tile([P, SLOTS], F32, name="ts_pow")
         a_fac = keep.tile([P, PACK, SLOTS], F32, name="a_fac")
-        y_fac = keep.tile([P, PACK, SLOTS], F32, name="y_fac")
-        nc.scalar.activation(ts_sq[:], ts_g[:], SQUARE)
+        y_fac = keep.tile([P, PACK, HSLOTS], F32, name="y_fac")
+        nc.scalar.copy(ts_pow[:, 0:HSLOTS], ts_g[:, 0:HSLOTS])
+        nc.scalar.activation(ts_pow[:, HSLOTS:SLOTS], ts_g[:, HSLOTS:SLOTS], SQUARE)
         for s in range(PACK):
-            nc.scalar.activation(y_fac[:, s, :], ts_g[:], COPY, scale=y_row[:, s : s + 1])
-            nc.scalar.activation(a_fac[:, s, :], ts_sq[:], COPY, scale=a_row[:, s : s + 1])
+            nc.scalar.activation(y_fac[:, s, :], ts_g[:, HSLOTS:SLOTS], COPY, scale=y_row[:, s : s + 1])
+            nc.scalar.activation(a_fac[:, s, :], ts_pow[:], COPY, scale=a_row[:, s : s + 1])
 
         gather_plane(1)
 
@@ -173,14 +188,16 @@ def tile_attend_gahead_nag_sq_kernel(tc, wT, mT, xT, y, ts, us, wt, fd, offs, ou
         w2_il = [keep.tile([P, QSLOTS, PACK], BF16, name=f"w2_il{q}", align_bytes=64) for q in range(QUARTERS)]
         w2_codes = [keep.tile([P, QSLOTS], U32, name=f"w2_codes{q}", align_bytes=64) for q in range(QUARTERS)]
         w2_scales = [keep.tile([P, QSLOTS], U8, name=f"w2_scales{q}", align_bytes=64) for q in range(QUARTERS)]
-        for q in range(QUARTERS):
+
+        def weave_w2(q):
             nc.scalar.copy(woven(w2_il[q][:]), planar(w2[:, :, q_cols(q)]))
 
         g_il = [keep.tile([P, QSLOTS, PACK], BF16, name=f"g_il{q}", align_bytes=64) for q in range(QUARTERS)]
         g_codes = keep.tile([P, SLOTS], U32, name="g_codes", align_bytes=64)
         g_scales = keep.tile([P, SLOTS], U8, name="g_scales", align_bytes=64)
         scores = [bank(q, f"scores{q}") for q in range(QUARTERS)]
-        y_term = [keep.tile([P, PACK, QSLOTS], F32, name=f"y_term{q}") for q in range(QUARTERS)]
+        y_term = {q: keep.tile([P, PACK, QSLOTS], F32, name=f"y_term{q}") for q in DIRECT}
+        y_scaled = keep.tile([P, PACK, HSLOTS], F32, name="y_scaled")
         a_term = [keep.tile([P, PACK, QSLOTS], F32, name=f"a_term{q}") for q in range(QUARTERS)]
 
         def score_quarter(q):
@@ -198,7 +215,7 @@ def tile_attend_gahead_nag_sq_kernel(tc, wT, mT, xT, y, ts, us, wt, fd, offs, ou
                 )
 
         def form_y_term(q):
-            nc.vector.tensor_tensor(y_term[q][:], y_raw[q // 2][:, :, q_cols(q % 2)], y_fac[:, :, q_cols(q)], MULT)
+            nc.vector.tensor_tensor(y_term[q][:], y_raw[q // 2][:, :, q_cols(q % 2)], y_fac[:, :, q_cols(q % 2)], MULT)
 
         def form_a_term(q):
             nc.vector.tensor_tensor(a_term[q][:], scores[q][:].rearrange("p (s n) -> p s n", s=PACK), a_fac[:, :, q_cols(q)], MULT)
@@ -209,7 +226,42 @@ def tile_attend_gahead_nag_sq_kernel(tc, wT, mT, xT, y, ts, us, wt, fd, offs, ou
         def quantise_g(q):
             nc.vector.quantize_mx(g_codes[:, q_cols(q)].bitcast(E5M2), g_scales[:, q_cols(q)], g_il[q][:].rearrange("p n s -> p (n s)"))
 
-        grad = [bank(4 + t, f"grad{t}") for t in range(PACK)]
+        def scale_y():
+            for s in range(PACK):
+                nc.scalar.activation(y_scaled[:, s, :], y_raw[0][:, s, :], COPY, scale=neg_y_row[:, s : s + 1])
+
+        summed = {q: bank(4 + q, f"summed{q}") for q in TURNED}
+
+        def turn_into_sum(q, term, opens):
+            for s in range(PACK):
+                nc.tensor.matmul(
+                    summed[q][:, q_cols(s)],
+                    term[:, s, :],
+                    ident[:],
+                    start=(opens and s == 0),
+                    stop=(not opens and s == PACK - 1),
+                    is_transpose=True,
+                )
+
+        g_words = {}
+
+        def round_and_turn_back(q):
+            g_turned = keep.tile([P, 2, P, 2], BF16, name=f"g_turned{q}")
+            nc.scalar.activation(
+                g_turned[:], summed[q][:].rearrange("i (u e p) -> i u p e", u=2, e=2), COPY, scale=ts_col[:, q : q + 1]
+            )
+            words = g_turned[:].rearrange("i u p e -> i (u p e)").bitcast(F32)
+            g_words[q] = bank(q, f"g_words{q}")
+            for u in range(2):
+                nc.tensor.transpose(g_words[q][:, q_cols(u)], words[:, q_cols(u)], ident[:])
+
+        def weave_words(q):
+            nc.scalar.copy(
+                g_il[q][:].rearrange("p n s -> p (n s)").bitcast(F32).rearrange("p (n u) -> p n u", u=2),
+                g_words[q][:, 0:HSLOTS].rearrange("p (u n) -> p n u", u=2),
+            )
+
+        grad = {}
 
         def grad_pass(t, lo, hi):
             rows = slice(t * P, (t + 1) * P)
@@ -223,63 +275,79 @@ def tile_attend_gahead_nag_sq_kernel(tc, wT, mT, xT, y, ts, us, wt, fd, offs, ou
                 stop=True,
             )
 
-        dw = [keep.tile([P, SLOTS], F32, name=f"dw{t}") for t in range(PACK)]
-        nm = [keep.tile([P, SLOTS], F32, name=f"nm{t}") for t in range(PACK)]
+        nm = {}
 
-        def scalar_scatter(window, values, lo, hi):
-            for at in range(lo, hi, HSLOTS):
-                nc.scalar.activation(window[:].indirect(offs_of(at, at + HSLOTS)), values[:, at : at + HSLOTS], COPY)
+        def staged(name, tag, width=SLOTS):
+            return keep.tile([P, width], F32, name=name, tag=tag)
 
-        def scalar_grad(t, lo, hi):
-            nc.scalar.copy(dw[t][:, lo:hi], grad[t][:, lo:hi])
-            scalar_scatter(grad_win[t % 3], dw[t], lo, hi)
-            if hi == SLOTS:
-                nc.scalar.dma_start(by_plane(out_1)[:, t, :], grad_win[t % 3][:])
+        def scalar_scatter(window, values, h):
+            nc.scalar.activation(window[:].indirect(offs_of(h * HSLOTS, (h + 1) * HSLOTS)), values, COPY)
 
-        def form_nm(t):
+        def scalar_grad(t, h):
+            half = staged(f"dw{t}_{h}", f"scalar_stage{h}", HSLOTS)
+            nc.scalar.copy(half[:], grad[t][:, h * HSLOTS : (h + 1) * HSLOTS])
+            scalar_scatter(grad_win[t], half[:], h)
+            if h == 1:
+                nc.sync.dma_start(by_plane(out_1)[:, t, :], grad_win[t][:])
+
+        def form_nm(t, tag):
+            nm[t] = staged(f"nm{t}", tag)
             nc.vector.scalar_tensor_tensor(nm[t][:], grad[t][:], neg_fd2[:, t : t + 1], m_g[t][:], MULT, ADD)
 
         def vector_mom(t):
-            form_nm(t)
             nc.vector.tensor_copy(mom_win[t][:].indirect(offsets[:]), nm[t][:])
             nc.sync.dma_start(by_plane(out_0)[:, t, :], mom_win[t][:])
 
+        weave_w2(0)
+        weave_w2(1)
+        scale_y()
+        weave_w2(2)
+        weave_w2(3)
         score_quarter(0)
-        form_y_term(0)
         score_quarter(1)
-        form_a_term(0)
-        score_quarter(2)
-        form_y_term(1)
-        form_a_term(1)
-        score_quarter(3)
-        form_g(0)
-        form_g(1)
-        quantise_g(0)
+        for q in TURNED:
+            form_a_term(q)
+            turn_into_sum(q, y_scaled[:, :, q_cols(q)], opens=True)
+            turn_into_sum(q, a_term[q], opens=False)
         form_y_term(2)
-        quantise_g(1)
-        for t in range(2):
-            grad_pass(t, 0, HSLOTS)
-            scalar_grad(t, 0, HSLOTS)
-        form_a_term(2)
+        score_quarter(2)
         form_y_term(3)
+        score_quarter(3)
+        for q in TURNED:
+            round_and_turn_back(q)
+        form_a_term(2)
+        for q in TURNED:
+            weave_words(q)
         form_a_term(3)
+        quantise_g(0)
+        quantise_g(1)
+        grad[0] = bank(6, "grad0")
+        grad_pass(0, 0, HSLOTS)
+        scalar_grad(0, 0)
         form_g(2)
         form_g(3)
         quantise_g(2)
         quantise_g(3)
-        for t in range(2):
-            grad_pass(t, HSLOTS, SLOTS)
-        for t in range(2, PACK):
+        grad_pass(0, HSLOTS, SLOTS)
+        for t, number in ((1, 7), (2, 4), (3, 5)):
+            grad[t] = bank(number, f"grad{t}")
             grad_pass(t, 0, SLOTS)
-        scalar_grad(0, HSLOTS, SLOTS)
-        nc.vector.tensor_copy(dw[1][:, HSLOTS:SLOTS], grad[1][:, HSLOTS:SLOTS])
-        nc.vector.tensor_copy(grad_win[1][:].indirect(offs_of(HSLOTS, SLOTS)), dw[1][:, HSLOTS:SLOTS])
+        scalar_grad(0, 1)
+        dw1 = staged("dw1", "vector_stage0")
+        nc.vector.tensor_copy(dw1[:], grad[1][:])
+        form_nm(1, "vector_stage1")
+        nc.vector.tensor_copy(grad_win[1][:].indirect(offsets[:]), dw1[:])
         nc.sync.dma_start(by_plane(out_1)[:, 1, :], grad_win[1][:])
-        scalar_grad(2, 0, SLOTS)
-        vector_mom(0)
-        scalar_grad(3, 0, SLOTS)
+        for h in range(2):
+            scalar_grad(2, h)
         vector_mom(1)
-        form_nm(LAST)
+        for h in range(2):
+            scalar_grad(3, h)
+        form_nm(LAST, "vector_stage1")
+        form_nm(0, f"m_g{LAST}")
+        vector_mom(0)
+        for h in range(2):
+            scalar_scatter(mom_win[LAST], nm[LAST][:, h * HSLOTS : (h + 1) * HSLOTS], h)
+        nc.scalar.dma_start(by_plane(out_0)[:, LAST, :], mom_win[LAST][:])
+        form_nm(2, "m_g0")
         vector_mom(2)
-        scalar_scatter(mom_win[0], nm[LAST], 0, SLOTS)
-        nc.scalar.dma_start(by_plane(out_0)[:, LAST, :], mom_win[0][:])

@@ -27,8 +27,9 @@ QUARTERS = 4
 QSLOTS = SLOTS // QUARTERS
 HSLOTS = SLOTS // 2
 OFFS_PER_COL = 16
-TURNED = (0, 1)
-DIRECT = (2, 3)
+TURNED = tuple(range(1))
+DIRECT = tuple(range(1, QUARTERS))
+DIRECT_LO = len(TURNED) * QSLOTS
 RUN = 2
 
 
@@ -163,11 +164,11 @@ def tile_attend_gahead_nag_sq_kernel(tc, wT, mT, xT, y, ts, us, wt, fd, offs, ou
 
         ts_pow = keep.tile([P, SLOTS], F32, name="ts_pow")
         a_fac = keep.tile([P, PACK, SLOTS], F32, name="a_fac")
-        y_fac = keep.tile([P, PACK, HSLOTS], F32, name="y_fac")
-        nc.scalar.copy(ts_pow[:, 0:HSLOTS], ts_g[:, 0:HSLOTS])
-        nc.scalar.activation(ts_pow[:, HSLOTS:SLOTS], ts_g[:, HSLOTS:SLOTS], SQUARE)
+        y_fac = keep.tile([P, PACK, SLOTS - DIRECT_LO], F32, name="y_fac")
+        nc.scalar.copy(ts_pow[:, 0:DIRECT_LO], ts_g[:, 0:DIRECT_LO])
+        nc.scalar.activation(ts_pow[:, DIRECT_LO:SLOTS], ts_g[:, DIRECT_LO:SLOTS], SQUARE)
         for s in range(PACK):
-            nc.scalar.activation(y_fac[:, s, :], ts_g[:, HSLOTS:SLOTS], COPY, scale=y_row[:, s : s + 1])
+            nc.scalar.activation(y_fac[:, s, :], ts_g[:, DIRECT_LO:SLOTS], COPY, scale=y_row[:, s : s + 1])
             nc.scalar.activation(a_fac[:, s, :], ts_pow[:], COPY, scale=a_row[:, s : s + 1])
 
         gather_plane(1)
@@ -197,7 +198,7 @@ def tile_attend_gahead_nag_sq_kernel(tc, wT, mT, xT, y, ts, us, wt, fd, offs, ou
         g_scales = keep.tile([P, SLOTS], U8, name="g_scales", align_bytes=64)
         scores = [bank(q, f"scores{q}") for q in range(QUARTERS)]
         y_term = {q: keep.tile([P, PACK, QSLOTS], F32, name=f"y_term{q}") for q in DIRECT}
-        y_scaled = keep.tile([P, PACK, HSLOTS], F32, name="y_scaled")
+        y_scaled = keep.tile([P, PACK, DIRECT_LO], F32, name="y_scaled")
         a_term = [keep.tile([P, PACK, QSLOTS], F32, name=f"a_term{q}") for q in range(QUARTERS)]
 
         def score_quarter(q):
@@ -215,7 +216,7 @@ def tile_attend_gahead_nag_sq_kernel(tc, wT, mT, xT, y, ts, us, wt, fd, offs, ou
                 )
 
         def form_y_term(q):
-            nc.vector.tensor_tensor(y_term[q][:], y_raw[q // 2][:, :, q_cols(q % 2)], y_fac[:, :, q_cols(q % 2)], MULT)
+            nc.vector.tensor_tensor(y_term[q][:], y_raw[q // 2][:, :, q_cols(q % 2)], y_fac[:, :, q_cols(q - len(TURNED))], MULT)
 
         def form_a_term(q):
             nc.vector.tensor_tensor(a_term[q][:], scores[q][:].rearrange("p (s n) -> p s n", s=PACK), a_fac[:, :, q_cols(q)], MULT)
@@ -228,7 +229,7 @@ def tile_attend_gahead_nag_sq_kernel(tc, wT, mT, xT, y, ts, us, wt, fd, offs, ou
 
         def scale_y():
             for s in range(PACK):
-                nc.scalar.activation(y_scaled[:, s, :], y_raw[0][:, s, :], COPY, scale=neg_y_row[:, s : s + 1])
+                nc.scalar.activation(y_scaled[:, s, :], y_raw[0][:, s, 0:DIRECT_LO], COPY, scale=neg_y_row[:, s : s + 1])
 
         summed = {q: bank(4 + q, f"summed{q}") for q in TURNED}
 
@@ -275,27 +276,27 @@ def tile_attend_gahead_nag_sq_kernel(tc, wT, mT, xT, y, ts, us, wt, fd, offs, ou
                 stop=True,
             )
 
-        nm = {}
-
-        def staged(name, tag, width=SLOTS):
-            return keep.tile([P, width], F32, name=name, tag=tag)
 
         def scalar_scatter(window, values, h):
             nc.scalar.activation(window[:].indirect(offs_of(h * HSLOTS, (h + 1) * HSLOTS)), values, COPY)
 
-        def scalar_grad(t, h):
-            half = staged(f"dw{t}_{h}", f"scalar_stage{h}", HSLOTS)
-            nc.scalar.copy(half[:], grad[t][:, h * HSLOTS : (h + 1) * HSLOTS])
-            scalar_scatter(grad_win[t], half[:], h)
+        def scatter_grad_half(t, h, half):
+            scalar_scatter(grad_win[t], half, h)
             if h == 1:
                 nc.sync.dma_start(by_plane(out_1)[:, t, :], grad_win[t][:])
 
-        def form_nm(t, tag):
-            nm[t] = staged(f"nm{t}", tag)
-            nc.vector.scalar_tensor_tensor(nm[t][:], grad[t][:], neg_fd2[:, t : t + 1], m_g[t][:], MULT, ADD)
+        grad[0] = bank(6, "grad0")
+        dw0 = [keep.tile([P, HSLOTS], F32, name=f"dw0_{h}") for h in range(2)]
+
+        def early_quarter(q):
+            quantise_g(q)
+            grad_pass(0, q * QSLOTS, (q + 1) * QSLOTS)
+            nc.scalar.copy(dw0[0][:, q_cols(q)], grad[0][:, q_cols(q)])
 
         def vector_mom(t):
-            nc.vector.tensor_copy(mom_win[t][:].indirect(offsets[:]), nm[t][:])
+            nm = keep.tile([P, SLOTS], F32, name=f"nm{t}", tag=f"nm_stage{t % 2}")
+            nc.vector.scalar_tensor_tensor(nm[:], grad[t][:], neg_fd2[:, t : t + 1], m_g[t][:], MULT, ADD)
+            nc.vector.tensor_copy(mom_win[t][:].indirect(offsets[:]), nm[:])
             nc.sync.dma_start(by_plane(out_0)[:, t, :], mom_win[t][:])
 
         weave_w2(0)
@@ -304,50 +305,40 @@ def tile_attend_gahead_nag_sq_kernel(tc, wT, mT, xT, y, ts, us, wt, fd, offs, ou
         weave_w2(2)
         weave_w2(3)
         score_quarter(0)
+        form_y_term(1)
         score_quarter(1)
-        for q in TURNED:
-            form_a_term(q)
-            turn_into_sum(q, y_scaled[:, :, q_cols(q)], opens=True)
-            turn_into_sum(q, a_term[q], opens=False)
-        form_y_term(2)
+        turn_into_sum(0, y_scaled[:, :, q_cols(0)], opens=True)
+        form_a_term(0)
+        turn_into_sum(0, a_term[0], opens=False)
+        round_and_turn_back(0)
+        form_a_term(1)
         score_quarter(2)
-        form_y_term(3)
+        form_g(1)
+        weave_words(0)
         score_quarter(3)
-        for q in TURNED:
-            round_and_turn_back(q)
+        early_quarter(1)
+        form_y_term(2)
+        early_quarter(0)
+        scatter_grad_half(0, 0, dw0[0][:])
         form_a_term(2)
-        for q in TURNED:
-            weave_words(q)
+        form_y_term(3)
         form_a_term(3)
-        quantise_g(0)
-        quantise_g(1)
-        grad[0] = bank(6, "grad0")
-        grad_pass(0, 0, HSLOTS)
-        scalar_grad(0, 0)
         form_g(2)
         form_g(3)
-        quantise_g(2)
-        quantise_g(3)
-        grad_pass(0, HSLOTS, SLOTS)
+        for q in (2, 3):
+            quantise_g(q)
+            grad_pass(0, q * QSLOTS, (q + 1) * QSLOTS)
         for t, number in ((1, 7), (2, 4), (3, 5)):
             grad[t] = bank(number, f"grad{t}")
             grad_pass(t, 0, SLOTS)
-        scalar_grad(0, 1)
-        dw1 = staged("dw1", "vector_stage0")
-        nc.vector.tensor_copy(dw1[:], grad[1][:])
-        form_nm(1, "vector_stage1")
-        nc.vector.tensor_copy(grad_win[1][:].indirect(offsets[:]), dw1[:])
-        nc.sync.dma_start(by_plane(out_1)[:, 1, :], grad_win[1][:])
-        for h in range(2):
-            scalar_grad(2, h)
-        vector_mom(1)
-        for h in range(2):
-            scalar_grad(3, h)
-        form_nm(LAST, "vector_stage1")
-        form_nm(0, f"m_g{LAST}")
+        nc.vector.tensor_copy(dw0[1][:], grad[0][:, HSLOTS:SLOTS])
+        scatter_grad_half(0, 1, dw0[1][:])
         vector_mom(0)
-        for h in range(2):
-            scalar_scatter(mom_win[LAST], nm[LAST][:, h * HSLOTS : (h + 1) * HSLOTS], h)
-        nc.scalar.dma_start(by_plane(out_0)[:, LAST, :], mom_win[LAST][:])
-        form_nm(2, "m_g0")
-        vector_mom(2)
+        reused = keep.tile([P, SLOTS], F32, name="dw_stage", tag="m_g0")
+        ring = (reused[:, 0:HSLOTS], dw0[1][:], reused[:, HSLOTS:SLOTS])
+        for t in range(1, PACK):
+            for h in range(2):
+                half = ring[(2 * (t - 1) + h) % len(ring)]
+                nc.scalar.copy(half, grad[t][:, h * HSLOTS : (h + 1) * HSLOTS])
+                scatter_grad_half(t, h, half)
+            vector_mom(t)

@@ -29,6 +29,7 @@ HSLOTS = SLOTS // 2
 OFFS_PER_COL = 16
 TURNED = tuple(range(1))
 DIRECT = tuple(range(1, QUARTERS))
+ORDER = (0, 2, 3, 1)
 DIRECT_LO = len(TURNED) * QSLOTS
 RUN = 2
 
@@ -62,7 +63,7 @@ def tile_attend_gahead_nag_sq_kernel(tc, wT, mT, xT, y, ts, us, wt, fd, offs, ou
         m_pair = [keep.tile([P, 2, TABLE], F32, name=f"m_pair{j}") for j in range(2)]
         w_win = [keep.tile([P, TABLE], F32, name=f"w_win{t}") for t in range(PACK)]
         x_raw = keep.tile([P, PACK, R], F32, name="x_raw", tag="x_raw")
-        y_raw = [keep.tile([P, PACK, HSLOTS], F32, name=f"y_raw{h}") for h in range(2)]
+        y_raw = [keep.tile([P, PACK, HSLOTS], F32, name=f"y_raw{h}", tag=f"y_raw{h}", align_bytes=64) for h in range(2)]
         ts_win = keep.tile([P, TABLE], F32, name="ts_win", tag="ts_win")
         us_c = keep.tile([P, PACK], F32, name="us_c")
         wt_c = keep.tile([P, PACK], F32, name="wt_c")
@@ -78,7 +79,7 @@ def tile_attend_gahead_nag_sq_kernel(tc, wT, mT, xT, y, ts, us, wt, fd, offs, ou
             nc.sync.dma_start(m_pair[j][:], by_plane(mT)[:, 2 * j : 2 * j + 2, :])
         for t in range(PACK):
             nc.sync.dma_start(w_win[t][:], by_plane(wT)[:, t, :])
-        for h in range(2):
+        for h in (1, 0):
             nc.sync.dma_start(y_raw[h][:], by_plane(y)[:, :, h * HSLOTS : (h + 1) * HSLOTS])
         nc.sync.dma_start(fd_c[:], by_plane(fd)[:, :, 0])
 
@@ -113,7 +114,7 @@ def tile_attend_gahead_nag_sq_kernel(tc, wT, mT, xT, y, ts, us, wt, fd, offs, ou
         def gather_plane(t):
             nc.vector.tensor_copy(m_g[t][:], m_pair[t // 2][:, t % 2, :].indirect(offsets[:]))
             width = QSLOTS if t == LAST else SLOTS
-            for lo in range(0, SLOTS, width):
+            for lo in [q * QSLOTS for q in ORDER] if t == LAST else [0]:
                 nc.vector.tensor_tensor(
                     w2[:, t, lo : lo + width], w_win[t][:].indirect(offs_of(lo, lo + width)), m_g[t][:, lo : lo + width], ADD
                 )
@@ -193,13 +194,13 @@ def tile_attend_gahead_nag_sq_kernel(tc, wT, mT, xT, y, ts, us, wt, fd, offs, ou
         def weave_w2(q):
             nc.scalar.copy(woven(w2_il[q][:]), planar(w2[:, :, q_cols(q)]))
 
-        g_il = [keep.tile([P, QSLOTS, PACK], BF16, name=f"g_il{q}", align_bytes=64) for q in range(QUARTERS)]
+        g_il = {q: keep.tile([P, QSLOTS, PACK], BF16, name=f"g_il{q}", tag=f"g_il{q}", align_bytes=64) for q in DIRECT}
         g_codes = keep.tile([P, SLOTS], U32, name="g_codes", align_bytes=64)
         g_scales = keep.tile([P, SLOTS], U8, name="g_scales", align_bytes=64)
         scores = [bank(q, f"scores{q}") for q in range(QUARTERS)]
-        y_term = {q: keep.tile([P, PACK, QSLOTS], F32, name=f"y_term{q}") for q in DIRECT}
+        y_term = {q: keep.tile([P, PACK, QSLOTS], F32, name=f"y_term{q}") for q in (2, 3)}
         y_scaled = keep.tile([P, PACK, DIRECT_LO], F32, name="y_scaled")
-        a_term = [keep.tile([P, PACK, QSLOTS], F32, name=f"a_term{q}") for q in range(QUARTERS)]
+        a_term = {q: keep.tile([P, PACK, QSLOTS], F32, name=f"a_term{q}") for q in (0, 2, 3)}
 
         def score_quarter(q):
             nc.vector.quantize_mx(w2_codes[q][:].bitcast(E4M3), w2_scales[q][:], w2_il[q][:].rearrange("p n t -> p (n t)"))
@@ -257,7 +258,7 @@ def tile_attend_gahead_nag_sq_kernel(tc, wT, mT, xT, y, ts, us, wt, fd, offs, ou
                 nc.tensor.transpose(g_words[q][:, q_cols(u)], words[:, q_cols(u)], ident[:])
 
         def weave_words(q):
-            nc.scalar.copy(
+            nc.vector.tensor_copy(
                 g_il[q][:].rearrange("p n s -> p (n s)").bitcast(F32).rearrange("p (n u) -> p n u", u=2),
                 g_words[q][:, 0:HSLOTS].rearrange("p (u n) -> p n u", u=2),
             )
@@ -282,16 +283,15 @@ def tile_attend_gahead_nag_sq_kernel(tc, wT, mT, xT, y, ts, us, wt, fd, offs, ou
 
         def scatter_grad_half(t, h, half):
             scalar_scatter(grad_win[t], half, h)
-            if h == 1:
+            if h == 0:
                 nc.sync.dma_start(by_plane(out_1)[:, t, :], grad_win[t][:])
 
-        grad[0] = bank(6, "grad0")
         dw0 = [keep.tile([P, HSLOTS], F32, name=f"dw0_{h}") for h in range(2)]
 
         def early_quarter(q):
             quantise_g(q)
             grad_pass(0, q * QSLOTS, (q + 1) * QSLOTS)
-            nc.scalar.copy(dw0[0][:, q_cols(q)], grad[0][:, q_cols(q)])
+            nc.scalar.copy(dw0[1][:, q_cols(q % 2)], grad[0][:, q_cols(q)])
 
         def vector_mom(t):
             nm = keep.tile([P, SLOTS], F32, name=f"nm{t}", tag=f"nm_stage{t % 2}")
@@ -300,45 +300,49 @@ def tile_attend_gahead_nag_sq_kernel(tc, wT, mT, xT, y, ts, us, wt, fd, offs, ou
             nc.sync.dma_start(by_plane(out_0)[:, t, :], mom_win[t][:])
 
         weave_w2(0)
-        weave_w2(1)
-        scale_y()
         weave_w2(2)
         weave_w2(3)
+        scale_y()
+        weave_w2(1)
         score_quarter(0)
-        form_y_term(1)
-        score_quarter(1)
+        form_y_term(2)
+        score_quarter(2)
         turn_into_sum(0, y_scaled[:, :, q_cols(0)], opens=True)
         form_a_term(0)
         turn_into_sum(0, a_term[0], opens=False)
         round_and_turn_back(0)
-        form_a_term(1)
-        score_quarter(2)
-        form_g(1)
-        weave_words(0)
         score_quarter(3)
-        early_quarter(1)
-        form_y_term(2)
-        early_quarter(0)
-        scatter_grad_half(0, 0, dw0[0][:])
-        form_a_term(2)
         form_y_term(3)
+        form_a_term(2)
         form_a_term(3)
+        score_quarter(1)
         form_g(2)
         form_g(3)
-        for q in (2, 3):
+        grad[0] = bank(6, "grad0")
+        early_quarter(2)
+        early_quarter(3)
+        scatter_grad_half(0, 1, dw0[1][:])
+        y_term[1] = keep.tile([P, PACK, QSLOTS], F32, name="y_term1", tag="g_il2", align_bytes=64)
+        a_term[1] = keep.tile([P, PACK, QSLOTS], F32, name="a_term1", tag="g_il3", align_bytes=64)
+        form_y_term(1)
+        form_a_term(1)
+        g_il[0] = keep.tile([P, QSLOTS, PACK], BF16, name="g_il0", tag="y_raw0", align_bytes=64)
+        weave_words(0)
+        form_g(1)
+        for q in (0, 1):
             quantise_g(q)
             grad_pass(0, q * QSLOTS, (q + 1) * QSLOTS)
         for t, number in ((1, 7), (2, 4), (3, 5)):
             grad[t] = bank(number, f"grad{t}")
             grad_pass(t, 0, SLOTS)
-        nc.vector.tensor_copy(dw0[1][:], grad[0][:, HSLOTS:SLOTS])
-        scatter_grad_half(0, 1, dw0[1][:])
+        nc.vector.tensor_copy(dw0[0][:], grad[0][:, 0:HSLOTS])
+        scatter_grad_half(0, 0, dw0[0][:])
         vector_mom(0)
         reused = keep.tile([P, SLOTS], F32, name="dw_stage", tag="m_g0")
-        ring = (reused[:, 0:HSLOTS], dw0[1][:], reused[:, HSLOTS:SLOTS])
+        ring = (reused[:, 0:HSLOTS], dw0[0][:], reused[:, HSLOTS:SLOTS])
         for t in range(1, PACK):
-            for h in range(2):
-                half = ring[(2 * (t - 1) + h) % len(ring)]
+            for k, h in enumerate((1, 0)):
+                half = ring[(2 * (t - 1) + k) % len(ring)]
                 nc.scalar.copy(half, grad[t][:, h * HSLOTS : (h + 1) * HSLOTS])
                 scatter_grad_half(t, h, half)
             vector_mom(t)

@@ -27,10 +27,8 @@ QUARTERS = 4
 QSLOTS = SLOTS // QUARTERS
 HSLOTS = SLOTS // 2
 OFFS_PER_COL = 16
-TURNED = tuple(range(1))
-DIRECT = tuple(range(1, QUARTERS))
-ORDER = (0, 2, 3, 1)
-DIRECT_LO = len(TURNED) * QSLOTS
+DIRECT = 1
+BY_SLOT = (0, 2, 3)
 RUN = 2
 
 
@@ -49,6 +47,9 @@ def tile_attend_gahead_nag_sq_kernel(tc, wT, mT, xT, y, ts, us, wt, fd, offs, ou
         def q_cols(q):
             return slice(q * QSLOTS, (q + 1) * QSLOTS)
 
+        def h_cols(h):
+            return slice(h * HSLOTS, (h + 1) * HSLOTS)
+
         def woven(tile):
             return tile.rearrange("p (c i) t -> p c t i", i=RUN)
 
@@ -57,13 +58,13 @@ def tile_attend_gahead_nag_sq_kernel(tc, wT, mT, xT, y, ts, us, wt, fd, offs, ou
 
         offsets = keep.tile([P, SLOTS // OFFS_PER_COL], U16, name="offsets")
 
-        def offs_of(lo, hi):
-            return offsets[:, lo // OFFS_PER_COL : hi // OFFS_PER_COL]
+        def offs_of(cols):
+            return offsets[:, cols.start // OFFS_PER_COL : cols.stop // OFFS_PER_COL]
 
         m_pair = [keep.tile([P, 2, TABLE], F32, name=f"m_pair{j}") for j in range(2)]
         w_win = [keep.tile([P, TABLE], F32, name=f"w_win{t}") for t in range(PACK)]
         x_raw = keep.tile([P, PACK, R], F32, name="x_raw", tag="x_raw")
-        y_raw = [keep.tile([P, PACK, HSLOTS], F32, name=f"y_raw{h}", tag=f"y_raw{h}", align_bytes=64) for h in range(2)]
+        y_raw = [keep.tile([P, PACK, HSLOTS], F32, name=f"y_raw{h}") for h in range(2)]
         ts_win = keep.tile([P, TABLE], F32, name="ts_win", tag="ts_win")
         us_c = keep.tile([P, PACK], F32, name="us_c")
         wt_c = keep.tile([P, PACK], F32, name="wt_c")
@@ -79,14 +80,16 @@ def tile_attend_gahead_nag_sq_kernel(tc, wT, mT, xT, y, ts, us, wt, fd, offs, ou
             nc.sync.dma_start(m_pair[j][:], by_plane(mT)[:, 2 * j : 2 * j + 2, :])
         for t in range(PACK):
             nc.sync.dma_start(w_win[t][:], by_plane(wT)[:, t, :])
-        for h in (1, 0):
-            nc.sync.dma_start(y_raw[h][:], by_plane(y)[:, :, h * HSLOTS : (h + 1) * HSLOTS])
+        for h in range(2):
+            nc.sync.dma_start(y_raw[h][:], by_plane(y)[:, :, h_cols(h)])
         nc.sync.dma_start(fd_c[:], by_plane(fd)[:, :, 0])
 
         grad_win = [keep.tile([P, TABLE], F32, name=f"grad_win{k}") for k in range(3)]
         mom_win = [keep.tile([P, TABLE], F32, name=f"mom_win{k}") for k in range(3)]
         ident = keep.tile([P, P], F32, name="ident")
         make_identity(nc, ident[:])
+        zeros = keep.tile([P, QSLOTS], F32, name="zeros")
+        nc.gpsimd.memset(zeros[:], 0.0)
         for k in range(2):
             nc.vector.memset(grad_win[k][:], 0.0)
             nc.vector.memset(mom_win[k][:], 0.0)
@@ -108,21 +111,16 @@ def tile_attend_gahead_nag_sq_kernel(tc, wT, mT, xT, y, ts, us, wt, fd, offs, ou
         a_row = keep.tile([P, PACK], F32, name="a_row")
         neg_fd2 = keep.tile([P, PACK], F32, name="neg_fd2")
 
-        m_g = [keep.tile([P, SLOTS], F32, name=f"m_g{t}", tag=f"m_g{t}") for t in range(PACK)]
+        m_g = [keep.tile([P, SLOTS], F32, name=f"m_g{t}") for t in range(PACK)]
         w2 = keep.tile([P, PACK, SLOTS], F32, name="w2")
 
         def gather_plane(t):
             nc.vector.tensor_copy(m_g[t][:], m_pair[t // 2][:, t % 2, :].indirect(offsets[:]))
-            width = QSLOTS if t == LAST else SLOTS
-            for lo in [q * QSLOTS for q in ORDER] if t == LAST else [0]:
-                nc.vector.tensor_tensor(
-                    w2[:, t, lo : lo + width], w_win[t][:].indirect(offs_of(lo, lo + width)), m_g[t][:, lo : lo + width], ADD
-                )
+            for cols in [q_cols(q) for q in range(QUARTERS)] if t == LAST else [slice(0, SLOTS)]:
+                nc.vector.tensor_tensor(w2[:, t, cols], w_win[t][:].indirect(offs_of(cols)), m_g[t][:, cols], ADD)
 
         nc.vector.tensor_tensor(y_row[:], wt_c[:], us_c[:], MULT)
         nc.vector.tensor_tensor(a_row[:], y_row[:], us_c[:], MULT)
-        neg_y_row = keep.tile([P, PACK], F32, name="neg_y_row")
-        nc.vector.tensor_scalar(neg_y_row[:], y_row[:], -1.0, 0.0, MULT, ADD)
         ts_g = keep.tile([P, SLOTS], F32, name="ts_g")
         nc.vector.tensor_copy(ts_g[:], ts_win[:].indirect(offsets[:]))
         mom_win.append(keep.tile([P, TABLE], F32, name="mom_win3", tag="ts_win"))
@@ -158,21 +156,27 @@ def tile_attend_gahead_nag_sq_kernel(tc, wT, mT, xT, y, ts, us, wt, fd, offs, ou
         )
 
         ts_turned = bank(6, "ts_turned")
-        for k, q in enumerate(TURNED):
+        for k, q in enumerate(BY_SLOT):
             nc.tensor.transpose(ts_turned[:, q_cols(k)], ts_g[:, q_cols(q)], ident[:])
-        ts_col = keep.tile([P, len(TURNED)], F32, name="ts_col")
-        nc.scalar.copy(ts_col[:], ts_turned[:, 0 : len(TURNED) * QSLOTS : QSLOTS])
+        ts_col = keep.tile([P, len(BY_SLOT)], F32, name="ts_col")
+        nc.scalar.copy(ts_col[:], ts_turned[:, 0 : len(BY_SLOT) * QSLOTS : QSLOTS])
 
-        ts_pow = keep.tile([P, SLOTS], F32, name="ts_pow")
-        a_fac = keep.tile([P, PACK, SLOTS], F32, name="a_fac")
-        y_fac = keep.tile([P, PACK, SLOTS - DIRECT_LO], F32, name="y_fac")
-        nc.scalar.copy(ts_pow[:, 0:DIRECT_LO], ts_g[:, 0:DIRECT_LO])
-        nc.scalar.activation(ts_pow[:, DIRECT_LO:SLOTS], ts_g[:, DIRECT_LO:SLOTS], SQUARE)
+        ts_sq = keep.tile([P, QSLOTS], F32, name="ts_sq")
+        a_fac = keep.tile([P, PACK, QSLOTS], F32, name="a_fac")
+        y_fac = keep.tile([P, PACK, SLOTS], F32, name="y_fac")
+        nc.scalar.activation(ts_sq[:], ts_g[:, q_cols(DIRECT)], SQUARE)
         for s in range(PACK):
-            nc.scalar.activation(y_fac[:, s, :], ts_g[:, DIRECT_LO:SLOTS], COPY, scale=y_row[:, s : s + 1])
-            nc.scalar.activation(a_fac[:, s, :], ts_pow[:], COPY, scale=a_row[:, s : s + 1])
+            nc.scalar.activation(y_fac[:, s, :], ts_g[:], COPY, scale=y_row[:, s : s + 1])
+            nc.scalar.activation(a_fac[:, s, :], ts_sq[:], COPY, scale=a_row[:, s : s + 1])
+
+        w2_il = [keep.tile([P, QSLOTS, PACK], BF16, name=f"w2_il{q}", align_bytes=64) for q in range(QUARTERS)]
+
+        def weave_w2(q, planes):
+            nc.scalar.copy(woven(w2_il[q][:, :, planes]), planar(w2[:, planes, q_cols(q)]))
 
         gather_plane(1)
+        for q in range(QUARTERS):
+            weave_w2(q, slice(0, 2))
 
         xd_codes = keep.tile([P, R], U32, name="xd_codes", align_bytes=64)
         xd_scales = keep.tile([P, R], U8, name="xd_scales", align_bytes=64)
@@ -187,162 +191,139 @@ def tile_attend_gahead_nag_sq_kernel(tc, wT, mT, xT, y, ts, us, wt, fd, offs, ou
         nc.gpsimd.tensor_tensor(fd2[:], fd_c[:], fd_c[:], MULT)
         nc.gpsimd.tensor_scalar(neg_fd2[:], fd2[:], -1.0, 0.0, MULT, ADD)
 
-        w2_il = [keep.tile([P, QSLOTS, PACK], BF16, name=f"w2_il{q}", align_bytes=64) for q in range(QUARTERS)]
         w2_codes = [keep.tile([P, QSLOTS], U32, name=f"w2_codes{q}", align_bytes=64) for q in range(QUARTERS)]
         w2_scales = [keep.tile([P, QSLOTS], U8, name=f"w2_scales{q}", align_bytes=64) for q in range(QUARTERS)]
-
-        def weave_w2(q):
-            nc.scalar.copy(woven(w2_il[q][:]), planar(w2[:, :, q_cols(q)]))
-
-        g_il = {q: keep.tile([P, QSLOTS, PACK], BF16, name=f"g_il{q}", tag=f"g_il{q}", align_bytes=64) for q in DIRECT}
+        g_il = [keep.tile([P, QSLOTS, PACK], BF16, name=f"g_il{q}", align_bytes=64) for q in range(QUARTERS)]
         g_codes = keep.tile([P, SLOTS], U32, name="g_codes", align_bytes=64)
         g_scales = keep.tile([P, SLOTS], U8, name="g_scales", align_bytes=64)
         scores = [bank(q, f"scores{q}") for q in range(QUARTERS)]
-        y_term = {q: keep.tile([P, PACK, QSLOTS], F32, name=f"y_term{q}") for q in (2, 3)}
-        y_scaled = keep.tile([P, PACK, DIRECT_LO], F32, name="y_scaled")
-        a_term = {q: keep.tile([P, PACK, QSLOTS], F32, name=f"a_term{q}") for q in (0, 2, 3)}
+
+        def y_of(q):
+            return y_raw[q // 2][:, :, q_cols(q % 2)]
 
         def score_quarter(q):
             nc.vector.quantize_mx(w2_codes[q][:].bitcast(E4M3), w2_scales[q][:], w2_il[q][:].rearrange("p n t -> p (n t)"))
-            for s in range(PACK):
-                rows = slice(s * P, (s + 1) * P)
+            w2_mx = (w2_codes[q][:].bitcast(E4M3), w2_scales[q][:])
+            if q == DIRECT:
+                for s in range(PACK):
+                    nc.tensor.matmul_mx(
+                        scores[q][:, q_cols(s)],
+                        lhsT=xd_codes[:, q_cols(s)].bitcast(E4M3),
+                        lhsT_scale=xd_scales[:, q_cols(s)],
+                        rhs=w2_mx[0],
+                        rhs_scale=w2_mx[1],
+                        start=True,
+                        stop=True,
+                    )
+            else:
                 nc.tensor.matmul_mx(
-                    scores[q][:, q_cols(s)],
-                    lhsT=xd_codes[:, rows].bitcast(E4M3),
-                    lhsT_scale=xd_scales[:, rows],
-                    rhs=w2_codes[q][:].bitcast(E4M3),
-                    rhs_scale=w2_scales[q][:],
+                    scores[q][:],
+                    lhsT=w2_mx[0],
+                    lhsT_scale=w2_mx[1],
+                    rhs=xd_codes[:].bitcast(E4M3),
+                    rhs_scale=xd_scales[:],
                     start=True,
                     stop=True,
                 )
 
-        def form_y_term(q):
-            nc.vector.tensor_tensor(y_term[q][:], y_raw[q // 2][:, :, q_cols(q % 2)], y_fac[:, :, q_cols(q - len(TURNED))], MULT)
+        turned = {}
 
-        def form_a_term(q):
-            nc.vector.tensor_tensor(a_term[q][:], scores[q][:].rearrange("p (s n) -> p s n", s=PACK), a_fac[:, :, q_cols(q)], MULT)
+        def scale_and_turn(q):
+            k = BY_SLOT.index(q)
+            scaled = keep.tile([P, R], F32, name=f"scaled{q}")
+            nc.scalar.activation(scaled[:], scores[q][:], COPY, scale=ts_col[:, k : k + 1])
+            turned[q] = bank(4 + k, f"turned{q}")
+            for s in range(PACK):
+                nc.tensor.transpose(turned[q][:, q_cols(s)], scaled[:, q_cols(s)], ident[:])
+
+        resid = {q: keep.tile([P, PACK, QSLOTS], F32, name=f"resid{q}") for q in BY_SLOT}
+
+        def form_resid(q):
+            for s in range(PACK):
+                nc.vector.scalar_tensor_tensor(
+                    resid[q][:, s, :], turned[q][:, q_cols(s)], us_c[:, s : s + 1], y_of(q)[:, s, :], MULT, SUB
+                )
 
         def form_g(q):
-            nc.vector.tensor_tensor(woven(g_il[q][:]), planar(a_term[q][:]), planar(y_term[q][:]), SUB)
+            nc.vector.tensor_tensor(woven(g_il[q][:]), planar(resid[q][:]), planar(y_fac[:, :, q_cols(q)]), MULT)
+
+        y_term = keep.tile([P, PACK, QSLOTS], F32, name="y_term")
+        a_term = keep.tile([P, PACK, QSLOTS], F32, name="a_term")
 
         def quantise_g(q):
             nc.vector.quantize_mx(g_codes[:, q_cols(q)].bitcast(E5M2), g_scales[:, q_cols(q)], g_il[q][:].rearrange("p n s -> p (n s)"))
 
-        def scale_y():
-            for s in range(PACK):
-                nc.scalar.activation(y_scaled[:, s, :], y_raw[0][:, s, 0:DIRECT_LO], COPY, scale=neg_y_row[:, s : s + 1])
-
-        summed = {q: bank(4 + q, f"summed{q}") for q in TURNED}
-
-        def turn_into_sum(q, term, opens):
-            for s in range(PACK):
-                nc.tensor.matmul(
-                    summed[q][:, q_cols(s)],
-                    term[:, s, :],
-                    ident[:],
-                    start=(opens and s == 0),
-                    stop=(not opens and s == PACK - 1),
-                    is_transpose=True,
-                )
-
-        g_words = {}
-
-        def round_and_turn_back(q):
-            g_turned = keep.tile([P, 2, P, 2], BF16, name=f"g_turned{q}")
-            nc.scalar.activation(
-                g_turned[:], summed[q][:].rearrange("i (u e p) -> i u p e", u=2, e=2), COPY, scale=ts_col[:, q : q + 1]
-            )
-            words = g_turned[:].rearrange("i u p e -> i (u p e)").bitcast(F32)
-            g_words[q] = bank(q, f"g_words{q}")
-            for u in range(2):
-                nc.tensor.transpose(g_words[q][:, q_cols(u)], words[:, q_cols(u)], ident[:])
-
-        def weave_words(q):
-            nc.vector.tensor_copy(
-                g_il[q][:].rearrange("p n s -> p (n s)").bitcast(F32).rearrange("p (n u) -> p n u", u=2),
-                g_words[q][:, 0:HSLOTS].rearrange("p (u n) -> p n u", u=2),
-            )
-
-        grad = {}
-
-        def grad_pass(t, lo, hi):
-            rows = slice(t * P, (t + 1) * P)
+        def grad_pass(out, t, cols):
             nc.tensor.matmul_mx(
-                grad[t][:, lo:hi],
-                lhsT=xr_codes[:, rows].bitcast(E4M3),
-                lhsT_scale=xr_scales[:, rows],
-                rhs=g_codes[:, lo:hi].bitcast(E5M2),
-                rhs_scale=g_scales[:, lo:hi],
+                out,
+                lhsT=xr_codes[:, q_cols(t)].bitcast(E4M3),
+                lhsT_scale=xr_scales[:, q_cols(t)],
+                rhs=g_codes[:, cols].bitcast(E5M2),
+                rhs_scale=g_scales[:, cols],
                 start=True,
                 stop=True,
             )
 
+        def scalar_half(t, h, staged, source):
+            nc.scalar.copy(staged, source)
+            nc.scalar.activation(grad_win[t][:].indirect(offs_of(h_cols(h))), staged, COPY)
 
-        def scalar_scatter(window, values, h):
-            nc.scalar.activation(window[:].indirect(offs_of(h * HSLOTS, (h + 1) * HSLOTS)), values, COPY)
-
-        def scatter_grad_half(t, h, half):
-            scalar_scatter(grad_win[t], half, h)
-            if h == 0:
-                nc.sync.dma_start(by_plane(out_1)[:, t, :], grad_win[t][:])
-
-        dw0 = [keep.tile([P, HSLOTS], F32, name=f"dw0_{h}") for h in range(2)]
-
-        def early_quarter(q):
-            quantise_g(q)
-            grad_pass(0, q * QSLOTS, (q + 1) * QSLOTS)
-            nc.scalar.copy(dw0[1][:, q_cols(q % 2)], grad[0][:, q_cols(q)])
-
-        def vector_mom(t):
-            nm = keep.tile([P, SLOTS], F32, name=f"nm{t}", tag=f"nm_stage{t % 2}")
-            nc.vector.scalar_tensor_tensor(nm[:], grad[t][:], neg_fd2[:, t : t + 1], m_g[t][:], MULT, ADD)
-            nc.vector.tensor_copy(mom_win[t][:].indirect(offsets[:]), nm[:])
-            nc.sync.dma_start(by_plane(out_0)[:, t, :], mom_win[t][:])
-
-        weave_w2(0)
-        weave_w2(2)
-        weave_w2(3)
-        scale_y()
-        weave_w2(1)
+        for q in range(QUARTERS):
+            weave_w2(q, slice(2, PACK))
         score_quarter(0)
-        form_y_term(2)
-        score_quarter(2)
-        turn_into_sum(0, y_scaled[:, :, q_cols(0)], opens=True)
-        form_a_term(0)
-        turn_into_sum(0, a_term[0], opens=False)
-        round_and_turn_back(0)
-        score_quarter(3)
-        form_y_term(3)
-        form_a_term(2)
-        form_a_term(3)
         score_quarter(1)
-        form_g(2)
-        form_g(3)
-        grad[0] = bank(6, "grad0")
-        early_quarter(2)
-        early_quarter(3)
-        scatter_grad_half(0, 1, dw0[1][:])
-        y_term[1] = keep.tile([P, PACK, QSLOTS], F32, name="y_term1", tag="g_il2", align_bytes=64)
-        a_term[1] = keep.tile([P, PACK, QSLOTS], F32, name="a_term1", tag="g_il3", align_bytes=64)
-        form_y_term(1)
-        form_a_term(1)
-        g_il[0] = keep.tile([P, QSLOTS, PACK], BF16, name="g_il0", tag="y_raw0", align_bytes=64)
-        weave_words(0)
-        form_g(1)
-        for q in (0, 1):
+        scale_and_turn(0)
+        score_quarter(2)
+        nc.vector.tensor_tensor(y_term[:], y_of(DIRECT), y_fac[:, :, q_cols(DIRECT)], MULT)
+        score_quarter(3)
+        scale_and_turn(2)
+        scale_and_turn(3)
+        nc.vector.tensor_tensor(a_term[:], scores[DIRECT][:].rearrange("p (s n) -> p s n", s=PACK), a_fac[:], MULT)
+        form_resid(0)
+        nc.vector.tensor_tensor(woven(g_il[DIRECT][:]), planar(a_term[:]), planar(y_term[:]), SUB)
+        form_g(0)
+        dw = [keep.tile([P, SLOTS], F32, name=f"dw{t}") for t in range(2)]
+        for q, number in ((1, 7), (0, 0)):
             quantise_g(q)
-            grad_pass(0, q * QSLOTS, (q + 1) * QSLOTS)
-        for t, number in ((1, 7), (2, 4), (3, 5)):
-            grad[t] = bank(number, f"grad{t}")
-            grad_pass(t, 0, SLOTS)
-        nc.vector.tensor_copy(dw0[0][:], grad[0][:, 0:HSLOTS])
-        scatter_grad_half(0, 0, dw0[0][:])
-        vector_mom(0)
-        reused = keep.tile([P, SLOTS], F32, name="dw_stage", tag="m_g0")
-        ring = (reused[:, 0:HSLOTS], dw0[0][:], reused[:, HSLOTS:SLOTS])
-        for t in range(1, PACK):
-            for k, h in enumerate((1, 0)):
-                half = ring[(2 * (t - 1) + k) % len(ring)]
-                nc.scalar.copy(half, grad[t][:, h * HSLOTS : (h + 1) * HSLOTS])
-                scatter_grad_half(t, h, half)
-            vector_mom(t)
+            early = bank(number, f"early{q}")
+            grad_pass(early[:, 0:QSLOTS], 0, q_cols(q))
+            nc.scalar.copy(dw[0][:, q_cols(q)], early[:, 0:QSLOTS])
+        nc.scalar.activation(grad_win[0][:].indirect(offs_of(h_cols(0))), dw[0][:, h_cols(0)], COPY)
+        early1 = bank(1, "early_plane1")
+        grad_pass(early1[:, 0:HSLOTS], 1, h_cols(0))
+        scalar_half(1, 0, dw[1][:, h_cols(0)], early1[:, 0:HSLOTS])
+
+        form_resid(2)
+        form_resid(3)
+        late = {}
+        for q, number in ((2, 4), (3, 5)):
+            form_g(q)
+            quantise_g(q)
+            late[q] = bank(number, f"late{q}")
+            grad_pass(late[q][:, 0:QSLOTS], 0, q_cols(q))
+        late1 = bank(6, "late1")
+        grad_pass(late1[:, 0:HSLOTS], 1, h_cols(1))
+        grad = {t: bank(t, f"grad{t}") for t in (2, 3)}
+        for t in (2, 3):
+            grad_pass(grad[t][:], t, slice(0, SLOTS))
+
+        for q in (2, 3):
+            nc.vector.tensor_copy(dw[0][:, q_cols(q)], late[q][:, 0:QSLOTS])
+            nc.vector.tensor_tensor(grad_win[0][:].indirect(offs_of(q_cols(q))), dw[0][:, q_cols(q)], zeros[:], ADD)
+        nc.sync.dma_start(by_plane(out_1)[:, 0, :], grad_win[0][:])
+        scalar_half(1, 1, dw[1][:, h_cols(1)], late1[:, 0:HSLOTS])
+        nc.scalar.dma_start(by_plane(out_1)[:, 1, :], grad_win[1][:])
+
+        ring = [keep.tile([P, HSLOTS], F32, name=f"ring{k}") for k in range(3)]
+        for t in range(PACK):
+            stage = keep.tile([P, SLOTS], F32, name=f"stage{t}", tag=f"stage{t % 2}")
+            if t < 2:
+                nc.vector.tensor_scalar(stage[:], dw[t][:], neg_fd2[:, t : t + 1], 0.0, MULT, ADD)
+                nc.vector.tensor_tensor(mom_win[t][:].indirect(offsets[:]), stage[:], m_g[t][:], ADD)
+            else:
+                for h in range(2):
+                    scalar_half(t, h, ring[(2 * t + h) % len(ring)][:], grad[t][:, h_cols(h)])
+                nc.scalar.dma_start(by_plane(out_1)[:, t, :], grad_win[t][:])
+                nc.vector.scalar_tensor_tensor(stage[:], grad[t][:], neg_fd2[:, t : t + 1], m_g[t][:], MULT, ADD)
+                nc.vector.tensor_copy(mom_win[t][:].indirect(offsets[:]), stage[:])
+            nc.sync.dma_start(by_plane(out_0)[:, t, :], mom_win[t][:])

@@ -111,7 +111,7 @@ def tile_attend_gahead_nag_sq_kernel(tc, wT, mT, xT, y, ts, us, wt, fd, offs, ou
         a_row = keep.tile([P, PACK], F32, name="a_row")
         neg_fd2 = keep.tile([P, PACK], F32, name="neg_fd2")
 
-        m_g = [keep.tile([P, SLOTS], F32, name=f"m_g{t}") for t in range(PACK)]
+        m_g = [keep.tile([P, SLOTS], F32, name=f"m_g{t}", tag=f"m_g{t}") for t in range(PACK)]
         w2 = keep.tile([P, PACK, SLOTS], F32, name="w2")
 
         def gather_plane(t):
@@ -314,16 +314,30 @@ def tile_attend_gahead_nag_sq_kernel(tc, wT, mT, xT, y, ts, us, wt, fd, offs, ou
         scalar_half(1, 1, dw[1][:, h_cols(1)], late1[:, 0:HSLOTS])
         nc.scalar.dma_start(by_plane(out_1)[:, 1, :], grad_win[1][:])
 
-        ring = [keep.tile([P, HSLOTS], F32, name=f"ring{k}") for k in range(3)]
-        for t in range(PACK):
-            stage = keep.tile([P, SLOTS], F32, name=f"stage{t}", tag=f"stage{t % 2}")
-            if t < 2:
-                nc.vector.tensor_scalar(stage[:], dw[t][:], neg_fd2[:, t : t + 1], 0.0, MULT, ADD)
-                nc.vector.tensor_tensor(mom_win[t][:].indirect(offsets[:]), stage[:], m_g[t][:], ADD)
-            else:
-                for h in range(2):
-                    scalar_half(t, h, ring[(2 * t + h) % len(ring)][:], grad[t][:, h_cols(h)])
-                nc.scalar.dma_start(by_plane(out_1)[:, t, :], grad_win[t][:])
-                nc.vector.scalar_tensor_tensor(stage[:], grad[t][:], neg_fd2[:, t : t + 1], m_g[t][:], MULT, ADD)
-                nc.vector.tensor_copy(mom_win[t][:].indirect(offsets[:]), stage[:])
-            nc.sync.dma_start(by_plane(out_0)[:, t, :], mom_win[t][:])
+        def store_mom(queue, t):
+            queue.dma_start(by_plane(out_0)[:, t, :], mom_win[t][:])
+
+        def mom_from_staged(t):
+            step = keep.tile([P, SLOTS], F32, name=f"step{t}", tag=f"stage{t}")
+            nc.vector.tensor_scalar(step[:], dw[t][:], neg_fd2[:, t : t + 1], 0.0, MULT, ADD)
+            nc.vector.tensor_tensor(mom_win[t][:].indirect(offsets[:]), step[:], m_g[t][:], ADD)
+            store_mom(nc.sync, t)
+
+        def mom_from_bank(t, tag):
+            nm = keep.tile([P, SLOTS], F32, name=f"nm{t}", tag=tag)
+            nc.vector.scalar_tensor_tensor(nm[:], grad[t][:], neg_fd2[:, t : t + 1], m_g[t][:], MULT, ADD)
+            return nm
+
+        for t, tags in ((2, ("ring0", "ring1")), (3, ("ring0", "ring2"))):
+            for h in range(2):
+                staged = keep.tile([P, HSLOTS], F32, name=f"staged{t}_{h}", tag=tags[h])
+                scalar_half(t, h, staged[:], grad[t][:, h_cols(h)])
+            nc.scalar.dma_start(by_plane(out_1)[:, t, :], grad_win[t][:])
+        mom_from_staged(0)
+        mom_from_staged(1)
+        nm_for_scalar = mom_from_bank(2, "ring1")
+        nc.vector.tensor_copy(mom_win[LAST][:].indirect(offsets[:]), mom_from_bank(LAST, "m_g2")[:])
+        store_mom(nc.sync, LAST)
+        for h in range(2):
+            nc.scalar.activation(mom_win[2][:].indirect(offs_of(h_cols(h))), nm_for_scalar[:, h_cols(h)], COPY)
+        store_mom(nc.scalar, 2)

@@ -27,8 +27,8 @@ QUARTERS = 4
 QSLOTS = SLOTS // QUARTERS
 HSLOTS = SLOTS // 2
 OFFS_PER_COL = 16
-DIRECT = 1
-BY_SLOT = (0, 2, 3)
+DIRECT = (0, 1)
+BY_SLOT = (2, 3)
 RUN = 2
 
 
@@ -116,7 +116,7 @@ def tile_attend_gahead_nag_sq_kernel(tc, wT, mT, xT, y, ts, us, wt, fd, offs, ou
 
         def gather_plane(t):
             nc.vector.tensor_copy(m_g[t][:], m_pair[t // 2][:, t % 2, :].indirect(offsets[:]))
-            for cols in [q_cols(q) for q in range(QUARTERS)] if t == LAST else [slice(0, SLOTS)]:
+            for cols in [q_cols(q) for q in DIRECT] if t == LAST else [slice(0, SLOTS)]:
                 nc.vector.tensor_tensor(w2[:, t, cols], w_win[t][:].indirect(offs_of(cols)), m_g[t][:, cols], ADD)
 
         nc.vector.tensor_tensor(y_row[:], wt_c[:], us_c[:], MULT)
@@ -161,10 +161,10 @@ def tile_attend_gahead_nag_sq_kernel(tc, wT, mT, xT, y, ts, us, wt, fd, offs, ou
         ts_col = keep.tile([P, len(BY_SLOT)], F32, name="ts_col")
         nc.scalar.copy(ts_col[:], ts_turned[:, 0 : len(BY_SLOT) * QSLOTS : QSLOTS])
 
-        ts_sq = keep.tile([P, QSLOTS], F32, name="ts_sq")
-        a_fac = keep.tile([P, PACK, QSLOTS], F32, name="a_fac")
+        ts_sq = keep.tile([P, HSLOTS], F32, name="ts_sq")
+        a_fac = keep.tile([P, PACK, HSLOTS], F32, name="a_fac")
         y_fac = keep.tile([P, PACK, SLOTS], F32, name="y_fac")
-        nc.scalar.activation(ts_sq[:], ts_g[:, q_cols(DIRECT)], SQUARE)
+        nc.scalar.activation(ts_sq[:], ts_g[:, h_cols(0)], SQUARE)
         for s in range(PACK):
             nc.scalar.activation(y_fac[:, s, :], ts_g[:], COPY, scale=y_row[:, s : s + 1])
             nc.scalar.activation(a_fac[:, s, :], ts_sq[:], COPY, scale=a_row[:, s : s + 1])
@@ -186,6 +186,9 @@ def tile_attend_gahead_nag_sq_kernel(tc, wT, mT, xT, y, ts, us, wt, fd, offs, ou
         nc.vector.quantize_mx(xr_codes[:].bitcast(E4M3), xr_scales[:], xr_il[:].rearrange("p d s -> p (d s)"))
         nc.vector.quantize_mx(xd_codes[:].bitcast(E4M3), xd_scales[:], xd_il[:].rearrange("p r t -> p (r t)"))
         gather_plane(LAST)
+        w_late = keep.tile([P, HSLOTS], F32, name="w_late")
+        nc.scalar.activation(w_late[:], w_win[LAST][:].indirect(offs_of(h_cols(1))), COPY)
+        nc.vector.tensor_tensor(w2[:, LAST, h_cols(1)], w_late[:], m_g[LAST][:, h_cols(1)], ADD)
 
         fd2 = keep.tile([P, PACK], F32, name="fd2")
         nc.gpsimd.tensor_tensor(fd2[:], fd_c[:], fd_c[:], MULT)
@@ -204,7 +207,7 @@ def tile_attend_gahead_nag_sq_kernel(tc, wT, mT, xT, y, ts, us, wt, fd, offs, ou
         def score_quarter(q):
             nc.vector.quantize_mx(w2_codes[q][:].bitcast(E4M3), w2_scales[q][:], w2_il[q][:].rearrange("p n t -> p (n t)"))
             w2_mx = (w2_codes[q][:].bitcast(E4M3), w2_scales[q][:])
-            if q == DIRECT:
+            if q in DIRECT:
                 for s in range(PACK):
                     nc.tensor.matmul_mx(
                         scores[q][:, q_cols(s)],
@@ -247,8 +250,17 @@ def tile_attend_gahead_nag_sq_kernel(tc, wT, mT, xT, y, ts, us, wt, fd, offs, ou
         def form_g(q):
             nc.vector.tensor_tensor(woven(g_il[q][:]), planar(resid[q][:]), planar(y_fac[:, :, q_cols(q)]), MULT)
 
-        y_term = keep.tile([P, PACK, QSLOTS], F32, name="y_term")
-        a_term = keep.tile([P, PACK, QSLOTS], F32, name="a_term")
+        y_term = {q: keep.tile([P, PACK, QSLOTS], F32, name=f"y_term{q}") for q in DIRECT}
+        a_term = {q: keep.tile([P, PACK, QSLOTS], F32, name=f"a_term{q}") for q in DIRECT}
+
+        def form_y_term(q):
+            nc.vector.tensor_tensor(y_term[q][:], y_of(q), y_fac[:, :, q_cols(q)], MULT)
+
+        def form_a_term(q):
+            nc.vector.tensor_tensor(a_term[q][:], scores[q][:].rearrange("p (s n) -> p s n", s=PACK), a_fac[:, :, q_cols(q)], MULT)
+
+        def form_direct_g(q):
+            nc.vector.tensor_tensor(woven(g_il[q][:]), planar(a_term[q][:]), planar(y_term[q][:]), SUB)
 
         def quantise_g(q):
             nc.vector.quantize_mx(g_codes[:, q_cols(q)].bitcast(E5M2), g_scales[:, q_cols(q)], g_il[q][:].rearrange("p n s -> p (n s)"))
@@ -272,36 +284,36 @@ def tile_attend_gahead_nag_sq_kernel(tc, wT, mT, xT, y, ts, us, wt, fd, offs, ou
             weave_w2(q, slice(2, PACK))
         score_quarter(0)
         score_quarter(1)
-        scale_and_turn(0)
-        score_quarter(2)
-        nc.vector.tensor_tensor(y_term[:], y_of(DIRECT), y_fac[:, :, q_cols(DIRECT)], MULT)
-        score_quarter(3)
-        scale_and_turn(2)
-        scale_and_turn(3)
-        nc.vector.tensor_tensor(a_term[:], scores[DIRECT][:].rearrange("p (s n) -> p s n", s=PACK), a_fac[:], MULT)
-        form_resid(0)
-        nc.vector.tensor_tensor(woven(g_il[DIRECT][:]), planar(a_term[:]), planar(y_term[:]), SUB)
-        form_g(0)
+        form_y_term(0)
+        for q in BY_SLOT:
+            score_quarter(q)
+        for q in BY_SLOT:
+            scale_and_turn(q)
+        form_a_term(0)
+        form_y_term(1)
+        form_a_term(1)
+        for q in DIRECT:
+            form_direct_g(q)
         dw = [keep.tile([P, SLOTS], F32, name=f"dw{t}") for t in range(2)]
-        for q, number in ((1, 7), (0, 0)):
+        for q, number in ((0, 7), (1, 6)):
             quantise_g(q)
             early = bank(number, f"early{q}")
             grad_pass(early[:, 0:QSLOTS], 0, q_cols(q))
             nc.scalar.copy(dw[0][:, q_cols(q)], early[:, 0:QSLOTS])
         nc.scalar.activation(grad_win[0][:].indirect(offs_of(h_cols(0))), dw[0][:, h_cols(0)], COPY)
-        early1 = bank(1, "early_plane1")
+        early1 = bank(0, "early_plane1")
         grad_pass(early1[:, 0:HSLOTS], 1, h_cols(0))
         scalar_half(1, 0, dw[1][:, h_cols(0)], early1[:, 0:HSLOTS])
 
         form_resid(2)
         form_resid(3)
         late = {}
-        for q, number in ((2, 4), (3, 5)):
+        for q, number in ((2, 1), (3, 4)):
             form_g(q)
             quantise_g(q)
             late[q] = bank(number, f"late{q}")
             grad_pass(late[q][:, 0:QSLOTS], 0, q_cols(q))
-        late1 = bank(6, "late1")
+        late1 = bank(5, "late1")
         grad_pass(late1[:, 0:HSLOTS], 1, h_cols(1))
         grad = {t: bank(t, f"grad{t}") for t in (2, 3)}
         for t in (2, 3):

@@ -64,7 +64,7 @@ def tile_attend_gahead_nag_sq_kernel(tc, wT, mT, xT, y, ts, us, wt, fd, offs, ou
         m_pair = [keep.tile([P, 2, TABLE], F32, name=f"m_pair{j}") for j in range(2)]
         w_win = [keep.tile([P, TABLE], F32, name=f"w_win{t}") for t in range(PACK)]
         x_raw = keep.tile([P, PACK, R], F32, name="x_raw", tag="x_raw")
-        y_raw = [keep.tile([P, PACK, HSLOTS], F32, name=f"y_raw{h}") for h in range(2)]
+        y_raw = [keep.tile([P, PACK, QSLOTS], F32, name=f"y_raw{q}") for q in range(QUARTERS)]
         ts_win = keep.tile([P, TABLE], F32, name="ts_win", tag="ts_win")
         us_c = keep.tile([P, PACK], F32, name="us_c")
         wt_c = keep.tile([P, PACK], F32, name="wt_c")
@@ -80,15 +80,15 @@ def tile_attend_gahead_nag_sq_kernel(tc, wT, mT, xT, y, ts, us, wt, fd, offs, ou
             nc.sync.dma_start(m_pair[j][:], by_plane(mT)[:, 2 * j : 2 * j + 2, :])
         for t in range(PACK):
             nc.sync.dma_start(w_win[t][:], by_plane(wT)[:, t, :])
-        for h in range(2):
-            nc.sync.dma_start(y_raw[h][:], by_plane(y)[:, :, h_cols(h)])
+        for q in range(QUARTERS):
+            nc.sync.dma_start(y_raw[q][:], by_plane(y)[:, :, q_cols(q)])
         nc.sync.dma_start(fd_c[:], by_plane(fd)[:, :, 0])
 
         grad_win = [keep.tile([P, TABLE], F32, name=f"grad_win{k}") for k in range(3)]
         mom_win = [keep.tile([P, TABLE], F32, name=f"mom_win{k}") for k in range(3)]
         ident = keep.tile([P, P], F32, name="ident")
         make_identity(nc, ident[:])
-        zeros = keep.tile([P, QSLOTS], F32, name="zeros")
+        zeros = keep.tile([P, QSLOTS], F32, name="zeros", tag="stage1")
         nc.gpsimd.memset(zeros[:], 0.0)
         for k in range(2):
             nc.vector.memset(grad_win[k][:], 0.0)
@@ -196,13 +196,13 @@ def tile_attend_gahead_nag_sq_kernel(tc, wT, mT, xT, y, ts, us, wt, fd, offs, ou
 
         w2_codes = [keep.tile([P, QSLOTS], U32, name=f"w2_codes{q}", align_bytes=64) for q in range(QUARTERS)]
         w2_scales = [keep.tile([P, QSLOTS], U8, name=f"w2_scales{q}", align_bytes=64) for q in range(QUARTERS)]
-        g_il = [keep.tile([P, QSLOTS, PACK], BF16, name=f"g_il{q}", align_bytes=64) for q in range(QUARTERS)]
+        g_il = [keep.tile([P, QSLOTS, PACK], BF16, name=f"g_il{q}", tag=f"g_il{q}", align_bytes=64) for q in range(QUARTERS)]
         g_codes = keep.tile([P, SLOTS], U32, name="g_codes", align_bytes=64)
         g_scales = keep.tile([P, SLOTS], U8, name="g_scales", align_bytes=64)
         scores = [bank(q, f"scores{q}") for q in range(QUARTERS)]
 
         def y_of(q):
-            return y_raw[q // 2][:, :, q_cols(q % 2)]
+            return y_raw[q][:]
 
         def score_quarter(q):
             nc.vector.quantize_mx(w2_codes[q][:].bitcast(E4M3), w2_scales[q][:], w2_il[q][:].rearrange("p n t -> p (n t)"))
@@ -239,9 +239,10 @@ def tile_attend_gahead_nag_sq_kernel(tc, wT, mT, xT, y, ts, us, wt, fd, offs, ou
             for s in range(PACK):
                 nc.tensor.transpose(turned[q][:, q_cols(s)], scaled[:, q_cols(s)], ident[:])
 
-        resid = {q: keep.tile([P, PACK, QSLOTS], F32, name=f"resid{q}") for q in BY_SLOT}
+        resid = {}
 
-        def form_resid(q):
+        def form_resid(q, tag):
+            resid[q] = keep.tile([P, PACK, QSLOTS], F32, name=f"resid{q}", tag=tag, align_bytes=64)
             for s in range(PACK):
                 nc.vector.scalar_tensor_tensor(
                     resid[q][:, s, :], turned[q][:, q_cols(s)], us_c[:, s : s + 1], y_of(q)[:, s, :], MULT, SUB
@@ -250,17 +251,17 @@ def tile_attend_gahead_nag_sq_kernel(tc, wT, mT, xT, y, ts, us, wt, fd, offs, ou
         def form_g(q):
             nc.vector.tensor_tensor(woven(g_il[q][:]), planar(resid[q][:]), planar(y_fac[:, :, q_cols(q)]), MULT)
 
-        y_term = {q: keep.tile([P, PACK, QSLOTS], F32, name=f"y_term{q}") for q in DIRECT}
-        a_term = {q: keep.tile([P, PACK, QSLOTS], F32, name=f"a_term{q}") for q in DIRECT}
+        y_term = {q: w2[:, :, q_cols(q)] for q in DIRECT}
+        a_term = {q: keep.tile([P, PACK, QSLOTS], F32, name=f"a_term{q}", tag=f"a_term{q}", align_bytes=64) for q in DIRECT}
 
         def form_y_term(q):
-            nc.vector.tensor_tensor(y_term[q][:], y_of(q), y_fac[:, :, q_cols(q)], MULT)
+            nc.vector.tensor_tensor(y_term[q], y_of(q), y_fac[:, :, q_cols(q)], MULT)
 
         def form_a_term(q):
             nc.vector.tensor_tensor(a_term[q][:], scores[q][:].rearrange("p (s n) -> p s n", s=PACK), a_fac[:, :, q_cols(q)], MULT)
 
         def form_direct_g(q):
-            nc.vector.tensor_tensor(woven(g_il[q][:]), planar(a_term[q][:]), planar(y_term[q][:]), SUB)
+            nc.vector.tensor_tensor(woven(g_il[q][:]), planar(a_term[q][:]), planar(y_term[q]), SUB)
 
         def quantise_g(q):
             nc.vector.quantize_mx(g_codes[:, q_cols(q)].bitcast(E5M2), g_scales[:, q_cols(q)], g_il[q][:].rearrange("p n s -> p (n s)"))
@@ -294,21 +295,21 @@ def tile_attend_gahead_nag_sq_kernel(tc, wT, mT, xT, y, ts, us, wt, fd, offs, ou
         form_a_term(1)
         for q in DIRECT:
             form_direct_g(q)
-        dw = [keep.tile([P, SLOTS], F32, name=f"dw{t}") for t in range(2)]
+        dw = [keep.tile([P, SLOTS], F32, name=f"dw{t}", tag=f"dw{t}") for t in range(2)]
         for q, number in ((0, 7), (1, 6)):
             quantise_g(q)
             early = bank(number, f"early{q}")
             grad_pass(early[:, 0:QSLOTS], 0, q_cols(q))
             nc.scalar.copy(dw[0][:, q_cols(q)], early[:, 0:QSLOTS])
-        nc.scalar.activation(grad_win[0][:].indirect(offs_of(h_cols(0))), dw[0][:, h_cols(0)], COPY)
         early1 = bank(0, "early_plane1")
         grad_pass(early1[:, 0:HSLOTS], 1, h_cols(0))
-        scalar_half(1, 0, dw[1][:, h_cols(0)], early1[:, 0:HSLOTS])
+        nc.scalar.copy(dw[1][:, h_cols(0)], early1[:, 0:HSLOTS])
+        for t in range(2):
+            nc.scalar.activation(grad_win[t][:].indirect(offs_of(h_cols(0))), dw[t][:, h_cols(0)], COPY)
 
-        form_resid(2)
-        form_resid(3)
         late = {}
-        for q, number in ((2, 1), (3, 4)):
+        for q, number, tag in ((2, 1, "a_term1"), (3, 4, "g_il1")):
+            form_resid(q, tag)
             form_g(q)
             quantise_g(q)
             late[q] = bank(number, f"late{q}")
@@ -324,7 +325,7 @@ def tile_attend_gahead_nag_sq_kernel(tc, wT, mT, xT, y, ts, us, wt, fd, offs, ou
             nc.vector.tensor_tensor(grad_win[0][:].indirect(offs_of(q_cols(q))), dw[0][:, q_cols(q)], zeros[:], ADD)
         nc.sync.dma_start(by_plane(out_1)[:, 0, :], grad_win[0][:])
         scalar_half(1, 1, dw[1][:, h_cols(1)], late1[:, 0:HSLOTS])
-        nc.scalar.dma_start(by_plane(out_1)[:, 1, :], grad_win[1][:])
+        nc.sync.dma_start(by_plane(out_1)[:, 1, :], grad_win[1][:])
 
         def store_mom(queue, t):
             queue.dma_start(by_plane(out_0)[:, t, :], mom_win[t][:])
@@ -333,23 +334,28 @@ def tile_attend_gahead_nag_sq_kernel(tc, wT, mT, xT, y, ts, us, wt, fd, offs, ou
             step = keep.tile([P, SLOTS], F32, name=f"step{t}", tag=f"stage{t}")
             nc.vector.tensor_scalar(step[:], dw[t][:], neg_fd2[:, t : t + 1], 0.0, MULT, ADD)
             nc.vector.tensor_tensor(mom_win[t][:].indirect(offsets[:]), step[:], m_g[t][:], ADD)
-            store_mom(nc.sync, t)
 
         def mom_from_bank(t, tag):
             nm = keep.tile([P, SLOTS], F32, name=f"nm{t}", tag=tag)
             nc.vector.scalar_tensor_tensor(nm[:], grad[t][:], neg_fd2[:, t : t + 1], m_g[t][:], MULT, ADD)
             return nm
 
-        for t, tags in ((2, ("ring0", "ring1")), (3, ("ring0", "ring2"))):
+        def grad_plane(t, tags):
             for h in range(2):
                 staged = keep.tile([P, HSLOTS], F32, name=f"staged{t}_{h}", tag=tags[h])
                 scalar_half(t, h, staged[:], grad[t][:, h_cols(h)])
-            nc.scalar.dma_start(by_plane(out_1)[:, t, :], grad_win[t][:])
+
         mom_from_staged(0)
+        store_mom(nc.sync, 0)
         mom_from_staged(1)
-        nm_for_scalar = mom_from_bank(2, "ring1")
+        grad_plane(2, ("ring", "dw1"))
+        nc.sync.dma_start(by_plane(out_1)[:, 2, :], grad_win[2][:])
+        store_mom(nc.sync, 1)
+        grad_plane(3, ("ring", "dw0"))
+        nc.sync.dma_start(by_plane(out_1)[:, 3, :], grad_win[3][:])
+        nm_for_scalar = mom_from_bank(2, "dw1")
         nc.vector.tensor_copy(mom_win[LAST][:].indirect(offsets[:]), mom_from_bank(LAST, "m_g2")[:])
         store_mom(nc.sync, LAST)
         for h in range(2):
             nc.scalar.activation(mom_win[2][:].indirect(offs_of(h_cols(h))), nm_for_scalar[:, h_cols(h)], COPY)
-        store_mom(nc.scalar, 2)
+        store_mom(nc.sync, 2)

@@ -116,7 +116,7 @@ def tile_attend_gahead_nag_sq_kernel(tc, wT, mT, xT, y, ts, us, wt, fd, offs, ou
 
         def gather_plane(t):
             nc.vector.tensor_copy(m_g[t][:], m_pair[t // 2][:, t % 2, :].indirect(offsets[:]))
-            for cols in [q_cols(q) for q in DIRECT] if t == LAST else [slice(0, SLOTS)]:
+            for cols in [q_cols(q) for q in range(QUARTERS - 1)] if t == LAST else [slice(0, SLOTS)]:
                 nc.vector.tensor_tensor(w2[:, t, cols], w_win[t][:].indirect(offs_of(cols)), m_g[t][:, cols], ADD)
 
         nc.vector.tensor_tensor(y_row[:], wt_c[:], us_c[:], MULT)
@@ -186,9 +186,9 @@ def tile_attend_gahead_nag_sq_kernel(tc, wT, mT, xT, y, ts, us, wt, fd, offs, ou
         nc.vector.quantize_mx(xr_codes[:].bitcast(E4M3), xr_scales[:], xr_il[:].rearrange("p d s -> p (d s)"))
         nc.vector.quantize_mx(xd_codes[:].bitcast(E4M3), xd_scales[:], xd_il[:].rearrange("p r t -> p (r t)"))
         gather_plane(LAST)
-        w_late = keep.tile([P, HSLOTS], F32, name="w_late")
-        nc.scalar.activation(w_late[:], w_win[LAST][:].indirect(offs_of(h_cols(1))), COPY)
-        nc.vector.tensor_tensor(w2[:, LAST, h_cols(1)], w_late[:], m_g[LAST][:, h_cols(1)], ADD)
+        w_late = keep.tile([P, QSLOTS], F32, name="w_late")
+        nc.scalar.activation(w_late[:], w_win[LAST][:].indirect(offs_of(q_cols(3))), COPY)
+        nc.vector.tensor_tensor(w2[:, LAST, q_cols(3)], w_late[:], m_g[LAST][:, q_cols(3)], ADD)
 
         fd2 = keep.tile([P, PACK], F32, name="fd2")
         nc.gpsimd.tensor_tensor(fd2[:], fd_c[:], fd_c[:], MULT)

@@ -191,8 +191,8 @@ def tile_attend_gahead_nag_sq_kernel(tc, wT, mT, xT, y, ts, us, wt, fd, offs, ou
         nc.vector.tensor_tensor(w2[:, LAST, q_cols(3)], w_late[:], m_g[LAST][:, q_cols(3)], ADD)
 
         fd2 = keep.tile([P, PACK], F32, name="fd2")
-        nc.gpsimd.tensor_tensor(fd2[:], fd_c[:], fd_c[:], MULT)
-        nc.gpsimd.tensor_scalar(neg_fd2[:], fd2[:], -1.0, 0.0, MULT, ADD)
+        nc.scalar.activation(fd2[:], fd_c[:], SQUARE)
+        nc.scalar.activation(neg_fd2[:], fd2[:], COPY, scale=-1.0)
 
         w2_codes = [keep.tile([P, QSLOTS], U32, name=f"w2_codes{q}", align_bytes=64) for q in range(QUARTERS)]
         w2_scales = [keep.tile([P, QSLOTS], U8, name=f"w2_scales{q}", align_bytes=64) for q in range(QUARTERS)]
@@ -286,13 +286,13 @@ def tile_attend_gahead_nag_sq_kernel(tc, wT, mT, xT, y, ts, us, wt, fd, offs, ou
         score_quarter(0)
         score_quarter(1)
         form_y_term(0)
-        for q in BY_SLOT:
-            score_quarter(q)
+        score_quarter(2)
+        form_y_term(1)
+        score_quarter(3)
         for q in BY_SLOT:
             scale_and_turn(q)
-        form_a_term(0)
-        form_y_term(1)
-        form_a_term(1)
+        for q in DIRECT:
+            form_a_term(q)
         for q in DIRECT:
             form_direct_g(q)
         dw = [keep.tile([P, SLOTS], F32, name=f"dw{t}", tag=f"dw{t}") for t in range(2)]

from contextlib import ExitStack

import concourse.mybir as mybir
from concourse.masks import make_identity

D, R, SLOTS, TABLE = 512, 512, 512, 2048
FLOPS = 2 * 2 * D * R * SLOTS

F32 = mybir.dt.float32
BF16 = mybir.dt.bfloat16
U32 = mybir.dt.uint32
U16 = mybir.dt.uint16
U8 = mybir.dt.uint8
E4M3 = mybir.dt.float8_e4m3fn_x4
E5M2 = mybir.dt.float8_e5m2_x4
MULT = mybir.AluOpType.mult
ADD = mybir.AluOpType.add
SUB = mybir.AluOpType.subtract
COPY = mybir.ActivationFunctionType.Copy
SQUARE = mybir.ActivationFunctionType.Square

P = 128
PACK = 4
LAST = PACK - 1
BANK = 512
QUARTERS = 4
QSLOTS = SLOTS // QUARTERS
HSLOTS = SLOTS // 2
OFFS_PER_COL = 16
DIRECT = (0, 1)
BY_SLOT = (2, 3)
RUN = 2


def tile_attend_gahead_nag_sq_kernel(tc, wT, mT, xT, y, ts, us, wt, fd, offs, out_0, out_1):
    nc = tc.nc
    with ExitStack() as ctx:
        keep = ctx.enter_context(tc.tile_pool(name="keep", bufs=1))
        psum = ctx.enter_context(tc.psum_pool(name="psum", bufs=1))

        def by_plane(ap):
            return ap.rearrange("(p t) c -> p t c", t=PACK)

        def bank(number, name):
            return psum.tile([P, BANK], F32, name=name, tag=f"bank{number}")

        def q_cols(q):
            return slice(q * QSLOTS, (q + 1) * QSLOTS)

        def h_cols(h):
            return slice(h * HSLOTS, (h + 1) * HSLOTS)

        def woven(tile):
            return tile.rearrange("p (c i) t -> p c t i", i=RUN)

        def planar(tile):
            return tile.rearrange("p t (c i) -> p c t i", i=RUN)

        offsets = keep.tile([P, SLOTS // OFFS_PER_COL], U16, name="offsets")

        def offs_of(cols):
            return offsets[:, cols.start // OFFS_PER_COL : cols.stop // OFFS_PER_COL]

        m_pair = [keep.tile([P, 2, TABLE], F32, name=f"m_pair{j}") for j in range(2)]
        w_win = [keep.tile([P, TABLE], F32, name=f"w_win{t}") for t in range(PACK)]
        x_raw = keep.tile([P, PACK, R], F32, name="x_raw", tag="x_raw")
        y_raw = [keep.tile([P, PACK, QSLOTS], F32, name=f"y_raw{q}") for q in range(QUARTERS)]
        ts_win = keep.tile([P, TABLE], F32, name="ts_win", tag="ts_win")
        us_c = keep.tile([P, PACK], F32, name="us_c")
        wt_c = keep.tile([P, PACK], F32, name="wt_c")
        fd_c = keep.tile([P, PACK], F32, name="fd_c")

        ts_row = keep.tile([P, TABLE // P], F32, name="ts_row")
        nc.scalar.dma_start(ts_row[:], ts[0:1, :].rearrange("o (p j) -> p (o j)", p=P))
        nc.sync.dma_start(x_raw[:], by_plane(xT))
        nc.sync.dma_start(offsets[:], offs)
        nc.scalar.dma_start(us_c[:], by_plane(us)[:, :, 0])
        nc.scalar.dma_start(wt_c[:], by_plane(wt)[:, :, 0])
        for j in range(2):
            nc.sync.dma_start(m_pair[j][:], by_plane(mT)[:, 2 * j : 2 * j + 2, :])
        for t in range(PACK):
            nc.sync.dma_start(w_win[t][:], by_plane(wT)[:, t, :])
        for q in range(QUARTERS):
            nc.sync.dma_start(y_raw[q][:], by_plane(y)[:, :, q_cols(q)])
        nc.sync.dma_start(fd_c[:], by_plane(fd)[:, :, 0])

        grad_win = [keep.tile([P, TABLE], F32, name=f"grad_win{k}") for k in range(3)]
        mom_win = [keep.tile([P, TABLE], F32, name=f"mom_win{k}") for k in range(3)]
        ident = keep.tile([P, P], F32, name="ident")
        make_identity(nc, ident[:])
        zeros = keep.tile([P, QSLOTS], F32, name="zeros", tag="stage1")
        nc.gpsimd.memset(zeros[:], 0.0)
        for k in range(2):
            nc.vector.memset(grad_win[k][:], 0.0)
            nc.vector.memset(mom_win[k][:], 0.0)
        nc.gpsimd.memset(grad_win[2][:], 0.0)
        nc.gpsimd.memset(mom_win[2][:], 0.0)

        for b in range(4):
            spread = bank(b, f"ts_spread{b}")
            for k in range(4):
                j = 4 * b + k
                nc.tensor.transpose(spread[:, k * P : (k + 1) * P], ts_row[:, j : j + 1].to_broadcast([P, P]), ident[:])
            nc.scalar.activation(
                ts_win[:].rearrange("p (n b k) -> p n b k", b=4, k=4)[:, :, b, :],
                spread[:].rearrange("p (k n) -> p n k", k=4),
                COPY,
            )

        y_row = keep.tile([P, PACK], F32, name="y_row")
        a_row = keep.tile([P, PACK], F32, name="a_row")
        neg_fd2 = keep.tile([P, PACK], F32, name="neg_fd2")

        m_g = [keep.tile([P, SLOTS], F32, name=f"m_g{t}", tag=f"m_g{t}") for t in range(PACK)]
        w2 = keep.tile([P, PACK, SLOTS], F32, name="w2")

        def gather_plane(t):
            nc.vector.tensor_copy(m_g[t][:], m_pair[t // 2][:, t % 2, :].indirect(offsets[:]))
            for cols in [q_cols(q) for q in range(QUARTERS - 1)] if t == LAST else [slice(0, SLOTS)]:
                nc.vector.tensor_tensor(w2[:, t, cols], w_win[t][:].indirect(offs_of(cols)), m_g[t][:, cols], ADD)

        nc.vector.tensor_tensor(y_row[:], wt_c[:], us_c[:], MULT)
        nc.vector.tensor_tensor(a_row[:], y_row[:], us_c[:], MULT)
        ts_g = keep.tile([P, SLOTS], F32, name="ts_g")
        nc.vector.tensor_copy(ts_g[:], ts_win[:].indirect(offsets[:]))
        mom_win.append(keep.tile([P, TABLE], F32, name="mom_win3", tag="ts_win"))
        nc.gpsimd.memset(mom_win[LAST][:], 0.0)
        gather_plane(0)

        x_bf = keep.tile([P, PACK, R], BF16, name="x_bf", align_bytes=64)
        nc.scalar.copy(x_bf[:], x_raw[:])
        grad_win.append(keep.tile([P, TABLE], F32, name="grad_win3", tag="x_raw"))
        nc.gpsimd.memset(grad_win[LAST][:], 0.0)
        x_words = x_bf[:].rearrange("p t r -> p (t r)").bitcast(F32)
        xr_il = keep.tile([P, D, PACK], BF16, name="xr_il", align_bytes=64)
        xr_words = xr_il[:].rearrange("p d s -> p (d s)").bitcast(F32)
        words_per_plane = R // 2
        for b in range(2):
            x_turned = bank(4 + b, f"x_turned{b}")
            for k in range(2):
                t = 2 * b + k
                for u in range(2):
                    nc.tensor.transpose(
                        x_turned[:, (2 * k + u) * P : (2 * k + u + 1) * P],
                        x_words[:, t * words_per_plane + u : (t + 1) * words_per_plane : 2],
                        ident[:],
                    )
            nc.scalar.copy(
                xr_words[:, b * BANK : (b + 1) * BANK].rearrange("p (k d u) -> p k d u", k=2, u=2),
                x_turned[:].rearrange("p (k u d) -> p k d u", k=2, u=2),
            )
        xd_il = keep.tile([P, R, PACK], BF16, name="xd_il", align_bytes=64)
        nc.scalar.copy(
            xd_il[:].rearrange("p (s r) t -> p s r t", s=PACK),
            x_bf[:].rearrange("p t (r s) -> p s r t", s=PACK),
        )

        ts_turned = bank(6, "ts_turned")
        for k, q in enumerate(BY_SLOT):
            nc.tensor.transpose(ts_turned[:, q_cols(k)], ts_g[:, q_cols(q)], ident[:])
        ts_col = keep.tile([P, len(BY_SLOT)], F32, name="ts_col")
        nc.scalar.copy(ts_col[:], ts_turned[:, 0 : len(BY_SLOT) * QSLOTS : QSLOTS])

        ts_sq = keep.tile([P, HSLOTS], F32, name="ts_sq")
        a_fac = keep.tile([P, PACK, HSLOTS], F32, name="a_fac")
        y_fac = keep.tile([P, PACK, SLOTS], F32, name="y_fac")
        nc.scalar.activation(ts_sq[:], ts_g[:, h_cols(0)], SQUARE)
        for s in range(PACK):
            nc.scalar.activation(y_fac[:, s, :], ts_g[:], COPY, scale=y_row[:, s : s + 1])
            nc.scalar.activation(a_fac[:, s, :], ts_sq[:], COPY, scale=a_row[:, s : s + 1])

        w2_il = [keep.tile([P, QSLOTS, PACK], BF16, name=f"w2_il{q}", align_bytes=64) for q in range(QUARTERS)]

        def weave_w2(q, planes):
            nc.scalar.copy(woven(w2_il[q][:, :, planes]), planar(w2[:, planes, q_cols(q)]))

        gather_plane(1)
        for q in range(QUARTERS):
            weave_w2(q, slice(0, 2))

        xd_codes = keep.tile([P, R], U32, name="xd_codes", align_bytes=64)
        xd_scales = keep.tile([P, R], U8, name="xd_scales", align_bytes=64)
        xr_codes = keep.tile([P, D], U32, name="xr_codes", align_bytes=64)
        xr_scales = keep.tile([P, D], U8, name="xr_scales", align_bytes=64)
        gather_plane(2)
        nc.vector.quantize_mx(xr_codes[:].bitcast(E4M3), xr_scales[:], xr_il[:].rearrange("p d s -> p (d s)"))
        nc.vector.quantize_mx(xd_codes[:].bitcast(E4M3), xd_scales[:], xd_il[:].rearrange("p r t -> p (r t)"))
        gather_plane(LAST)
        w_late = keep.tile([P, QSLOTS], F32, name="w_late")
        nc.scalar.activation(w_late[:], w_win[LAST][:].indirect(offs_of(q_cols(3))), COPY)
        nc.vector.tensor_tensor(w2[:, LAST, q_cols(3)], w_late[:], m_g[LAST][:, q_cols(3)], ADD)

        fd2 = keep.tile([P, PACK], F32, name="fd2")
        nc.scalar.activation(fd2[:], fd_c[:], SQUARE)
        nc.scalar.activation(neg_fd2[:], fd2[:], COPY, scale=-1.0)

        w2_codes = [keep.tile([P, QSLOTS], U32, name=f"w2_codes{q}", align_bytes=64) for q in range(QUARTERS)]
        w2_scales = [keep.tile([P, QSLOTS], U8, name=f"w2_scales{q}", align_bytes=64) for q in range(QUARTERS)]
        g_il = [keep.tile([P, QSLOTS, PACK], BF16, name=f"g_il{q}", tag=f"g_il{q}", align_bytes=64) for q in range(QUARTERS)]
        g_codes = keep.tile([P, SLOTS], U32, name="g_codes", align_bytes=64)
        g_scales = keep.tile([P, SLOTS], U8, name="g_scales", align_bytes=64)
        scores = [bank(q, f"scores{q}") for q in range(QUARTERS)]

        def y_of(q):
            return y_raw[q][:]

        def score_quarter(q):
            nc.vector.quantize_mx(w2_codes[q][:].bitcast(E4M3), w2_scales[q][:], w2_il[q][:].rearrange("p n t -> p (n t)"))
            w2_mx = (w2_codes[q][:].bitcast(E4M3), w2_scales[q][:])
            if q in DIRECT:
                for s in range(PACK):
                    nc.tensor.matmul_mx(
                        scores[q][:, q_cols(s)],
                        lhsT=xd_codes[:, q_cols(s)].bitcast(E4M3),
                        lhsT_scale=xd_scales[:, q_cols(s)],
                        rhs=w2_mx[0],
                        rhs_scale=w2_mx[1],
                        start=True,
                        stop=True,
                    )
            else:
                nc.tensor.matmul_mx(
                    scores[q][:],
                    lhsT=w2_mx[0],
                    lhsT_scale=w2_mx[1],
                    rhs=xd_codes[:].bitcast(E4M3),
                    rhs_scale=xd_scales[:],
                    start=True,
                    stop=True,
                )

        turned = {}

        def scale_and_turn(q):
            k = BY_SLOT.index(q)
            scaled = keep.tile([P, R], F32, name=f"scaled{q}")
            nc.scalar.activation(scaled[:], scores[q][:], COPY, scale=ts_col[:, k : k + 1])
            turned[q] = bank(4 + k, f"turned{q}")
            for s in range(PACK):
                nc.tensor.transpose(turned[q][:, q_cols(s)], scaled[:, q_cols(s)], ident[:])

        resid = {}

        def form_resid(q, tag):
            resid[q] = keep.tile([P, PACK, QSLOTS], F32, name=f"resid{q}", tag=tag, align_bytes=64)
            for s in range(PACK):
                nc.vector.scalar_tensor_tensor(
                    resid[q][:, s, :], turned[q][:, q_cols(s)], us_c[:, s : s + 1], y_of(q)[:, s, :], MULT, SUB
                )

        def form_g(q):
            nc.vector.tensor_tensor(woven(g_il[q][:]), planar(resid[q][:]), planar(y_fac[:, :, q_cols(q)]), MULT)

        y_term = {q: w2[:, :, q_cols(q)] for q in DIRECT}
        a_term = {q: keep.tile([P, PACK, QSLOTS], F32, name=f"a_term{q}", tag=f"a_term{q}", align_bytes=64) for q in DIRECT}

        def form_y_term(q):
            nc.vector.tensor_tensor(y_term[q], y_of(q), y_fac[:, :, q_cols(q)], MULT)

        def form_a_term(q):
            nc.vector.tensor_tensor(a_term[q][:], scores[q][:].rearrange("p (s n) -> p s n", s=PACK), a_fac[:, :, q_cols(q)], MULT)

        def form_direct_g(q):
            nc.vector.tensor_tensor(woven(g_il[q][:]), planar(a_term[q][:]), planar(y_term[q]), SUB)

        def quantise_g(q):
            nc.vector.quantize_mx(g_codes[:, q_cols(q)].bitcast(E5M2), g_scales[:, q_cols(q)], g_il[q][:].rearrange("p n s -> p (n s)"))

        def grad_pass(out, t, cols):
            nc.tensor.matmul_mx(
                out,
                lhsT=xr_codes[:, q_cols(t)].bitcast(E4M3),
                lhsT_scale=xr_scales[:, q_cols(t)],
                rhs=g_codes[:, cols].bitcast(E5M2),
                rhs_scale=g_scales[:, cols],
                start=True,
                stop=True,
            )

        def scalar_half(t, h, staged, source):
            nc.scalar.copy(staged, source)
            nc.scalar.activation(grad_win[t][:].indirect(offs_of(h_cols(h))), staged, COPY)

        for q in range(QUARTERS):
            weave_w2(q, slice(2, PACK))
        score_quarter(0)
        score_quarter(1)
        form_y_term(0)
        score_quarter(2)
        form_y_term(1)
        score_quarter(3)
        for q in BY_SLOT:
            scale_and_turn(q)
        for q in DIRECT:
            form_a_term(q)
        for q in DIRECT:
            form_direct_g(q)
        dw = [keep.tile([P, SLOTS], F32, name=f"dw{t}", tag=f"dw{t}") for t in range(2)]
        for q, number in ((0, 7), (1, 6)):
            quantise_g(q)
            early = bank(number, f"early{q}")
            grad_pass(early[:, 0:QSLOTS], 0, q_cols(q))
            nc.scalar.copy(dw[0][:, q_cols(q)], early[:, 0:QSLOTS])
        early1 = bank(0, "early_plane1")
        grad_pass(early1[:, 0:HSLOTS], 1, h_cols(0))
        nc.scalar.copy(dw[1][:, h_cols(0)], early1[:, 0:HSLOTS])
        for t in range(2):
            nc.scalar.activation(grad_win[t][:].indirect(offs_of(h_cols(0))), dw[t][:, h_cols(0)], COPY)

        late = {}
        for q, number, tag in ((2, 1, "a_term1"), (3, 4, "g_il1")):
            form_resid(q, tag)
            form_g(q)
            quantise_g(q)
            late[q] = bank(number, f"late{q}")
            grad_pass(late[q][:, 0:QSLOTS], 0, q_cols(q))
        late1 = bank(5, "late1")
        grad_pass(late1[:, 0:HSLOTS], 1, h_cols(1))
        grad = {t: bank(t, f"grad{t}") for t in (2, 3)}
        for t in (2, 3):
            grad_pass(grad[t][:], t, slice(0, SLOTS))

        for q in (2, 3):
            nc.vector.tensor_copy(dw[0][:, q_cols(q)], late[q][:, 0:QSLOTS])
            nc.vector.tensor_tensor(grad_win[0][:].indirect(offs_of(q_cols(q))), dw[0][:, q_cols(q)], zeros[:], ADD)
        nc.sync.dma_start(by_plane(out_1)[:, 0, :], grad_win[0][:])
        scalar_half(1, 1, dw[1][:, h_cols(1)], late1[:, 0:HSLOTS])
        nc.sync.dma_start(by_plane(out_1)[:, 1, :], grad_win[1][:])

        def store_mom(queue, t):
            queue.dma_start(by_plane(out_0)[:, t, :], mom_win[t][:])

        def mom_from_staged(t):
            step = keep.tile([P, SLOTS], F32, name=f"step{t}", tag=f"stage{t}")
            nc.vector.tensor_scalar(step[:], dw[t][:], neg_fd2[:, t : t + 1], 0.0, MULT, ADD)
            nc.vector.tensor_tensor(mom_win[t][:].indirect(offsets[:]), step[:], m_g[t][:], ADD)

        def mom_from_bank(t, tag):
            nm = keep.tile([P, SLOTS], F32, name=f"nm{t}", tag=tag)
            nc.vector.scalar_tensor_tensor(nm[:], grad[t][:], neg_fd2[:, t : t + 1], m_g[t][:], MULT, ADD)
            return nm

        def grad_plane(t, tags):
            for h in range(2):
                staged = keep.tile([P, HSLOTS], F32, name=f"staged{t}_{h}", tag=tags[h])
                scalar_half(t, h, staged[:], grad[t][:, h_cols(h)])

        mom_from_staged(0)
        store_mom(nc.sync, 0)
        mom_from_staged(1)
        grad_plane(2, ("ring", "dw1"))
        nc.sync.dma_start(by_plane(out_1)[:, 2, :], grad_win[2][:])
        store_mom(nc.sync, 1)
        grad_plane(3, ("ring", "dw0"))
        nc.sync.dma_start(by_plane(out_1)[:, 3, :], grad_win[3][:])
        nm_for_scalar = mom_from_bank(2, "dw1")
        nc.vector.tensor_copy(mom_win[LAST][:].indirect(offsets[:]), mom_from_bank(LAST, "m_g2")[:])
        store_mom(nc.sync, LAST)
        for h in range(2):
            nc.scalar.activation(mom_win[2][:].indirect(offs_of(h_cols(h))), nm_for_scalar[:, h_cols(h)], COPY)
        store_mom(nc.sync, 2)
